import numpy as np
import ml_dtypes


def mxq(x, axis, fmt="e4m3"):
    dtype, down = {"e4m3": (ml_dtypes.float8_e4m3fn, 7), "e5m2": (ml_dtypes.float8_e5m2, 14)}[fmt]
    v = np.moveaxis(np.asarray(x, np.float32).astype(ml_dtypes.bfloat16).astype(np.float64), axis, -1)
    blocks = v.reshape(v.shape[:-1] + (-1, 32))
    amax = np.abs(blocks).max(-1, keepdims=True)
    byte = np.maximum(np.where(amax > 0, np.frexp(amax)[1] - 1 + 127, 0) - down, 1)
    scale = np.exp2(byte - 127.0)
    codes = (blocks / scale).astype(np.float32).astype(dtype).astype(np.float64)
    return np.moveaxis((codes * scale).reshape(v.shape), -1, axis)


WIDE = False


def mx_kscale(k):
    if not WIDE:
        return np.ones(k)
    levels = np.array([10, -10, 5, -5, 0])
    if k % 512:
        return np.exp2(np.random.permutation(np.resize(levels, k // 32))).repeat(32)
    a = np.empty((k // 512, 16))
    for p in range(k // 512):
        a[p, :8] = np.random.permutation(np.resize(levels, 8))
        for g in range(8):
            far = levels[np.abs(levels - a[p, g]) >= 10]
            a[p, g + 8] = far[np.random.randint(len(far))]
    return np.exp2(a.ravel()).repeat(32)


def f64(x):
    return np.asarray(x).astype(np.float64)


def striped(idx):
    return np.tile(idx.reshape(-1, 16).T, (8, 1)).astype(np.uint16)


def unstriped(offs):
    return offs[:16].T.reshape(-1).astype(np.int64)


E2M1 = np.array([0.0, 0.5, 1.0, 1.5, 2.0, 3.0, 4.0, 6.0, -0.0, -0.5, -1.0, -1.5, -2.0, -3.0, -4.0, -6.0])


def pack_weight(w, fmt):
    k, n = w.shape
    w = f64(np.asarray(w, np.float32).astype(ml_dtypes.bfloat16)).reshape(k // 32, 32, n)
    amax = np.abs(w).max(1)
    if fmt == "e4m3":
        byte = np.frexp(amax)[1] - 1 + 127 - 7
    else:
        mant, ex = np.frexp(amax / 6.0)
        byte = np.where(mant > 0.5, ex, ex - 1) + 127
    byte = np.clip(np.where(amax > 0, byte, 1), 1, 254)
    scaled = (w * np.exp2(127.0 - byte)[:, None, :]).reshape(k, n).astype(np.float32)
    by_word = np.ascontiguousarray(scaled.reshape(k // 512, 128, 4, n).transpose(0, 1, 3, 2))
    if fmt == "e4m3":
        words = by_word.astype(ml_dtypes.float8_e4m3fn).view(np.uint8)
    else:
        c = by_word.astype(ml_dtypes.float4_e2m1fn).view(np.uint8) & 0xF
        words = (c[..., 0::2] | (c[..., 1::2] << 4)).reshape(k // 512, 128, 2 * n)
    return np.ascontiguousarray(words), np.ascontiguousarray(byte.astype(np.uint8).reshape(k // 512, 16, n))


def unpack_weight(words, scales, fmt):
    g, _, n = scales.shape
    words = np.ascontiguousarray(words).reshape(g, 128, n, -1)
    if fmt == "e4m3":
        vals = words.view(ml_dtypes.float8_e4m3fn).astype(np.float64)
    else:
        nib = np.empty((g, 128, n, 4), np.uint8)
        nib[..., 0::2] = words & 0xF
        nib[..., 1::2] = words >> 4
        vals = E2M1[nib]
    vals = vals * np.repeat(np.exp2(scales.astype(np.float64) - 127.0), 8, axis=1)[..., None]
    return vals.transpose(0, 1, 3, 2).reshape(g * 512, n)


K, T, E, C, N = 1024, 1280, 6, 128, 256


def by_expert(wq, xq):
    return np.concatenate([wq[e].T @ xq[:, e * C:(e + 1) * C] for e in range(E)], axis=1)


def setup_inputs():
    n = np.random.standard_normal
    s = mx_kscale(K)[:, None]
    w = [pack_weight(m, "e2m1") for m in n((E, K, N)) / np.sqrt(K) / s[None]]
    return {
        "xT": (n((K, T)) * s).astype(np.float32),
        "xr": n((N, T)).astype(np.float32),
        "w_words": np.stack([m[0] for m in w]),
        "w_scales": np.stack([m[1] for m in w]),
        "b": (0.3 * n((N, E))).astype(np.float32),
        "gate": np.tile(np.random.uniform(0.2, 1.0, E * C), (N, 1)).astype(np.float32),
        "offs": striped(np.random.permutation(T)[:E * C]),
    }


def reference(xT, xr, w_words, w_scales, b, gate, offs):
    idx = unstriped(offs)
    w = np.stack([unpack_weight(w_words[e], w_scales[e], "e2m1") for e in range(E)])
    xq = mxq(f64(xT)[:, idx], 0, "e4m3")
    y = by_expert(w, xq)
    y = y + np.repeat(f64(b), C, axis=1)
    out = f64(xr).copy()
    out[:, idx] += f64(gate) * y
    return out

@@ -1,0 +1,170 @@
+from contextlib import ExitStack
+
+import concourse.mybir as mybir
+
+K, T, E, C, N = 1024, 1280, 6, 128, 256
+S = E * C
+P = 128
+K_PASS = 512
+PASSES = K // K_PASS
+HALVES = N // P
+
+FLOPS = 2 * S * K * N
+BYTES = 4 * K * T + 8 * N * T + E * K * N // 2 + E * K * N // 32 + 4 * N * E + 4 * S + 2 * P * S // 16
+
+F32 = mybir.dt.float32
+BF16 = mybir.dt.bfloat16
+I32 = mybir.dt.int32
+U32 = mybir.dt.uint32
+U16 = mybir.dt.uint16
+U8 = mybir.dt.uint8
+FP8X4 = mybir.dt.float8_e4m3fn_x4
+FP4X4 = mybir.dt.float4_e2m1fn_x4
+ADD, MULT = mybir.AluOpType.add, mybir.AluOpType.mult
+IDENTITY = mybir.ActivationFunctionType.Identity
+
+CHUNKS = (
+    ((0, 512, 184), (512, 512, 184), (1024, 256, 96)),
+    ((0, 256, 256), (256, 512, 448), (768, 256, 192), (1024, 256, 96)),
+)
+PIECE = 2
+
+
+def interleave(ap_in, ap_out):
+    src = ap_in.rearrange("p j (c i) -> p c j i", i=4)
+    dst = ap_out.rearrange("p (c i) j -> p c j i", i=4)
+    return dst, src
+
+
+def tile_moe_res_lin_bias_kernel(tc, xT, xr, w_words, w_scales, b, gate, offs, out):
+    nc = tc.nc
+    with ExitStack() as ctx:
+        keep = ctx.enter_context(tc.tile_pool(name="keep", bufs=1))
+        psum = ctx.enter_context(tc.psum_pool(name="psum", bufs=1))
+
+        offsets = keep.tile([P, S // 16], U16, name="offsets")
+
+        words = [keep.tile([P, T], U32, name=f"words{a}", align_bytes=64) for a in range(PASSES)]
+        scales = [keep.tile([P, T], U8, name=f"scales{a}", align_bytes=64) for a in range(PASSES)]
+        slot_words = [keep.tile([P, S], U32, name=f"slot_words{a}", align_bytes=64) for a in range(PASSES)]
+        slot_scales = [keep.tile([P, S], U8, name=f"slot_scales{a}", align_bytes=64) for a in range(PASSES)]
+        w_code = keep.tile([P, E * PASSES, 2 * N], U8, name="w_code", align_bytes=64)
+        w_scale = keep.tile([P, E * PASSES * N], U8, name="w_scale", align_bytes=64)
+        window = [keep.tile([P, T], F32, name=f"window{h}") for h in range(HALVES)]
+        result = [keep.tile([P, S], F32, name=f"result{h}") for h in range(HALVES)]
+        scaled = [keep.tile([P, S], F32, name=f"scaled{h}") for h in range(HALVES)]
+        total = [keep.tile([P, T], F32, name=f"total{h}") for h in range(HALVES)]
+        residual = [keep.tile([P, T], F32, name=f"residual{h}") for h in range(HALVES)]
+        bias = keep.tile([P, HALVES, 8], F32, name="bias")
+        gates = keep.tile([P, S], F32, name="gates")
+
+        nc.gpsimd.memset(scales[0][:].bitcast(I32), 0)
+        nc.gpsimd.memset(scales[1][:].bitcast(I32), 0)
+        nc.gpsimd.memset(w_scale[:].bitcast(I32), 0)
+        for h in range(HALVES):
+            nc.vector.memset(window[h][:], 0.0)
+
+        raws = []
+        for a in range(PASSES):
+            row = []
+            for i, (t0, width, on_scalar) in enumerate(CHUNKS[a]):
+                raw = keep.tile([P, 4, width], F32, name=f"raw{a}_{i}")
+                nc.sync.dma_start(
+                    raw[:], xT[a * K_PASS : (a + 1) * K_PASS, t0 : t0 + width].rearrange("(p j) w -> p j w", j=4)
+                )
+                row.append(raw)
+                if a == 0 and i == 0:
+                    nc.sync.dma_start(offsets[:], offs)
+            raws.append(row)
+
+        w_scale_words = w_scale[:].bitcast(I32).rearrange("p (g n) -> p g n", g=E * PASSES)
+        scale_rows = w_scales.bitcast(I32).rearrange("e a (q r) n -> r q (e a) n", r=4)
+        for r in range(4):
+            nc.sync.dma_start(w_scale_words[r:P:32], scale_rows[r])
+        code_rows = w_words.rearrange("e a p n -> p (e a) n")
+        for e0 in range(0, E, PIECE):
+            g = slice(e0 * PASSES, (e0 + PIECE) * PASSES)
+            nc.sync.dma_start(w_code[:, g, :], code_rows[:, g, :])
+            if e0 == 0:
+                nc.sync.dma_start(bias[:, :, 0:E], b.rearrange("(h p) e -> p h e", p=P))
+                nc.sync.dma_start(gates[:], gate[0:P, :])
+        for h in range(HALVES):
+            nc.sync.dma_start(residual[h][:], xr[h * P : (h + 1) * P, :])
+
+        for a in range(PASSES):
+            for i, (t0, width, on_scalar) in enumerate(CHUNKS[a]):
+                raw = raws[a][i]
+                grouped = keep.tile([P, width, 4], BF16, name=f"grouped{a}_{i}", align_bytes=64)
+                dst, src = interleave(raw[:, :, 0:on_scalar], grouped[:, 0:on_scalar, :])
+                nc.scalar.activation(dst, src, IDENTITY)
+                if on_scalar < width:
+                    dst, src = interleave(raw[:, :, on_scalar:width], grouped[:, on_scalar:width, :])
+                    nc.vector.tensor_copy(dst, src)
+                flat = grouped[:].rearrange("p w j -> p (w j)")
+                done = 0
+                while done < width:
+                    cut = max(n for n in (512, 256, 128) if n <= width - done)
+                    nc.vector.quantize_mx(
+                        out=words[a][:, t0 + done : t0 + done + cut].bitcast(FP8X4),
+                        scales=scales[a][:, t0 + done : t0 + done + cut],
+                        in_=flat[:, 4 * done : 4 * (done + cut)],
+                    )
+                    done += cut
+            if a == 0:
+                nc.vector.tensor_copy(slot_words[a][:], words[a][:].indirect(offsets[:]))
+                nc.vector.tensor_copy(slot_scales[a][:], scales[a][:].indirect(offsets[:]))
+
+        banks = [
+            [psum.tile([P, PIECE * C], F32, name=f"bank{h}_{i}") for i in range(E // PIECE)] for h in range(HALVES)
+        ]
+
+        def multiply(h, i):
+            for e in range(i * PIECE, (i + 1) * PIECE):
+                slots = slice(e * C, (e + 1) * C)
+                local = slice((e - i * PIECE) * C, (e - i * PIECE + 1) * C)
+                for a in range(PASSES):
+                    g = e * PASSES + a
+                    nc.tensor.matmul_mx(
+                        out=banks[h][i][:, local],
+                        lhsT=w_code[:, g, 2 * P * h : 2 * P * (h + 1)].bitcast(FP4X4),
+                        lhsT_scale=w_scale[:, g * N + h * P : g * N + (h + 1) * P],
+                        rhs=slot_words[a][:, slots].bitcast(FP8X4),
+                        rhs_scale=slot_scales[a][:, slots],
+                        start=(a == 0),
+                        stop=(a == PASSES - 1),
+                    )
+
+        def leave_bank(h, i):
+            for e in range(i * PIECE, (i + 1) * PIECE):
+                slots = slice(e * C, (e + 1) * C)
+                local = slice((e - i * PIECE) * C, (e - i * PIECE + 1) * C)
+                nc.scalar.activation(result[h][:, slots], banks[h][i][:, local], IDENTITY, bias=bias[:, h, e : e + 1])
+
+            slots = slice(i * PIECE * C, (i + 1) * PIECE * C)
+            nc.gpsimd.tensor_tensor(scaled[h][:, slots], result[h][:, slots], gates[:, slots], MULT)
+
+        def scatter(h, i0, i1):
+            slots = slice(i0 * PIECE * C, i1 * PIECE * C)
+            part = slice(i0 * PIECE * C // 16, i1 * PIECE * C // 16)
+            nc.vector.tensor_copy(window[h][:].indirect(offsets[:, part]), scaled[h][:, slots])
+
+        def finish(engine, h, cuts):
+            for t0, t1 in cuts:
+                engine.tensor_tensor(total[h][:, t0:t1], window[h][:, t0:t1], residual[h][:, t0:t1], ADD)
+                nc.sync.dma_start(out[h * P : (h + 1) * P, t0:t1], total[h][:, t0:t1])
+
+        a = PASSES - 1
+        for i0, i1 in ((0, 1), (1, 3)):
+            slots = slice(i0 * PIECE * C, i1 * PIECE * C)
+            part = slice(i0 * PIECE * C // 16, i1 * PIECE * C // 16)
+            nc.vector.tensor_copy(slot_words[a][:, slots], words[a][:].indirect(offsets[:, part]))
+            nc.vector.tensor_copy(slot_scales[a][:, slots], scales[a][:].indirect(offsets[:, part]))
+        for h, i in ((0, 0), (1, 0), (0, 1), (0, 2), (1, 1), (1, 2)):
+            multiply(h, i)
+            leave_bank(h, i)
+        scatter(0, 0, 1)
+        scatter(1, 0, 1)
+        scatter(0, 1, 3)
+        finish(nc.gpsimd, 0, ((0, 640), (640, T)))
+        scatter(1, 1, 3)
+        finish(nc.vector, 1, ((0, 768), (768, T)))

@@ -23,17 +23,10 @@ FP4X4 = mybir.dt.float4_e2m1fn_x4
 ADD, MULT = mybir.AluOpType.add, mybir.AluOpType.mult
 IDENTITY = mybir.ActivationFunctionType.Identity
 
-CHUNKS = (
-    ((0, 512, 184), (512, 512, 184), (1024, 256, 96)),
-    ((0, 256, 256), (256, 512, 448), (768, 256, 192), (1024, 256, 96)),
-)
+CUTS = (0, 480, 960, T)
 PIECE = 2
-
-
-def interleave(ap_in, ap_out):
-    src = ap_in.rearrange("p j (c i) -> p c j i", i=4)
-    dst = ap_out.rearrange("p (c i) j -> p c j i", i=4)
-    return dst, src
+PIECES = E // PIECE
+W = PIECE * C
 
 
 def tile_moe_res_lin_bias_kernel(tc, xT, xr, w_words, w_scales, b, gate, offs, out):
@@ -43,11 +36,8 @@ def tile_moe_res_lin_bias_kernel(tc, xT, xr, w_words, w_scales, b, gate, offs, o
         psum = ctx.enter_context(tc.psum_pool(name="psum", bufs=1))
 
         offsets = keep.tile([P, S // 16], U16, name="offsets")
+        planes = [(a, u) for a in range(PASSES) for u in range(2)]
 
-        words = [keep.tile([P, T], U32, name=f"words{a}", align_bytes=64) for a in range(PASSES)]
-        scales = [keep.tile([P, T], U8, name=f"scales{a}", align_bytes=64) for a in range(PASSES)]
-        slot_words = [keep.tile([P, S], U32, name=f"slot_words{a}", align_bytes=64) for a in range(PASSES)]
-        slot_scales = [keep.tile([P, S], U8, name=f"slot_scales{a}", align_bytes=64) for a in range(PASSES)]
         w_code = keep.tile([P, E * PASSES, 2 * N], U8, name="w_code", align_bytes=64)
         w_scale = keep.tile([P, E * PASSES * N], U8, name="w_scale", align_bytes=64)
         window = [keep.tile([P, T], F32, name=f"window{h}") for h in range(HALVES)]
@@ -56,115 +46,169 @@ def tile_moe_res_lin_bias_kernel(tc, xT, xr, w_words, w_scales, b, gate, offs, o
         total = [keep.tile([P, T], F32, name=f"total{h}") for h in range(HALVES)]
         residual = [keep.tile([P, T], F32, name=f"residual{h}") for h in range(HALVES)]
         bias = keep.tile([P, HALVES, 8], F32, name="bias")
-        gates = keep.tile([P, S], F32, name="gates")
+        gates = [keep.tile([P, W], F32, name=f"gates{i}") for i in range(PIECES)]
 
-        nc.gpsimd.memset(scales[0][:].bitcast(I32), 0)
-        nc.gpsimd.memset(scales[1][:].bitcast(I32), 0)
         nc.gpsimd.memset(w_scale[:].bitcast(I32), 0)
         for h in range(HALVES):
             nc.vector.memset(window[h][:], 0.0)
 
-        raws = []
-        for a in range(PASSES):
-            row = []
-            for i, (t0, width, on_scalar) in enumerate(CHUNKS[a]):
-                raw = keep.tile([P, 4, width], F32, name=f"raw{a}_{i}")
-                nc.sync.dma_start(
-                    raw[:], xT[a * K_PASS : (a + 1) * K_PASS, t0 : t0 + width].rearrange("(p j) w -> p j w", j=4)
-                )
-                row.append(raw)
-                if a == 0 and i == 0:
+        raws = {}
+        for a, u in planes:
+            rows = xT[a * K_PASS : (a + 1) * K_PASS, :].rearrange("(p j) w -> p j w", j=4)
+            for c in range(3):
+                raw = keep.tile([P, 2, CUTS[c + 1] - CUTS[c]], F32, name=f"raw{a}{u}{c}", align_bytes=64)
+                nc.sync.dma_start(raw[:], rows[:, 2 * u : 2 * u + 2, CUTS[c] : CUTS[c + 1]])
+                raws[a, u, c] = raw
+                if (a, u, c) == (0, 0, 0):
                     nc.sync.dma_start(offsets[:], offs)
-            raws.append(row)
 
+        code_rows = w_words.rearrange("e a p n -> p (e a) n")
+
+        def load_codes(i):
+            g = slice(i * PIECE * PASSES, (i + 1) * PIECE * PASSES)
+            nc.sync.dma_start(w_code[:, g, :], code_rows[:, g, :])
+
+        nc.sync.dma_start(bias[:, :, 0:E], b.rearrange("(h p) e -> p h e", p=P))
+        load_codes(0)
         w_scale_words = w_scale[:].bitcast(I32).rearrange("p (g n) -> p g n", g=E * PASSES)
         scale_rows = w_scales.bitcast(I32).rearrange("e a (q r) n -> r q (e a) n", r=4)
         for r in range(4):
             nc.sync.dma_start(w_scale_words[r:P:32], scale_rows[r])
-        code_rows = w_words.rearrange("e a p n -> p (e a) n")
-        for e0 in range(0, E, PIECE):
-            g = slice(e0 * PASSES, (e0 + PIECE) * PASSES)
-            nc.sync.dma_start(w_code[:, g, :], code_rows[:, g, :])
-            if e0 == 0:
-                nc.sync.dma_start(bias[:, :, 0:E], b.rearrange("(h p) e -> p h e", p=P))
-                nc.sync.dma_start(gates[:], gate[0:P, :])
+        nc.sync.dma_start(gates[0][:], gate[0:P, 0:W])
+        for i in range(1, PIECES):
+            load_codes(i)
+            nc.sync.dma_start(gates[i][:], gate[0:P, i * W : (i + 1) * W])
         for h in range(HALVES):
             nc.sync.dma_start(residual[h][:], xr[h * P : (h + 1) * P, :])
 
-        for a in range(PASSES):
-            for i, (t0, width, on_scalar) in enumerate(CHUNKS[a]):
-                raw = raws[a][i]
-                grouped = keep.tile([P, width, 4], BF16, name=f"grouped{a}_{i}", align_bytes=64)
-                dst, src = interleave(raw[:, :, 0:on_scalar], grouped[:, 0:on_scalar, :])
-                nc.scalar.activation(dst, src, IDENTITY)
-                if on_scalar < width:
-                    dst, src = interleave(raw[:, :, on_scalar:width], grouped[:, on_scalar:width, :])
-                    nc.vector.tensor_copy(dst, src)
-                flat = grouped[:].rearrange("p w j -> p (w j)")
-                done = 0
-                while done < width:
-                    cut = max(n for n in (512, 256, 128) if n <= width - done)
-                    nc.vector.quantize_mx(
-                        out=words[a][:, t0 + done : t0 + done + cut].bitcast(FP8X4),
-                        scales=scales[a][:, t0 + done : t0 + done + cut],
-                        in_=flat[:, 4 * done : 4 * (done + cut)],
-                    )
-                    done += cut
-            if a == 0:
-                nc.vector.tensor_copy(slot_words[a][:], words[a][:].indirect(offsets[:]))
-                nc.vector.tensor_copy(slot_scales[a][:], scales[a][:].indirect(offsets[:]))
+        pairs = {}
 
-        banks = [
-            [psum.tile([P, PIECE * C], F32, name=f"bank{h}_{i}") for i in range(E // PIECE)] for h in range(HALVES)
-        ]
+        def round_tokens(copy, a, u, c):
+            dst = pairs[a, u][:, CUTS[c] : CUTS[c + 1]].bitcast(BF16).rearrange("p (w e) -> p w e", e=2)
+            copy(dst, raws[a, u, c][:].rearrange("p e w -> p w e"))
+
+        def on_scalar(dst, src):
+            nc.scalar.activation(dst, src, IDENTITY)
+
+        def round_plane(a, u):
+            pairs[a, u] = keep.tile([P, T], U32, name=f"pairs{a}{u}", align_bytes=64)
+            round_tokens(nc.vector.tensor_copy if (a, u) == (0, 0) else on_scalar, a, u, 0)
+            round_tokens(on_scalar, a, u, 1)
+            round_tokens(nc.vector.tensor_copy, a, u, 2)
+
+        def gather(dst, a, u, i0, i1):
+            nc.vector.tensor_copy(dst, pairs[a, u][:].indirect(offsets[:, i0 * W // 16 : i1 * W // 16]))
+
+        codes, scales = {}, {}
+
+        def quantise(a, i0, i1, woven, tag=""):
+            n = (i1 - i0) * W
+            code = keep.tile([P, n], U32, name=f"codes{a}{i0}", tag=tag, align_bytes=64)
+            scale = keep.tile([P, n], U8, name=f"scales{a}{i0}", align_bytes=64)
+            nc.vector.quantize_mx(
+                out=code[:].bitcast(FP8X4),
+                scales=scale[:],
+                in_=woven.rearrange("p s u -> p (s u)").bitcast(BF16),
+            )
+            for i in range(i0, i1):
+                codes[a, i] = code[:, (i - i0) * W : (i - i0 + 1) * W]
+                scales[a, i] = scale[:, (i - i0) * W : (i - i0 + 1) * W]
+
+        sums = [[None] * E for h in range(HALVES)]
+        for h in range(HALVES):
+            for i in range(PIECES):
+                if (h, i) == (0, 0):
+                    for e in range(PIECE):
+                        sums[h][e] = psum.tile([P, C], F32, name=f"lone{e}")[:]
+                else:
+                    bank = psum.tile([P, W], F32, name=f"bank{h}_{i}")
+                    for j in range(PIECE):
+                        sums[h][i * PIECE + j] = bank[:, j * C : (j + 1) * C]
+
+        def one_pass(h, e, a):
+            i, j = divmod(e, PIECE)
+            g = e * PASSES + a
+            nc.tensor.matmul_mx(
+                out=sums[h][e],
+                lhsT=w_code[:, g, 2 * P * h : 2 * P * (h + 1)].bitcast(FP4X4),
+                lhsT_scale=w_scale[:, g * N + h * P : g * N + (h + 1) * P],
+                rhs=codes[a, i][:, j * C : (j + 1) * C].bitcast(FP8X4),
+                rhs_scale=scales[a, i][:, j * C : (j + 1) * C],
+                start=(a == 0),
+                stop=(a == PASSES - 1),
+            )
 
         def multiply(h, i):
             for e in range(i * PIECE, (i + 1) * PIECE):
-                slots = slice(e * C, (e + 1) * C)
-                local = slice((e - i * PIECE) * C, (e - i * PIECE + 1) * C)
                 for a in range(PASSES):
-                    g = e * PASSES + a
-                    nc.tensor.matmul_mx(
-                        out=banks[h][i][:, local],
-                        lhsT=w_code[:, g, 2 * P * h : 2 * P * (h + 1)].bitcast(FP4X4),
-                        lhsT_scale=w_scale[:, g * N + h * P : g * N + (h + 1) * P],
-                        rhs=slot_words[a][:, slots].bitcast(FP8X4),
-                        rhs_scale=slot_scales[a][:, slots],
-                        start=(a == 0),
-                        stop=(a == PASSES - 1),
-                    )
+                    one_pass(h, e, a)
+
+        def add_bias(h, e):
+            nc.scalar.activation(result[h][:, e * C : (e + 1) * C], sums[h][e], IDENTITY, bias=bias[:, h, e : e + 1])
+
+        def times_gate(h, s0, s1):
+            i = s0 // W
+            nc.gpsimd.tensor_tensor(scaled[h][:, s0:s1], result[h][:, s0:s1], gates[i][:, s0 - i * W : s1 - i * W], MULT)
 
         def leave_bank(h, i):
             for e in range(i * PIECE, (i + 1) * PIECE):
-                slots = slice(e * C, (e + 1) * C)
-                local = slice((e - i * PIECE) * C, (e - i * PIECE + 1) * C)
-                nc.scalar.activation(result[h][:, slots], banks[h][i][:, local], IDENTITY, bias=bias[:, h, e : e + 1])
-
-            slots = slice(i * PIECE * C, (i + 1) * PIECE * C)
-            nc.gpsimd.tensor_tensor(scaled[h][:, slots], result[h][:, slots], gates[:, slots], MULT)
+                add_bias(h, e)
+            times_gate(h, i * W, (i + 1) * W)
 
         def scatter(h, i0, i1):
-            slots = slice(i0 * PIECE * C, i1 * PIECE * C)
-            part = slice(i0 * PIECE * C // 16, i1 * PIECE * C // 16)
-            nc.vector.tensor_copy(window[h][:].indirect(offsets[:, part]), scaled[h][:, slots])
+            part = slice(i0 * W // 16, i1 * W // 16)
+            nc.vector.tensor_copy(window[h][:].indirect(offsets[:, part]), scaled[h][:, i0 * W : i1 * W])
 
         def finish(engine, h, cuts):
             for t0, t1 in cuts:
                 engine.tensor_tensor(total[h][:, t0:t1], window[h][:, t0:t1], residual[h][:, t0:t1], ADD)
                 nc.sync.dma_start(out[h * P : (h + 1) * P, t0:t1], total[h][:, t0:t1])
 
-        a = PASSES - 1
-        for i0, i1 in ((0, 1), (1, 3)):
-            slots = slice(i0 * PIECE * C, i1 * PIECE * C)
-            part = slice(i0 * PIECE * C // 16, i1 * PIECE * C // 16)
-            nc.vector.tensor_copy(slot_words[a][:, slots], words[a][:].indirect(offsets[:, part]))
-            nc.vector.tensor_copy(slot_scales[a][:, slots], scales[a][:].indirect(offsets[:, part]))
-        for h, i in ((0, 0), (1, 0), (0, 1), (0, 2), (1, 1), (1, 2)):
+        first0 = keep.tile([P, W, 2], U32, name="first0", align_bytes=64)
+        rest0 = keep.tile([P, 2, S - W], U32, name="rest0")
+        rest1 = keep.tile([P, 2, S - W], U32, name="rest1", align_bytes=64)
+        first1 = rest1[:, 1, :].rearrange("p (s u) -> p s u", u=2)
+
+        def weave(copy, dtype, rest, i, tag):
+            woven = keep.tile([P, W, 2], U32, name=f"woven_{tag}", tag=tag, align_bytes=64)
+            copy(woven[:].bitcast(dtype), rest[:, :, (i - 1) * W : i * W].bitcast(dtype).rearrange("p u s -> p s u"))
+            return woven[:]
+
+        for u in range(2):
+            round_plane(0, u)
+            gather(first0[:, :, u], 0, u, 0, 1)
+            gather(rest0[:, u, :], 0, u, 1, PIECES)
+        quantise(0, 0, 1, first0[:])
+        round_plane(1, 0)
+        for e in range(PIECE):
+            one_pass(0, e, 0)
+        woven = weave(nc.scalar.copy, U32, rest0, 1, "raw101")
+        gather(first1[:, :, 0], 1, 0, 0, 1)
+        gather(rest1[:, 0, :], 1, 0, 1, PIECES)
+        round_plane(1, 1)
+        later = weave(nc.scalar.copy, U32, rest0, 2, "raw111")
+        gather(first1[:, :, 1], 1, 1, 0, 1)
+        quantise(0, 1, 2, woven, "raw112")
+        quantise(1, 0, 1, first1)
+        quantise(0, 2, 3, later)
+        for e in range(PIECE):
+            one_pass(0, e, 1)
+            add_bias(0, e)
+            times_gate(0, e * C, (e + 1) * C)
+        multiply(1, 0)
+        gather(rest1[:, 1, 0:W], 1, 1, 1, 2)
+        gather(rest1[:, 1, W : 2 * W], 1, 1, 2, 3)
+        quantise(1, 1, 2, weave(nc.vector.tensor_copy, I32, rest1, 1, "own"))
+        woven = weave(nc.scalar.copy, U32, rest1, 2, "codes10")
+        leave_bank(1, 0)
+        quantise(1, 2, 3, woven)
+        scatter(0, 0, 1)
+        for h, i in ((0, 1), (0, 2), (1, 1), (1, 2)):
             multiply(h, i)
             leave_bank(h, i)
-        scatter(0, 0, 1)
         scatter(1, 0, 1)
-        scatter(0, 1, 3)
+        scatter(0, 1, 2)
+        scatter(0, 2, 3)
         finish(nc.gpsimd, 0, ((0, 640), (640, T)))
         scatter(1, 1, 3)
-        finish(nc.vector, 1, ((0, 768), (768, T)))
+        finish(nc.vector, 1, ((0, 512), (512, 1024), (1024, T)))

@@ -23,7 +23,7 @@ FP4X4 = mybir.dt.float4_e2m1fn_x4
 ADD, MULT = mybir.AluOpType.add, mybir.AluOpType.mult
 IDENTITY = mybir.ActivationFunctionType.Identity
 
-CUTS = (0, 480, 960, T)
+CUTS = (0, 768, T)
 PIECE = 2
 PIECES = E // PIECE
 W = PIECE * C
@@ -55,7 +55,7 @@ def tile_moe_res_lin_bias_kernel(tc, xT, xr, w_words, w_scales, b, gate, offs, o
         raws = {}
         for a, u in planes:
             rows = xT[a * K_PASS : (a + 1) * K_PASS, :].rearrange("(p j) w -> p j w", j=4)
-            for c in range(3):
+            for c in range(2):
                 raw = keep.tile([P, 2, CUTS[c + 1] - CUTS[c]], F32, name=f"raw{a}{u}{c}", align_bytes=64)
                 nc.sync.dma_start(raw[:], rows[:, 2 * u : 2 * u + 2, CUTS[c] : CUTS[c + 1]])
                 raws[a, u, c] = raw
@@ -93,8 +93,7 @@ def tile_moe_res_lin_bias_kernel(tc, xT, xr, w_words, w_scales, b, gate, offs, o
         def round_plane(a, u):
             pairs[a, u] = keep.tile([P, T], U32, name=f"pairs{a}{u}", align_bytes=64)
             round_tokens(nc.vector.tensor_copy if (a, u) == (0, 0) else on_scalar, a, u, 0)
-            round_tokens(on_scalar, a, u, 1)
-            round_tokens(nc.vector.tensor_copy, a, u, 2)
+            round_tokens(nc.vector.tensor_copy, a, u, 1)
 
         def gather(dst, a, u, i0, i1):
             nc.vector.tensor_copy(dst, pairs[a, u][:].indirect(offsets[:, i0 * W // 16 : i1 * W // 16]))
@@ -182,13 +181,13 @@ def tile_moe_res_lin_bias_kernel(tc, xT, xr, w_words, w_scales, b, gate, offs, o
         round_plane(1, 0)
         for e in range(PIECE):
             one_pass(0, e, 0)
-        woven = weave(nc.scalar.copy, U32, rest0, 1, "raw101")
+        woven = weave(nc.scalar.copy, U32, rest0, 1, "raw100")
         gather(first1[:, :, 0], 1, 0, 0, 1)
         gather(rest1[:, 0, :], 1, 0, 1, PIECES)
         round_plane(1, 1)
-        later = weave(nc.scalar.copy, U32, rest0, 2, "raw111")
+        later = weave(nc.scalar.copy, U32, rest0, 2, "raw110")
         gather(first1[:, :, 1], 1, 1, 0, 1)
-        quantise(0, 1, 2, woven, "raw112")
+        quantise(0, 1, 2, woven, "raw111")
         quantise(1, 0, 1, first1)
         quantise(0, 2, 3, later)
         for e in range(PIECE):

@@ -165,8 +165,8 @@ def tile_moe_res_lin_bias_kernel(tc, xT, xr, w_words, w_scales, b, gate, offs, o
 
         first0 = keep.tile([P, W, 2], U32, name="first0", align_bytes=64)
         rest0 = keep.tile([P, 2, S - W], U32, name="rest0")
-        rest1 = keep.tile([P, 2, S - W], U32, name="rest1", align_bytes=64)
-        first1 = rest1[:, 1, :].rearrange("p (s u) -> p s u", u=2)
+        first1 = keep.tile([P, W, 2], U32, name="first1", align_bytes=64)
+        rest1 = keep.tile([P, 2, S - W], U32, name="rest1")
 
         def weave(copy, dtype, rest, i, tag):
             woven = keep.tile([P, W, 2], U32, name=f"woven_{tag}", tag=tag, align_bytes=64)
@@ -188,16 +188,17 @@ def tile_moe_res_lin_bias_kernel(tc, xT, xr, w_words, w_scales, b, gate, offs, o
         later = weave(nc.scalar.copy, U32, rest0, 2, "raw110")
         gather(first1[:, :, 1], 1, 1, 0, 1)
         quantise(0, 1, 2, woven, "raw111")
-        quantise(1, 0, 1, first1)
+        quantise(1, 0, 1, first1[:])
+        gather(rest1[:, 1, 0:W], 1, 1, 1, 2)
         quantise(0, 2, 3, later)
+        woven = weave(nc.vector.tensor_copy, I32, rest1, 1, "own")
+        gather(rest1[:, 1, W : 2 * W], 1, 1, 2, 3)
+        quantise(1, 1, 2, woven)
         for e in range(PIECE):
             one_pass(0, e, 1)
             add_bias(0, e)
             times_gate(0, e * C, (e + 1) * C)
         multiply(1, 0)
-        gather(rest1[:, 1, 0:W], 1, 1, 1, 2)
-        gather(rest1[:, 1, W : 2 * W], 1, 1, 2, 3)
-        quantise(1, 1, 2, weave(nc.vector.tensor_copy, I32, rest1, 1, "own"))
         woven = weave(nc.scalar.copy, U32, rest1, 2, "codes10")
         leave_bank(1, 0)
         quantise(1, 2, 3, woven)

@@ -40,7 +40,7 @@ def tile_moe_res_lin_bias_kernel(tc, xT, xr, w_words, w_scales, b, gate, offs, o
 
         w_code = keep.tile([P, E * PASSES, 2 * N], U8, name="w_code", align_bytes=64)
         w_scale = keep.tile([P, E * PASSES * N], U8, name="w_scale", align_bytes=64)
-        window = [keep.tile([P, T], F32, name=f"window{h}") for h in range(HALVES)]
+        window = [keep.tile([P, T + 2 * W * h], F32, name=f"window{h}") for h in range(HALVES)]
         result = [keep.tile([P, S], F32, name=f"result{h}") for h in range(HALVES)]
         scaled = [keep.tile([P, S], F32, name=f"scaled{h}") for h in range(HALVES)]
         total = [keep.tile([P, T], F32, name=f"total{h}") for h in range(HALVES)]
@@ -50,7 +50,7 @@ def tile_moe_res_lin_bias_kernel(tc, xT, xr, w_words, w_scales, b, gate, offs, o
 
         nc.gpsimd.memset(w_scale[:].bitcast(I32), 0)
         for h in range(HALVES):
-            nc.vector.memset(window[h][:], 0.0)
+            nc.vector.memset(window[h][:, 0:T], 0.0)
 
         raws = {}
         for a, u in planes:
@@ -166,11 +166,14 @@ def tile_moe_res_lin_bias_kernel(tc, xT, xr, w_words, w_scales, b, gate, offs, o
         first0 = keep.tile([P, W, 2], U32, name="first0", align_bytes=64)
         rest0 = keep.tile([P, 2, S - W], U32, name="rest0")
         first1 = keep.tile([P, W, 2], U32, name="first1", align_bytes=64)
-        rest1 = keep.tile([P, 2, S - W], U32, name="rest1")
+        rest1 = {
+            1: keep.tile([P, 2, W], U32, name="rest11")[:],
+            2: window[1][:, T : T + 2 * W].bitcast(U32).rearrange("p (u s) -> p u s", u=2),
+        }
 
-        def weave(copy, dtype, rest, i, tag):
+        def weave(copy, dtype, rest, tag):
             woven = keep.tile([P, W, 2], U32, name=f"woven_{tag}", tag=tag, align_bytes=64)
-            copy(woven[:].bitcast(dtype), rest[:, :, (i - 1) * W : i * W].bitcast(dtype).rearrange("p u s -> p s u"))
+            copy(woven[:].bitcast(dtype), rest.bitcast(dtype).rearrange("p u s -> p s u"))
             return woven[:]
 
         for u in range(2):
@@ -181,28 +184,31 @@ def tile_moe_res_lin_bias_kernel(tc, xT, xr, w_words, w_scales, b, gate, offs, o
         round_plane(1, 0)
         for e in range(PIECE):
             one_pass(0, e, 0)
-        woven = weave(nc.scalar.copy, U32, rest0, 1, "raw100")
+        woven = weave(nc.scalar.copy, U32, rest0[:, :, 0:W], "raw100")
         gather(first1[:, :, 0], 1, 0, 0, 1)
-        gather(rest1[:, 0, :], 1, 0, 1, PIECES)
+        for i in range(1, PIECES):
+            gather(rest1[i][:, 0, :], 1, 0, i, i + 1)
         round_plane(1, 1)
-        later = weave(nc.scalar.copy, U32, rest0, 2, "raw110")
+        later = weave(nc.scalar.copy, U32, rest0[:, :, W : 2 * W], "raw110")
         gather(first1[:, :, 1], 1, 1, 0, 1)
         quantise(0, 1, 2, woven, "raw111")
         quantise(1, 0, 1, first1[:])
-        gather(rest1[:, 1, 0:W], 1, 1, 1, 2)
+        gather(rest1[1][:, 1, :], 1, 1, 1, 2)
         quantise(0, 2, 3, later)
-        woven = weave(nc.vector.tensor_copy, I32, rest1, 1, "own")
-        gather(rest1[:, 1, W : 2 * W], 1, 1, 2, 3)
-        quantise(1, 1, 2, woven)
+        woven = weave(nc.scalar.copy, U32, rest1[1], "own")
+        gather(rest1[2][:, 1, :], 1, 1, 2, 3)
         for e in range(PIECE):
             one_pass(0, e, 1)
-            add_bias(0, e)
-            times_gate(0, e * C, (e + 1) * C)
+            slots = slice(e * C, (e + 1) * C)
+            nc.vector.scalar_tensor_tensor(
+                scaled[0][:, slots], sums[0][e], bias[:, 0, e : e + 1], gates[0][:, slots], ADD, MULT
+            )
         multiply(1, 0)
-        woven = weave(nc.scalar.copy, U32, rest1, 2, "codes10")
+        quantise(1, 1, 2, woven)
         leave_bank(1, 0)
-        quantise(1, 2, 3, woven)
+        woven = weave(nc.scalar.copy, U32, rest1[2], "codes10")
         scatter(0, 0, 1)
+        quantise(1, 2, 3, woven)
         for h, i in ((0, 1), (0, 2), (1, 1), (1, 2)):
             multiply(h, i)
             leave_bank(h, i)

@@ -23,7 +23,7 @@ FP4X4 = mybir.dt.float4_e2m1fn_x4
 ADD, MULT = mybir.AluOpType.add, mybir.AluOpType.mult
 IDENTITY = mybir.ActivationFunctionType.Identity
 
-CUTS = (0, 768, T)
+SCALAR_TOKENS = (432, 448, 560, 896)
 PIECE = 2
 PIECES = E // PIECE
 W = PIECE * C
@@ -53,14 +53,20 @@ def tile_moe_res_lin_bias_kernel(tc, xT, xr, w_words, w_scales, b, gate, offs, o
             nc.vector.memset(window[h][:, 0:T], 0.0)
 
         raws = {}
-        for a, u in planes:
-            rows = xT[a * K_PASS : (a + 1) * K_PASS, :].rearrange("(p j) w -> p j w", j=4)
-            for c in range(2):
-                raw = keep.tile([P, 2, CUTS[c + 1] - CUTS[c]], F32, name=f"raw{a}{u}{c}", align_bytes=64)
-                nc.sync.dma_start(raw[:], rows[:, 2 * u : 2 * u + 2, CUTS[c] : CUTS[c + 1]])
-                raws[a, u, c] = raw
-                if (a, u, c) == (0, 0, 0):
-                    nc.sync.dma_start(offsets[:], offs)
+        for n, (a, u) in enumerate(planes):
+            rows = xT[a * K_PASS : (a + 1) * K_PASS, :].rearrange("(p j) w -> p j w", j=4)[:, 2 * u : 2 * u + 2, :]
+            cut = SCALAR_TOKENS[n]
+            if n < len(planes) - 1:
+                raw = keep.tile([P, 2, T], F32, name=f"raw{a}{u}", align_bytes=64)
+                nc.sync.dma_start(raw[:], rows)
+                raws[a, u, 0], raws[a, u, 1] = raw[:, :, 0:cut], raw[:, :, cut:T]
+            else:
+                for c, (t0, t1) in enumerate(((0, cut), (cut, T))):
+                    raw = keep.tile([P, 2, t1 - t0], F32, name=f"raw{a}{u}{c}", align_bytes=64)
+                    nc.sync.dma_start(raw[:], rows[:, :, t0:t1])
+                    raws[a, u, c] = raw[:]
+            if n == 0:
+                nc.sync.dma_start(offsets[:], offs)
 
         code_rows = w_words.rearrange("e a p n -> p (e a) n")
 
@@ -84,15 +90,16 @@ def tile_moe_res_lin_bias_kernel(tc, xT, xr, w_words, w_scales, b, gate, offs, o
         pairs = {}
 
         def round_tokens(copy, a, u, c):
-            dst = pairs[a, u][:, CUTS[c] : CUTS[c + 1]].bitcast(BF16).rearrange("p (w e) -> p w e", e=2)
-            copy(dst, raws[a, u, c][:].rearrange("p e w -> p w e"))
+            cuts = (0, SCALAR_TOKENS[2 * a + u], T)
+            dst = pairs[a, u][:, cuts[c] : cuts[c + 1]].bitcast(BF16).rearrange("p (w e) -> p w e", e=2)
+            copy(dst, raws[a, u, c].rearrange("p e w -> p w e"))
 
         def on_scalar(dst, src):
             nc.scalar.activation(dst, src, IDENTITY)
 
         def round_plane(a, u):
             pairs[a, u] = keep.tile([P, T], U32, name=f"pairs{a}{u}", align_bytes=64)
-            round_tokens(nc.vector.tensor_copy if (a, u) == (0, 0) else on_scalar, a, u, 0)
+            round_tokens(on_scalar, a, u, 0)
             round_tokens(nc.vector.tensor_copy, a, u, 1)
 
         def gather(dst, a, u, i0, i1):
@@ -184,19 +191,19 @@ def tile_moe_res_lin_bias_kernel(tc, xT, xr, w_words, w_scales, b, gate, offs, o
         round_plane(1, 0)
         for e in range(PIECE):
             one_pass(0, e, 0)
-        woven = weave(nc.scalar.copy, U32, rest0[:, :, 0:W], "raw100")
+        woven = weave(nc.scalar.copy, U32, rest0[:, :, 0:W], "raw10")
         gather(first1[:, :, 0], 1, 0, 0, 1)
         for i in range(1, PIECES):
             gather(rest1[i][:, 0, :], 1, 0, i, i + 1)
+        quantise(0, 1, 2, woven)
         round_plane(1, 1)
         later = weave(nc.scalar.copy, U32, rest0[:, :, W : 2 * W], "raw110")
         gather(first1[:, :, 1], 1, 1, 0, 1)
-        quantise(0, 1, 2, woven, "raw111")
-        quantise(1, 0, 1, first1[:])
         gather(rest1[1][:, 1, :], 1, 1, 1, 2)
-        quantise(0, 2, 3, later)
+        quantise(1, 0, 1, first1[:])
         woven = weave(nc.scalar.copy, U32, rest1[1], "own")
         gather(rest1[2][:, 1, :], 1, 1, 2, 3)
+        quantise(0, 2, 3, later)
         for e in range(PIECE):
             one_pass(0, e, 1)
             slots = slice(e * C, (e + 1) * C)

@@ -23,7 +23,8 @@ FP4X4 = mybir.dt.float4_e2m1fn_x4
 ADD, MULT = mybir.AluOpType.add, mybir.AluOpType.mult
 IDENTITY = mybir.ActivationFunctionType.Identity
 
-SCALAR_TOKENS = (432, 448, 560, 896)
+LOAD_CUT = (640, 640, 768, 768)
+SCALAR_CUT = (920, 920, 768, 768)
 PIECE = 2
 PIECES = E // PIECE
 W = PIECE * C
@@ -40,9 +41,7 @@ def tile_moe_res_lin_bias_kernel(tc, xT, xr, w_words, w_scales, b, gate, offs, o
 
         w_code = keep.tile([P, E * PASSES, 2 * N], U8, name="w_code", align_bytes=64)
         w_scale = keep.tile([P, E * PASSES * N], U8, name="w_scale", align_bytes=64)
-        window = [keep.tile([P, T + 2 * W * h], F32, name=f"window{h}") for h in range(HALVES)]
-        result = [keep.tile([P, S], F32, name=f"result{h}") for h in range(HALVES)]
-        scaled = [keep.tile([P, S], F32, name=f"scaled{h}") for h in range(HALVES)]
+        window = [keep.tile([P, T], F32, name=f"window{h}") for h in range(HALVES)]
         total = [keep.tile([P, T], F32, name=f"total{h}") for h in range(HALVES)]
         residual = [keep.tile([P, T], F32, name=f"residual{h}") for h in range(HALVES)]
         bias = keep.tile([P, HALVES, 8], F32, name="bias")
@@ -52,21 +51,23 @@ def tile_moe_res_lin_bias_kernel(tc, xT, xr, w_words, w_scales, b, gate, offs, o
         for h in range(HALVES):
             nc.vector.memset(window[h][:, 0:T], 0.0)
 
+        def on_scalar(dst, src):
+            nc.scalar.activation(dst, src, IDENTITY)
+
         raws = {}
         for n, (a, u) in enumerate(planes):
             rows = xT[a * K_PASS : (a + 1) * K_PASS, :].rearrange("(p j) w -> p j w", j=4)[:, 2 * u : 2 * u + 2, :]
-            cut = SCALAR_TOKENS[n]
-            if n < len(planes) - 1:
-                raw = keep.tile([P, 2, T], F32, name=f"raw{a}{u}", align_bytes=64)
-                nc.sync.dma_start(raw[:], rows)
-                raws[a, u, 0], raws[a, u, 1] = raw[:, :, 0:cut], raw[:, :, cut:T]
-            else:
-                for c, (t0, t1) in enumerate(((0, cut), (cut, T))):
-                    raw = keep.tile([P, 2, t1 - t0], F32, name=f"raw{a}{u}{c}", align_bytes=64)
-                    nc.sync.dma_start(raw[:], rows[:, :, t0:t1])
-                    raws[a, u, c] = raw[:]
+            cut, share = LOAD_CUT[n], SCALAR_CUT[n]
+            early = keep.tile([P, 2, cut], F32, name=f"early{a}{u}", align_bytes=64)
+            nc.sync.dma_start(early[:], rows[:, :, 0:cut])
             if n == 0:
                 nc.sync.dma_start(offsets[:], offs)
+            late = keep.tile([P, 2, T - cut], F32, name=f"late{a}{u}", align_bytes=64)
+            nc.sync.dma_start(late[:], rows[:, :, cut:T])
+            raws[a, u] = [(on_scalar, 0, cut, early[:])]
+            if share > cut:
+                raws[a, u].append((on_scalar, cut, share, late[:, :, 0 : share - cut]))
+            raws[a, u].append((nc.vector.tensor_copy, share, T, late[:, :, share - cut :]))
 
         code_rows = w_words.rearrange("e a p n -> p (e a) n")
 
@@ -89,18 +90,11 @@ def tile_moe_res_lin_bias_kernel(tc, xT, xr, w_words, w_scales, b, gate, offs, o
 
         pairs = {}
 
-        def round_tokens(copy, a, u, c):
-            cuts = (0, SCALAR_TOKENS[2 * a + u], T)
-            dst = pairs[a, u][:, cuts[c] : cuts[c + 1]].bitcast(BF16).rearrange("p (w e) -> p w e", e=2)
-            copy(dst, raws[a, u, c].rearrange("p e w -> p w e"))
-
-        def on_scalar(dst, src):
-            nc.scalar.activation(dst, src, IDENTITY)
-
         def round_plane(a, u):
             pairs[a, u] = keep.tile([P, T], U32, name=f"pairs{a}{u}", align_bytes=64)
-            round_tokens(on_scalar, a, u, 0)
-            round_tokens(nc.vector.tensor_copy, a, u, 1)
+            for copy, t0, t1, raw in raws[a, u]:
+                dst = pairs[a, u][:, t0:t1].bitcast(BF16).rearrange("p (w e) -> p w e", e=2)
+                copy(dst, raw.rearrange("p e w -> p w e"))
 
         def gather(dst, a, u, i0, i1):
             nc.vector.tensor_copy(dst, pairs[a, u][:].indirect(offsets[:, i0 * W // 16 : i1 * W // 16]))
@@ -109,10 +103,10 @@ def tile_moe_res_lin_bias_kernel(tc, xT, xr, w_words, w_scales, b, gate, offs, o
 
         def quantise(a, i0, i1, woven, tag=""):
             n = (i1 - i0) * W
-            code = keep.tile([P, n], U32, name=f"codes{a}{i0}", tag=tag, align_bytes=64)
+            code = keep.tile([P, n], U32, name=f"codes{a}{i0}", tag=tag, align_bytes=64)[:]
             scale = keep.tile([P, n], U8, name=f"scales{a}{i0}", align_bytes=64)
             nc.vector.quantize_mx(
-                out=code[:].bitcast(FP8X4),
+                out=code.bitcast(FP8X4),
                 scales=scale[:],
                 in_=woven.rearrange("p s u -> p (s u)").bitcast(BF16),
             )
@@ -149,79 +143,68 @@ def tile_moe_res_lin_bias_kernel(tc, xT, xr, w_words, w_scales, b, gate, offs, o
                 for a in range(PASSES):
                     one_pass(h, e, a)
 
-        def add_bias(h, e):
-            nc.scalar.activation(result[h][:, e * C : (e + 1) * C], sums[h][e], IDENTITY, bias=bias[:, h, e : e + 1])
+        def add_bias(h, i):
+            result = keep.tile([P, W], F32, name=f"result{h}{i}", align_bytes=64)
+            for j in range(PIECE):
+                e = i * PIECE + j
+                nc.scalar.activation(result[:, j * C : (j + 1) * C], sums[h][e], IDENTITY, bias=bias[:, h, e : e + 1])
+            return result[:]
 
-        def times_gate(h, s0, s1):
-            i = s0 // W
-            nc.gpsimd.tensor_tensor(scaled[h][:, s0:s1], result[h][:, s0:s1], gates[i][:, s0 - i * W : s1 - i * W], MULT)
+        def times_gate(scaled, result, i):
+            nc.gpsimd.tensor_tensor(scaled, result, gates[i][:], MULT)
 
-        def leave_bank(h, i):
-            for e in range(i * PIECE, (i + 1) * PIECE):
-                add_bias(h, e)
-            times_gate(h, i * W, (i + 1) * W)
-
-        def scatter(h, i0, i1):
+        def scatter(h, i0, i1, scaled):
             part = slice(i0 * W // 16, i1 * W // 16)
-            nc.vector.tensor_copy(window[h][:].indirect(offsets[:, part]), scaled[h][:, i0 * W : i1 * W])
+            nc.vector.tensor_copy(window[h][:].indirect(offsets[:, part]), scaled)
 
         def finish(engine, h, cuts):
             for t0, t1 in cuts:
                 engine.tensor_tensor(total[h][:, t0:t1], window[h][:, t0:t1], residual[h][:, t0:t1], ADD)
                 nc.sync.dma_start(out[h * P : (h + 1) * P, t0:t1], total[h][:, t0:t1])
 
-        first0 = keep.tile([P, W, 2], U32, name="first0", align_bytes=64)
-        rest0 = keep.tile([P, 2, S - W], U32, name="rest0")
-        first1 = keep.tile([P, W, 2], U32, name="first1", align_bytes=64)
-        rest1 = {
-            1: keep.tile([P, 2, W], U32, name="rest11")[:],
-            2: window[1][:, T : T + 2 * W].bitcast(U32).rearrange("p (u s) -> p u s", u=2),
-        }
-
-        def weave(copy, dtype, rest, tag):
-            woven = keep.tile([P, W, 2], U32, name=f"woven_{tag}", tag=tag, align_bytes=64)
-            copy(woven[:].bitcast(dtype), rest.bitcast(dtype).rearrange("p u s -> p s u"))
+        def weave(plain, i0, i1, name, tag=""):
+            woven = keep.tile([P, (i1 - i0) * W, 2], U32, name=name, tag=tag, align_bytes=64)
+            nc.scalar.copy(woven[:], plain[:, :, i0 * W : i1 * W].rearrange("p u s -> p s u"))
             return woven[:]
 
+        plain = [keep.tile([P, 2, S], U32, name=f"plain{a}") for a in range(PASSES)]
         for u in range(2):
             round_plane(0, u)
-            gather(first0[:, :, u], 0, u, 0, 1)
-            gather(rest0[:, u, :], 0, u, 1, PIECES)
-        quantise(0, 0, 1, first0[:])
+            gather(plain[0][:, u, :], 0, u, 0, PIECES)
         round_plane(1, 0)
+        woven = weave(plain[0], 0, 2, "woven00", "early10")
+        gather(plain[1][:, 0, :], 1, 0, 0, PIECES)
+        quantise(0, 0, 2, woven)
         for e in range(PIECE):
             one_pass(0, e, 0)
-        woven = weave(nc.scalar.copy, U32, rest0[:, :, 0:W], "raw10")
-        gather(first1[:, :, 0], 1, 0, 0, 1)
-        for i in range(1, PIECES):
-            gather(rest1[i][:, 0, :], 1, 0, i, i + 1)
-        quantise(0, 1, 2, woven)
         round_plane(1, 1)
-        later = weave(nc.scalar.copy, U32, rest0[:, :, W : 2 * W], "raw110")
-        gather(first1[:, :, 1], 1, 1, 0, 1)
-        gather(rest1[1][:, 1, :], 1, 1, 1, 2)
-        quantise(1, 0, 1, first1[:])
-        woven = weave(nc.scalar.copy, U32, rest1[1], "own")
-        gather(rest1[2][:, 1, :], 1, 1, 2, 3)
-        quantise(0, 2, 3, later)
+        woven02 = weave(plain[0], 2, 3, "woven02", "early11")
+        woven1 = []
+        for i in range(PIECES):
+            gather(plain[1][:, 1, i * W : (i + 1) * W], 1, 1, i, i + 1)
+            woven1.append(weave(plain[1], i, i + 1, f"woven1{i}"))
+        quantise(1, 0, 1, woven1[0])
+        quantise(0, 2, 3, woven02)
+        quantise(1, 1, 2, woven1[1])
+        scaled00 = keep.tile([P, W], F32, name="scaled00")
         for e in range(PIECE):
             one_pass(0, e, 1)
             slots = slice(e * C, (e + 1) * C)
             nc.vector.scalar_tensor_tensor(
-                scaled[0][:, slots], sums[0][e], bias[:, 0, e : e + 1], gates[0][:, slots], ADD, MULT
+                scaled00[:, slots], sums[0][e], bias[:, 0, e : e + 1], gates[0][:, slots], ADD, MULT
             )
         multiply(1, 0)
-        quantise(1, 1, 2, woven)
-        leave_bank(1, 0)
-        woven = weave(nc.scalar.copy, U32, rest1[2], "codes10")
-        scatter(0, 0, 1)
-        quantise(1, 2, 3, woven)
-        for h, i in ((0, 1), (0, 2), (1, 1), (1, 2)):
-            multiply(h, i)
-            leave_bank(h, i)
-        scatter(1, 0, 1)
-        scatter(0, 1, 2)
-        scatter(0, 2, 3)
+        quantise(1, 2, 3, woven1[2], "codes10")
+        scaled10 = keep.tile([P, W], F32, name="scaled10")
+        times_gate(scaled10[:], add_bias(1, 0), 0)
+        scatter(0, 0, 1, scaled00[:])
+        scatter(1, 0, 1, scaled10[:])
+        later = [keep.tile([P, S - W], F32, name=f"later{h}") for h in range(HALVES)]
+        for h in range(HALVES):
+            for i in range(1, PIECES):
+                multiply(h, i)
+                times_gate(later[h][:, (i - 1) * W : i * W], add_bias(h, i), i)
+        scatter(0, 1, PIECES, later[0][:])
         finish(nc.gpsimd, 0, ((0, 640), (640, T)))
-        scatter(1, 1, 3)
-        finish(nc.vector, 1, ((0, 512), (512, 1024), (1024, T)))
+        scatter(1, 1, PIECES, later[1][:])
+        finish(nc.vector, 1, ((0, 320), (320, 768), (768, T)))

@@ -23,8 +23,8 @@ FP4X4 = mybir.dt.float4_e2m1fn_x4
 ADD, MULT = mybir.AluOpType.add, mybir.AluOpType.mult
 IDENTITY = mybir.ActivationFunctionType.Identity
 
-LOAD_CUT = (640, 640, 768, 768)
-SCALAR_CUT = (920, 920, 768, 768)
+LOAD_CUT = (T, 640, 640, 704)
+SCALAR_CUT = (512, 920, 896, 704)
 PIECE = 2
 PIECES = E // PIECE
 W = PIECE * C
@@ -45,7 +45,9 @@ def tile_moe_res_lin_bias_kernel(tc, xT, xr, w_words, w_scales, b, gate, offs, o
         total = [keep.tile([P, T], F32, name=f"total{h}") for h in range(HALVES)]
         residual = [keep.tile([P, T], F32, name=f"residual{h}") for h in range(HALVES)]
         bias = keep.tile([P, HALVES, 8], F32, name="bias")
-        gates = [keep.tile([P, W], F32, name=f"gates{i}") for i in range(PIECES)]
+        first_gates = keep.tile([P, W], F32, name="first_gates")
+        later_gates = keep.tile([P, S - W], F32, name="later_gates")
+        gates = [first_gates[:], later_gates[:, 0:W], later_gates[:, W : 2 * W]]
 
         nc.gpsimd.memset(w_scale[:].bitcast(I32), 0)
         for h in range(HALVES):
@@ -62,29 +64,34 @@ def tile_moe_res_lin_bias_kernel(tc, xT, xr, w_words, w_scales, b, gate, offs, o
             nc.sync.dma_start(early[:], rows[:, :, 0:cut])
             if n == 0:
                 nc.sync.dma_start(offsets[:], offs)
-            late = keep.tile([P, 2, T - cut], F32, name=f"late{a}{u}", align_bytes=64)
-            nc.sync.dma_start(late[:], rows[:, :, cut:T])
-            raws[a, u] = [(on_scalar, 0, cut, early[:])]
-            if share > cut:
-                raws[a, u].append((on_scalar, cut, share, late[:, :, 0 : share - cut]))
-            raws[a, u].append((nc.vector.tensor_copy, share, T, late[:, :, share - cut :]))
+            if cut == T:
+                raws[a, u] = [
+                    (on_scalar, 0, share, early[:, :, 0:share]),
+                    (nc.vector.tensor_copy, share, T, early[:, :, share:T]),
+                ]
+            else:
+                late = keep.tile([P, 2, T - cut], F32, name=f"late{a}{u}", align_bytes=64)
+                nc.sync.dma_start(late[:], rows[:, :, cut:T])
+                raws[a, u] = [(on_scalar, 0, cut, early[:])]
+                if share > cut:
+                    raws[a, u].append((on_scalar, cut, share, late[:, :, 0 : share - cut]))
+                raws[a, u].append((nc.vector.tensor_copy, share, T, late[:, :, share - cut :]))
 
         code_rows = w_words.rearrange("e a p n -> p (e a) n")
 
-        def load_codes(i):
-            g = slice(i * PIECE * PASSES, (i + 1) * PIECE * PASSES)
+        def load_codes(i0, i1):
+            g = slice(i0 * PIECE * PASSES, i1 * PIECE * PASSES)
             nc.sync.dma_start(w_code[:, g, :], code_rows[:, g, :])
 
         nc.sync.dma_start(bias[:, :, 0:E], b.rearrange("(h p) e -> p h e", p=P))
-        load_codes(0)
+        load_codes(0, 1)
         w_scale_words = w_scale[:].bitcast(I32).rearrange("p (g n) -> p g n", g=E * PASSES)
         scale_rows = w_scales.bitcast(I32).rearrange("e a (q r) n -> r q (e a) n", r=4)
         for r in range(4):
             nc.sync.dma_start(w_scale_words[r:P:32], scale_rows[r])
-        nc.sync.dma_start(gates[0][:], gate[0:P, 0:W])
-        for i in range(1, PIECES):
-            load_codes(i)
-            nc.sync.dma_start(gates[i][:], gate[0:P, i * W : (i + 1) * W])
+        nc.sync.dma_start(gates[0], gate[0:P, 0:W])
+        load_codes(1, PIECES)
+        nc.sync.dma_start(later_gates[:], gate[0:P, W:S])
         for h in range(HALVES):
             nc.sync.dma_start(residual[h][:], xr[h * P : (h + 1) * P, :])
 
@@ -125,7 +132,7 @@ def tile_moe_res_lin_bias_kernel(tc, xT, xr, w_words, w_scales, b, gate, offs, o
                     for j in range(PIECE):
                         sums[h][i * PIECE + j] = bank[:, j * C : (j + 1) * C]
 
-        def one_pass(h, e, a):
+        def one_pass(h, e, a, first):
             i, j = divmod(e, PIECE)
             g = e * PASSES + a
             nc.tensor.matmul_mx(
@@ -134,14 +141,14 @@ def tile_moe_res_lin_bias_kernel(tc, xT, xr, w_words, w_scales, b, gate, offs, o
                 lhsT_scale=w_scale[:, g * N + h * P : g * N + (h + 1) * P],
                 rhs=codes[a, i][:, j * C : (j + 1) * C].bitcast(FP8X4),
                 rhs_scale=scales[a, i][:, j * C : (j + 1) * C],
-                start=(a == 0),
-                stop=(a == PASSES - 1),
+                start=(a == first),
+                stop=(a != first),
             )
 
         def multiply(h, i):
             for e in range(i * PIECE, (i + 1) * PIECE):
-                for a in range(PASSES):
-                    one_pass(h, e, a)
+                for a in reversed(range(PASSES)):
+                    one_pass(h, e, a, PASSES - 1)
 
         def add_bias(h, i):
             result = keep.tile([P, W], F32, name=f"result{h}{i}", align_bytes=64)
@@ -151,7 +158,7 @@ def tile_moe_res_lin_bias_kernel(tc, xT, xr, w_words, w_scales, b, gate, offs, o
             return result[:]
 
         def times_gate(scaled, result, i):
-            nc.gpsimd.tensor_tensor(scaled, result, gates[i][:], MULT)
+            nc.gpsimd.tensor_tensor(scaled, result, gates[i], MULT)
 
         def scatter(h, i0, i1, scaled):
             part = slice(i0 * W // 16, i1 * W // 16)
@@ -172,13 +179,14 @@ def tile_moe_res_lin_bias_kernel(tc, xT, xr, w_words, w_scales, b, gate, offs, o
             round_plane(0, u)
             gather(plain[0][:, u, :], 0, u, 0, PIECES)
         round_plane(1, 0)
-        woven = weave(plain[0], 0, 2, "woven00", "early10")
+        woven = weave(plain[0], 0, 2, "woven00", "late10")
         gather(plain[1][:, 0, :], 1, 0, 0, PIECES)
-        quantise(0, 0, 2, woven)
+        quantise(0, 0, 1, woven[:, 0:W, :])
         for e in range(PIECE):
-            one_pass(0, e, 0)
+            one_pass(0, e, 0, 0)
         round_plane(1, 1)
-        woven02 = weave(plain[0], 2, 3, "woven02", "early11")
+        quantise(0, 1, 2, woven[:, W : 2 * W, :], "early11")
+        woven02 = weave(plain[0], 2, 3, "woven02", "late11")
         woven1 = []
         for i in range(PIECES):
             gather(plain[1][:, 1, i * W : (i + 1) * W], 1, 1, i, i + 1)
@@ -188,7 +196,7 @@ def tile_moe_res_lin_bias_kernel(tc, xT, xr, w_words, w_scales, b, gate, offs, o
         quantise(1, 1, 2, woven1[1])
         scaled00 = keep.tile([P, W], F32, name="scaled00")
         for e in range(PIECE):
-            one_pass(0, e, 1)
+            one_pass(0, e, 1, 0)
             slots = slice(e * C, (e + 1) * C)
             nc.vector.scalar_tensor_tensor(
                 scaled00[:, slots], sums[0][e], bias[:, 0, e : e + 1], gates[0][:, slots], ADD, MULT
@@ -207,4 +215,4 @@ def tile_moe_res_lin_bias_kernel(tc, xT, xr, w_words, w_scales, b, gate, offs, o
         scatter(0, 1, PIECES, later[0][:])
         finish(nc.gpsimd, 0, ((0, 640), (640, T)))
         scatter(1, 1, PIECES, later[1][:])
-        finish(nc.vector, 1, ((0, 320), (320, 768), (768, T)))
+        finish(nc.vector, 1, ((0, 448), (448, 896), (896, T)))

@@ -192,8 +192,8 @@ def tile_moe_res_lin_bias_kernel(tc, xT, xr, w_words, w_scales, b, gate, offs, o
             gather(plain[1][:, 1, i * W : (i + 1) * W], 1, 1, i, i + 1)
             woven1.append(weave(plain[1], i, i + 1, f"woven1{i}"))
         quantise(1, 0, 1, woven1[0])
-        quantise(0, 2, 3, woven02)
         quantise(1, 1, 2, woven1[1])
+        quantise(0, 2, 3, woven02, "woven10")
         scaled00 = keep.tile([P, W], F32, name="scaled00")
         for e in range(PIECE):
             one_pass(0, e, 1, 0)

@@ -23,8 +23,9 @@ FP4X4 = mybir.dt.float4_e2m1fn_x4
 ADD, MULT = mybir.AluOpType.add, mybir.AluOpType.mult
 IDENTITY = mybir.ActivationFunctionType.Identity
 
-LOAD_CUT = (T, 640, 640, 704)
-SCALAR_CUT = (512, 920, 896, 704)
+ALIGN = 256
+LOAD_CUT = (T, 704, 704, 704)
+SCALAR_CUT = (512, 704, 704, 704)
 PIECE = 2
 PIECES = E // PIECE
 W = PIECE * C
@@ -39,14 +40,14 @@ def tile_moe_res_lin_bias_kernel(tc, xT, xr, w_words, w_scales, b, gate, offs, o
         offsets = keep.tile([P, S // 16], U16, name="offsets")
         planes = [(a, u) for a in range(PASSES) for u in range(2)]
 
-        w_code = keep.tile([P, E * PASSES, 2 * N], U8, name="w_code", align_bytes=64)
-        w_scale = keep.tile([P, E * PASSES * N], U8, name="w_scale", align_bytes=64)
-        window = [keep.tile([P, T], F32, name=f"window{h}") for h in range(HALVES)]
-        total = [keep.tile([P, T], F32, name=f"total{h}") for h in range(HALVES)]
-        residual = [keep.tile([P, T], F32, name=f"residual{h}") for h in range(HALVES)]
+        w_code = keep.tile([P, E * PASSES, 2 * N], U8, name="w_code", align_bytes=ALIGN)
+        w_scale = keep.tile([P, E * PASSES * N], U8, name="w_scale", align_bytes=ALIGN)
+        window = [keep.tile([P, T], F32, name=f"window{h}", align_bytes=ALIGN) for h in range(HALVES)]
+        total = [keep.tile([P, T], F32, name=f"total{h}", align_bytes=ALIGN) for h in range(HALVES)]
+        residual = [keep.tile([P, T], F32, name=f"residual{h}", align_bytes=ALIGN) for h in range(HALVES)]
         bias = keep.tile([P, HALVES, 8], F32, name="bias")
-        first_gates = keep.tile([P, W], F32, name="first_gates")
-        later_gates = keep.tile([P, S - W], F32, name="later_gates")
+        first_gates = keep.tile([P, W], F32, name="first_gates", align_bytes=ALIGN)
+        later_gates = keep.tile([P, S - W], F32, name="later_gates", align_bytes=ALIGN)
         gates = [first_gates[:], later_gates[:, 0:W], later_gates[:, W : 2 * W]]
 
         nc.gpsimd.memset(w_scale[:].bitcast(I32), 0)
@@ -60,17 +61,23 @@ def tile_moe_res_lin_bias_kernel(tc, xT, xr, w_words, w_scales, b, gate, offs, o
         for n, (a, u) in enumerate(planes):
             rows = xT[a * K_PASS : (a + 1) * K_PASS, :].rearrange("(p j) w -> p j w", j=4)[:, 2 * u : 2 * u + 2, :]
             cut, share = LOAD_CUT[n], SCALAR_CUT[n]
-            early = keep.tile([P, 2, cut], F32, name=f"early{a}{u}", align_bytes=64)
-            nc.sync.dma_start(early[:], rows[:, :, 0:cut])
-            if n == 0:
-                nc.sync.dma_start(offsets[:], offs)
-            if cut == T:
+            if n < len(planes) - 1:
+                run = rows.rearrange("p e w -> p (e w)")
+                raw = keep.tile([P, 2 * T], F32, name=f"raw{a}{u}", align_bytes=ALIGN)
+                nc.sync.dma_start(raw[:, 0 : T + cut], run[:, 0 : T + cut])
+                if n == 0:
+                    nc.sync.dma_start(offsets[:], offs)
+                if cut < T:
+                    nc.sync.dma_start(raw[:, T + cut :], run[:, T + cut :])
+                both = raw[:].rearrange("p (e w) -> p e w", e=2)
                 raws[a, u] = [
-                    (on_scalar, 0, share, early[:, :, 0:share]),
-                    (nc.vector.tensor_copy, share, T, early[:, :, share:T]),
+                    (on_scalar, 0, share, both[:, :, 0:share]),
+                    (nc.vector.tensor_copy, share, T, both[:, :, share:T]),
                 ]
             else:
-                late = keep.tile([P, 2, T - cut], F32, name=f"late{a}{u}", align_bytes=64)
+                early = keep.tile([P, 2, cut], F32, name=f"early{a}{u}", align_bytes=ALIGN)
+                nc.sync.dma_start(early[:], rows[:, :, 0:cut])
+                late = keep.tile([P, 2, T - cut], F32, name=f"late{a}{u}", align_bytes=ALIGN)
                 nc.sync.dma_start(late[:], rows[:, :, cut:T])
                 raws[a, u] = [(on_scalar, 0, cut, early[:])]
                 if share > cut:
@@ -98,7 +105,7 @@ def tile_moe_res_lin_bias_kernel(tc, xT, xr, w_words, w_scales, b, gate, offs, o
         pairs = {}
 
         def round_plane(a, u):
-            pairs[a, u] = keep.tile([P, T], U32, name=f"pairs{a}{u}", align_bytes=64)
+            pairs[a, u] = keep.tile([P, T], U32, name=f"pairs{a}{u}", align_bytes=ALIGN)
             for copy, t0, t1, raw in raws[a, u]:
                 dst = pairs[a, u][:, t0:t1].bitcast(BF16).rearrange("p (w e) -> p w e", e=2)
                 copy(dst, raw.rearrange("p e w -> p w e"))
@@ -110,8 +117,8 @@ def tile_moe_res_lin_bias_kernel(tc, xT, xr, w_words, w_scales, b, gate, offs, o
 
         def quantise(a, i0, i1, woven, tag=""):
             n = (i1 - i0) * W
-            code = keep.tile([P, n], U32, name=f"codes{a}{i0}", tag=tag, align_bytes=64)[:]
-            scale = keep.tile([P, n], U8, name=f"scales{a}{i0}", align_bytes=64)
+            code = keep.tile([P, n], U32, name=f"codes{a}{i0}", tag=tag, align_bytes=ALIGN)[:]
+            scale = keep.tile([P, n], U8, name=f"scales{a}{i0}", align_bytes=ALIGN)
             nc.vector.quantize_mx(
                 out=code.bitcast(FP8X4),
                 scales=scale[:],
@@ -151,7 +158,7 @@ def tile_moe_res_lin_bias_kernel(tc, xT, xr, w_words, w_scales, b, gate, offs, o
                     one_pass(h, e, a, PASSES - 1)
 
         def add_bias(h, i):
-            result = keep.tile([P, W], F32, name=f"result{h}{i}", align_bytes=64)
+            result = keep.tile([P, W], F32, name=f"result{h}{i}", align_bytes=ALIGN)
             for j in range(PIECE):
                 e = i * PIECE + j
                 nc.scalar.activation(result[:, j * C : (j + 1) * C], sums[h][e], IDENTITY, bias=bias[:, h, e : e + 1])
@@ -170,7 +177,7 @@ def tile_moe_res_lin_bias_kernel(tc, xT, xr, w_words, w_scales, b, gate, offs, o
                 nc.sync.dma_start(out[h * P : (h + 1) * P, t0:t1], total[h][:, t0:t1])
 
         def weave(plain, i0, i1, name, tag=""):
-            woven = keep.tile([P, (i1 - i0) * W, 2], U32, name=name, tag=tag, align_bytes=64)
+            woven = keep.tile([P, (i1 - i0) * W, 2], U32, name=name, tag=tag, align_bytes=ALIGN)
             nc.scalar.copy(woven[:], plain[:, :, i0 * W : i1 * W].rearrange("p u s -> p s u"))
             return woven[:]
 
@@ -179,7 +186,7 @@ def tile_moe_res_lin_bias_kernel(tc, xT, xr, w_words, w_scales, b, gate, offs, o
             round_plane(0, u)
             gather(plain[0][:, u, :], 0, u, 0, PIECES)
         round_plane(1, 0)
-        woven = weave(plain[0], 0, 2, "woven00", "late10")
+        woven = weave(plain[0], 0, 2, "woven00", "raw10")
         gather(plain[1][:, 0, :], 1, 0, 0, PIECES)
         quantise(0, 0, 1, woven[:, 0:W, :])
         for e in range(PIECE):

@@ -24,8 +24,10 @@ ADD, MULT = mybir.AluOpType.add, mybir.AluOpType.mult
 IDENTITY = mybir.ActivationFunctionType.Identity
 
 ALIGN = 256
-LOAD_CUT = (T, 704, 704, 704)
-SCALAR_CUT = (512, 704, 704, 704)
+LOAD_CUT = (640, 640, 640, 704)
+SCALAR_CUT = (864, 920, 640, 960)
+SCALAR_FIRST = 208
+SECOND = 192
 PIECE = 2
 PIECES = E // PIECE
 W = PIECE * C
@@ -44,7 +46,8 @@ def tile_moe_res_lin_bias_kernel(tc, xT, xr, w_words, w_scales, b, gate, offs, o
         w_scale = keep.tile([P, E * PASSES * N], U8, name="w_scale", align_bytes=ALIGN)
         window = [keep.tile([P, T], F32, name=f"window{h}", align_bytes=ALIGN) for h in range(HALVES)]
         total = [keep.tile([P, T], F32, name=f"total{h}", align_bytes=ALIGN) for h in range(HALVES)]
-        residual = [keep.tile([P, T], F32, name=f"residual{h}", align_bytes=ALIGN) for h in range(HALVES)]
+        residuals = keep.tile([P, HALVES, T], F32, name="residuals", align_bytes=ALIGN)
+        residual = [residuals[:, h, :] for h in range(HALVES)]
         bias = keep.tile([P, HALVES, 8], F32, name="bias")
         first_gates = keep.tile([P, W], F32, name="first_gates", align_bytes=ALIGN)
         later_gates = keep.tile([P, S - W], F32, name="later_gates", align_bytes=ALIGN)
@@ -61,7 +64,7 @@ def tile_moe_res_lin_bias_kernel(tc, xT, xr, w_words, w_scales, b, gate, offs, o
         for n, (a, u) in enumerate(planes):
             rows = xT[a * K_PASS : (a + 1) * K_PASS, :].rearrange("(p j) w -> p j w", j=4)[:, 2 * u : 2 * u + 2, :]
             cut, share = LOAD_CUT[n], SCALAR_CUT[n]
-            if n < len(planes) - 1:
+            if n == 0:
                 run = rows.rearrange("p e w -> p (e w)")
                 raw = keep.tile([P, 2 * T], F32, name=f"raw{a}{u}", align_bytes=ALIGN)
                 nc.sync.dma_start(raw[:, 0 : T + cut], run[:, 0 : T + cut])
@@ -71,7 +74,9 @@ def tile_moe_res_lin_bias_kernel(tc, xT, xr, w_words, w_scales, b, gate, offs, o
                     nc.sync.dma_start(raw[:, T + cut :], run[:, T + cut :])
                 both = raw[:].rearrange("p (e w) -> p e w", e=2)
                 raws[a, u] = [
-                    (on_scalar, 0, share, both[:, :, 0:share]),
+                    (on_scalar, 0, SCALAR_FIRST, both[:, :, 0:SCALAR_FIRST]),
+                    (nc.vector.tensor_copy, SCALAR_FIRST, cut, both[:, :, SCALAR_FIRST:cut]),
+                    (on_scalar, cut, share, both[:, :, cut:share]),
                     (nc.vector.tensor_copy, share, T, both[:, :, share:T]),
                 ]
             else:
@@ -99,8 +104,7 @@ def tile_moe_res_lin_bias_kernel(tc, xT, xr, w_words, w_scales, b, gate, offs, o
         nc.sync.dma_start(gates[0], gate[0:P, 0:W])
         load_codes(1, PIECES)
         nc.sync.dma_start(later_gates[:], gate[0:P, W:S])
-        for h in range(HALVES):
-            nc.sync.dma_start(residual[h][:], xr[h * P : (h + 1) * P, :])
+        nc.sync.dma_start(residuals[:], xr.rearrange("(h p) t -> p h t", p=P))
 
         pairs = {}
 
@@ -167,14 +171,14 @@ def tile_moe_res_lin_bias_kernel(tc, xT, xr, w_words, w_scales, b, gate, offs, o
         def times_gate(scaled, result, i):
             nc.gpsimd.tensor_tensor(scaled, result, gates[i], MULT)
 
-        def scatter(h, i0, i1, scaled):
-            part = slice(i0 * W // 16, i1 * W // 16)
+        def scatter(h, s0, s1, scaled):
+            part = slice(s0 // 16, s1 // 16)
             nc.vector.tensor_copy(window[h][:].indirect(offsets[:, part]), scaled)
 
-        def finish(engine, h, cuts):
+        def finish(engine, queue, h, cuts):
             for t0, t1 in cuts:
                 engine.tensor_tensor(total[h][:, t0:t1], window[h][:, t0:t1], residual[h][:, t0:t1], ADD)
-                nc.sync.dma_start(out[h * P : (h + 1) * P, t0:t1], total[h][:, t0:t1])
+                queue.dma_start(out[h * P : (h + 1) * P, t0:t1], total[h][:, t0:t1])
 
         def weave(plain, i0, i1, name, tag=""):
             woven = keep.tile([P, (i1 - i0) * W, 2], U32, name=name, tag=tag, align_bytes=ALIGN)
@@ -186,7 +190,7 @@ def tile_moe_res_lin_bias_kernel(tc, xT, xr, w_words, w_scales, b, gate, offs, o
             round_plane(0, u)
             gather(plain[0][:, u, :], 0, u, 0, PIECES)
         round_plane(1, 0)
-        woven = weave(plain[0], 0, 2, "woven00", "raw10")
+        woven = weave(plain[0], 0, 2, "woven00", "early10")
         gather(plain[1][:, 0, :], 1, 0, 0, PIECES)
         quantise(0, 0, 1, woven[:, 0:W, :])
         for e in range(PIECE):
@@ -210,16 +214,17 @@ def tile_moe_res_lin_bias_kernel(tc, xT, xr, w_words, w_scales, b, gate, offs, o
             )
         multiply(1, 0)
         quantise(1, 2, 3, woven1[2], "codes10")
-        scaled10 = keep.tile([P, W], F32, name="scaled10")
-        times_gate(scaled10[:], add_bias(1, 0), 0)
-        scatter(0, 0, 1, scaled00[:])
-        scatter(1, 0, 1, scaled10[:])
-        later = [keep.tile([P, S - W], F32, name=f"later{h}") for h in range(HALVES)]
+        scaled1 = keep.tile([P, S], F32, name="scaled1")
+        times_gate(scaled1[:, 0:W], add_bias(1, 0), 0)
+        scatter(0, 0, W, scaled00[:])
+        scatter(1, 0, SECOND, scaled1[:, 0:SECOND])
+        later0 = keep.tile([P, S - W], F32, name="later0")
+        later = [later0[:], scaled1[:, W:S]]
         for h in range(HALVES):
             for i in range(1, PIECES):
                 multiply(h, i)
                 times_gate(later[h][:, (i - 1) * W : i * W], add_bias(h, i), i)
-        scatter(0, 1, PIECES, later[0][:])
-        finish(nc.gpsimd, 0, ((0, 640), (640, T)))
-        scatter(1, 1, PIECES, later[1][:])
-        finish(nc.vector, 1, ((0, 448), (448, 896), (896, T)))
+        scatter(0, W, S, later[0])
+        finish(nc.gpsimd, nc.sync, 0, ((0, 640), (640, T)))
+        scatter(1, SECOND, S, scaled1[:, SECOND:S])
+        finish(nc.vector, nc.scalar, 1, ((0, 448), (448, 896), (896, T)))

@@ -24,8 +24,8 @@ ADD, MULT = mybir.AluOpType.add, mybir.AluOpType.mult
 IDENTITY = mybir.ActivationFunctionType.Identity
 
 ALIGN = 256
-LOAD_CUT = (640, 640, 640, 704)
-SCALAR_CUT = (864, 920, 640, 960)
+LOAD_CUT = (T, 704, 640, 704)
+SCALAR_CUT = (512, 704, 640, 960)
 SCALAR_FIRST = 208
 SECOND = 192
 PIECE = 2
@@ -64,19 +64,17 @@ def tile_moe_res_lin_bias_kernel(tc, xT, xr, w_words, w_scales, b, gate, offs, o
         for n, (a, u) in enumerate(planes):
             rows = xT[a * K_PASS : (a + 1) * K_PASS, :].rearrange("(p j) w -> p j w", j=4)[:, 2 * u : 2 * u + 2, :]
             cut, share = LOAD_CUT[n], SCALAR_CUT[n]
-            if n == 0:
+            if n < 2:
                 run = rows.rearrange("p e w -> p (e w)")
                 raw = keep.tile([P, 2 * T], F32, name=f"raw{a}{u}", align_bytes=ALIGN)
                 nc.sync.dma_start(raw[:, 0 : T + cut], run[:, 0 : T + cut])
                 if n == 0:
                     nc.sync.dma_start(offsets[:], offs)
-                if cut < T:
+                else:
                     nc.sync.dma_start(raw[:, T + cut :], run[:, T + cut :])
                 both = raw[:].rearrange("p (e w) -> p e w", e=2)
                 raws[a, u] = [
-                    (on_scalar, 0, SCALAR_FIRST, both[:, :, 0:SCALAR_FIRST]),
-                    (nc.vector.tensor_copy, SCALAR_FIRST, cut, both[:, :, SCALAR_FIRST:cut]),
-                    (on_scalar, cut, share, both[:, :, cut:share]),
+                    (on_scalar, 0, share, both[:, :, 0:share]),
                     (nc.vector.tensor_copy, share, T, both[:, :, share:T]),
                 ]
             else:
@@ -227,4 +225,4 @@ def tile_moe_res_lin_bias_kernel(tc, xT, xr, w_words, w_scales, b, gate, offs, o
         scatter(0, W, S, later[0])
         finish(nc.gpsimd, nc.sync, 0, ((0, 640), (640, T)))
         scatter(1, SECOND, S, scaled1[:, SECOND:S])
-        finish(nc.vector, nc.scalar, 1, ((0, 448), (448, 896), (896, T)))
+        finish(nc.vector, nc.scalar, 1, ((0, 320), (320, 640), (640, 960), (960, T)))

@@ -8,6 +8,9 @@ P = 128
 K_PASS = 512
 PASSES = K // K_PASS
 HALVES = N // P
+PIECE = 2
+PIECES = E // PIECE
+W = PIECE * C
 
 FLOPS = 2 * S * K * N
 BYTES = 4 * K * T + 8 * N * T + E * K * N // 2 + E * K * N // 32 + 4 * N * E + 4 * S + 2 * P * S // 16
@@ -24,13 +27,11 @@ ADD, MULT = mybir.AluOpType.add, mybir.AluOpType.mult
 IDENTITY = mybir.ActivationFunctionType.Identity
 
 ALIGN = 256
-LOAD_CUT = (T, 704, 640, 704)
-SCALAR_CUT = (512, 704, 640, 960)
-SCALAR_FIRST = 208
-SECOND = 192
-PIECE = 2
-PIECES = E // PIECE
-W = PIECE * C
+BIAS_ROW = 8
+FIRST_LOAD = (T, 704, 640, 672)
+SCALAR_TOKENS = (512, 704, 640, 928)
+SECOND_SCATTER = 224
+GPSIMD_SUMS, VECTOR_SUMS = 2, 4
 
 
 def tile_moe_res_lin_bias_kernel(tc, xT, xr, w_words, w_scales, b, gate, offs, out):
@@ -40,58 +41,60 @@ def tile_moe_res_lin_bias_kernel(tc, xT, xr, w_words, w_scales, b, gate, offs, o
         psum = ctx.enter_context(tc.psum_pool(name="psum", bufs=1))
 
         offsets = keep.tile([P, S // 16], U16, name="offsets")
-        planes = [(a, u) for a in range(PASSES) for u in range(2)]
-
         w_code = keep.tile([P, E * PASSES, 2 * N], U8, name="w_code", align_bytes=ALIGN)
         w_scale = keep.tile([P, E * PASSES * N], U8, name="w_scale", align_bytes=ALIGN)
         window = [keep.tile([P, T], F32, name=f"window{h}", align_bytes=ALIGN) for h in range(HALVES)]
         total = [keep.tile([P, T], F32, name=f"total{h}", align_bytes=ALIGN) for h in range(HALVES)]
-        residuals = keep.tile([P, HALVES, T], F32, name="residuals", align_bytes=ALIGN)
-        residual = [residuals[:, h, :] for h in range(HALVES)]
-        bias = keep.tile([P, HALVES, 8], F32, name="bias")
+        residual = keep.tile([P, HALVES, T], F32, name="residual", align_bytes=ALIGN)
+        bias = keep.tile([P, HALVES, BIAS_ROW], F32, name="bias")
         first_gates = keep.tile([P, W], F32, name="first_gates", align_bytes=ALIGN)
         later_gates = keep.tile([P, S - W], F32, name="later_gates", align_bytes=ALIGN)
         gates = [first_gates[:], later_gates[:, 0:W], later_gates[:, W : 2 * W]]
 
         nc.gpsimd.memset(w_scale[:].bitcast(I32), 0)
         for h in range(HALVES):
-            nc.vector.memset(window[h][:, 0:T], 0.0)
+            nc.vector.memset(window[h][:], 0.0)
 
-        def on_scalar(dst, src):
+        def round_on_scalar(dst, src):
             nc.scalar.activation(dst, src, IDENTITY)
 
-        raws = {}
-        for n, (a, u) in enumerate(planes):
-            rows = xT[a * K_PASS : (a + 1) * K_PASS, :].rearrange("(p j) w -> p j w", j=4)[:, 2 * u : 2 * u + 2, :]
-            cut, share = LOAD_CUT[n], SCALAR_CUT[n]
-            if n < 2:
-                run = rows.rearrange("p e w -> p (e w)")
-                raw = keep.tile([P, 2 * T], F32, name=f"raw{a}{u}", align_bytes=ALIGN)
-                nc.sync.dma_start(raw[:, 0 : T + cut], run[:, 0 : T + cut])
-                if n == 0:
-                    nc.sync.dma_start(offsets[:], offs)
-                else:
-                    nc.sync.dma_start(raw[:, T + cut :], run[:, T + cut :])
-                both = raw[:].rearrange("p (e w) -> p e w", e=2)
-                raws[a, u] = [
-                    (on_scalar, 0, share, both[:, :, 0:share]),
-                    (nc.vector.tensor_copy, share, T, both[:, :, share:T]),
-                ]
+        shares = {}
+
+        def plane_rows(a, u):
+            rows = xT[a * K_PASS : (a + 1) * K_PASS, :].rearrange("(p d) t -> p d t", d=4)
+            return rows[:, 2 * u : 2 * u + 2, :]
+
+        for u in range(2):
+            cut, share = FIRST_LOAD[u], SCALAR_TOKENS[u]
+            run = plane_rows(0, u).rearrange("p e t -> p (e t)")
+            raw = keep.tile([P, 2 * T], F32, name=f"raw0{u}", align_bytes=ALIGN)
+            nc.sync.dma_start(raw[:, 0 : T + cut], run[:, 0 : T + cut])
+            if u == 0:
+                nc.sync.dma_start(offsets[:], offs)
             else:
-                early = keep.tile([P, 2, cut], F32, name=f"early{a}{u}", align_bytes=ALIGN)
-                nc.sync.dma_start(early[:], rows[:, :, 0:cut])
-                late = keep.tile([P, 2, T - cut], F32, name=f"late{a}{u}", align_bytes=ALIGN)
-                nc.sync.dma_start(late[:], rows[:, :, cut:T])
-                raws[a, u] = [(on_scalar, 0, cut, early[:])]
-                if share > cut:
-                    raws[a, u].append((on_scalar, cut, share, late[:, :, 0 : share - cut]))
-                raws[a, u].append((nc.vector.tensor_copy, share, T, late[:, :, share - cut :]))
+                nc.sync.dma_start(raw[:, T + cut :], run[:, T + cut :])
+            both = raw[:].rearrange("p (e t) -> p e t", e=2)
+            shares[0, u] = [
+                (round_on_scalar, 0, share, both[:, :, 0:share]),
+                (nc.vector.tensor_copy, share, T, both[:, :, share:T]),
+            ]
+
+        for u in range(2):
+            cut, share = FIRST_LOAD[2 + u], SCALAR_TOKENS[2 + u]
+            early = keep.tile([P, 2, cut], F32, name=f"early1{u}", align_bytes=ALIGN)
+            nc.sync.dma_start(early[:], plane_rows(1, u)[:, :, 0:cut])
+            late = keep.tile([P, 2, T - cut], F32, name=f"late1{u}", align_bytes=ALIGN)
+            nc.sync.dma_start(late[:], plane_rows(1, u)[:, :, cut:T])
+            shares[1, u] = [(round_on_scalar, 0, cut, early[:])]
+            if share > cut:
+                shares[1, u].append((round_on_scalar, cut, share, late[:, :, 0 : share - cut]))
+            shares[1, u].append((nc.vector.tensor_copy, share, T, late[:, :, share - cut :]))
 
         code_rows = w_words.rearrange("e a p n -> p (e a) n")
 
         def load_codes(i0, i1):
-            g = slice(i0 * PIECE * PASSES, i1 * PIECE * PASSES)
-            nc.sync.dma_start(w_code[:, g, :], code_rows[:, g, :])
+            groups = slice(i0 * PIECE * PASSES, i1 * PIECE * PASSES)
+            nc.sync.dma_start(w_code[:, groups, :], code_rows[:, groups, :])
 
         nc.sync.dma_start(bias[:, :, 0:E], b.rearrange("(h p) e -> p h e", p=P))
         load_codes(0, 1)
@@ -99,36 +102,40 @@ def tile_moe_res_lin_bias_kernel(tc, xT, xr, w_words, w_scales, b, gate, offs, o
         scale_rows = w_scales.bitcast(I32).rearrange("e a (q r) n -> r q (e a) n", r=4)
         for r in range(4):
             nc.sync.dma_start(w_scale_words[r:P:32], scale_rows[r])
-        nc.sync.dma_start(gates[0], gate[0:P, 0:W])
+        nc.sync.dma_start(first_gates[:], gate[0:P, 0:W])
         load_codes(1, PIECES)
         nc.sync.dma_start(later_gates[:], gate[0:P, W:S])
-        nc.sync.dma_start(residuals[:], xr.rearrange("(h p) t -> p h t", p=P))
+        nc.sync.dma_start(residual[:], xr.rearrange("(h p) t -> p h t", p=P))
 
         pairs = {}
 
         def round_plane(a, u):
             pairs[a, u] = keep.tile([P, T], U32, name=f"pairs{a}{u}", align_bytes=ALIGN)
-            for copy, t0, t1, raw in raws[a, u]:
-                dst = pairs[a, u][:, t0:t1].bitcast(BF16).rearrange("p (w e) -> p w e", e=2)
-                copy(dst, raw.rearrange("p e w -> p w e"))
+            for copy, t0, t1, src in shares[a, u]:
+                dst = pairs[a, u][:, t0:t1].bitcast(BF16).rearrange("p (t e) -> p t e", e=2)
+                copy(dst, src.rearrange("p e t -> p t e"))
 
-        def gather(dst, a, u, i0, i1):
-            nc.vector.tensor_copy(dst, pairs[a, u][:].indirect(offsets[:, i0 * W // 16 : i1 * W // 16]))
+        gathered = [keep.tile([P, 2, S], U32, name=f"gathered{a}") for a in range(PASSES)]
+
+        def gather(a, u, i0, i1):
+            listed = pairs[a, u][:].indirect(offsets[:, i0 * W // 16 : i1 * W // 16])
+            nc.vector.tensor_copy(gathered[a][:, u, i0 * W : i1 * W], listed)
+
+        def weave(a, i0, i1, behind=""):
+            woven = keep.tile([P, (i1 - i0) * W, 2], U32, name=f"woven{a}{i0}", tag=behind, align_bytes=ALIGN)
+            nc.scalar.copy(woven[:], gathered[a][:, :, i0 * W : i1 * W].rearrange("p u s -> p s u"))
+            return woven[:]
 
         codes, scales = {}, {}
 
-        def quantise(a, i0, i1, woven, tag=""):
-            n = (i1 - i0) * W
-            code = keep.tile([P, n], U32, name=f"codes{a}{i0}", tag=tag, align_bytes=ALIGN)[:]
-            scale = keep.tile([P, n], U8, name=f"scales{a}{i0}", align_bytes=ALIGN)
+        def quantise(a, i, woven, behind=""):
+            codes[a, i] = keep.tile([P, W], U32, name=f"codes{a}{i}", tag=behind, align_bytes=ALIGN)
+            scales[a, i] = keep.tile([P, W], U8, name=f"scales{a}{i}", align_bytes=ALIGN)
             nc.vector.quantize_mx(
-                out=code.bitcast(FP8X4),
-                scales=scale[:],
+                out=codes[a, i][:].bitcast(FP8X4),
+                scales=scales[a, i][:],
                 in_=woven.rearrange("p s u -> p (s u)").bitcast(BF16),
             )
-            for i in range(i0, i1):
-                codes[a, i] = code[:, (i - i0) * W : (i - i0 + 1) * W]
-                scales[a, i] = scale[:, (i - i0) * W : (i - i0 + 1) * W]
 
         sums = [[None] * E for h in range(HALVES)]
         for h in range(HALVES):
@@ -141,17 +148,17 @@ def tile_moe_res_lin_bias_kernel(tc, xT, xr, w_words, w_scales, b, gate, offs, o
                     for j in range(PIECE):
                         sums[h][i * PIECE + j] = bank[:, j * C : (j + 1) * C]
 
-        def one_pass(h, e, a, first):
+        def one_pass(h, e, a, opening_pass):
             i, j = divmod(e, PIECE)
-            g = e * PASSES + a
+            group = e * PASSES + a
             nc.tensor.matmul_mx(
                 out=sums[h][e],
-                lhsT=w_code[:, g, 2 * P * h : 2 * P * (h + 1)].bitcast(FP4X4),
-                lhsT_scale=w_scale[:, g * N + h * P : g * N + (h + 1) * P],
+                lhsT=w_code[:, group, 2 * P * h : 2 * P * (h + 1)].bitcast(FP4X4),
+                lhsT_scale=w_scale[:, group * N + h * P : group * N + (h + 1) * P],
                 rhs=codes[a, i][:, j * C : (j + 1) * C].bitcast(FP8X4),
                 rhs_scale=scales[a, i][:, j * C : (j + 1) * C],
-                start=(a == first),
-                stop=(a != first),
+                start=(a == opening_pass),
+                stop=(a != opening_pass),
             )
 
         def multiply(h, i):
@@ -159,70 +166,61 @@ def tile_moe_res_lin_bias_kernel(tc, xT, xr, w_words, w_scales, b, gate, offs, o
                 for a in reversed(range(PASSES)):
                     one_pass(h, e, a, PASSES - 1)
 
-        def add_bias(h, i):
-            result = keep.tile([P, W], F32, name=f"result{h}{i}", align_bytes=ALIGN)
+        def bias_and_gate(h, i, scaled):
+            biased = keep.tile([P, W], F32, name=f"biased{h}{i}", align_bytes=ALIGN)
             for j in range(PIECE):
                 e = i * PIECE + j
-                nc.scalar.activation(result[:, j * C : (j + 1) * C], sums[h][e], IDENTITY, bias=bias[:, h, e : e + 1])
-            return result[:]
-
-        def times_gate(scaled, result, i):
-            nc.gpsimd.tensor_tensor(scaled, result, gates[i], MULT)
+                nc.scalar.activation(biased[:, j * C : (j + 1) * C], sums[h][e], IDENTITY, bias=bias[:, h, e : e + 1])
+            nc.gpsimd.tensor_tensor(scaled, biased[:], gates[i], MULT)
 
         def scatter(h, s0, s1, scaled):
-            part = slice(s0 // 16, s1 // 16)
-            nc.vector.tensor_copy(window[h][:].indirect(offsets[:, part]), scaled)
+            nc.vector.tensor_copy(window[h][:].indirect(offsets[:, s0 // 16 : s1 // 16]), scaled)
 
-        def finish(engine, queue, h, cuts):
-            for t0, t1 in cuts:
-                engine.tensor_tensor(total[h][:, t0:t1], window[h][:, t0:t1], residual[h][:, t0:t1], ADD)
-                queue.dma_start(out[h * P : (h + 1) * P, t0:t1], total[h][:, t0:t1])
+        def add_residual_and_store(engine, queue, h, parts):
+            for t0 in range(0, T, T // parts):
+                tokens = slice(t0, t0 + T // parts)
+                engine.tensor_tensor(total[h][:, tokens], window[h][:, tokens], residual[:, h, tokens], ADD)
+                queue.dma_start(out[h * P : (h + 1) * P, tokens], total[h][:, tokens])
 
-        def weave(plain, i0, i1, name, tag=""):
-            woven = keep.tile([P, (i1 - i0) * W, 2], U32, name=name, tag=tag, align_bytes=ALIGN)
-            nc.scalar.copy(woven[:], plain[:, :, i0 * W : i1 * W].rearrange("p u s -> p s u"))
-            return woven[:]
-
-        plain = [keep.tile([P, 2, S], U32, name=f"plain{a}") for a in range(PASSES)]
         for u in range(2):
             round_plane(0, u)
-            gather(plain[0][:, u, :], 0, u, 0, PIECES)
+            gather(0, u, 0, PIECES)
         round_plane(1, 0)
-        woven = weave(plain[0], 0, 2, "woven00", "early10")
-        gather(plain[1][:, 0, :], 1, 0, 0, PIECES)
-        quantise(0, 0, 1, woven[:, 0:W, :])
+        woven_first = weave(0, 0, 2, "early10")
+        gather(1, 0, 0, PIECES)
+        quantise(0, 0, woven_first[:, 0:W, :])
         for e in range(PIECE):
             one_pass(0, e, 0, 0)
         round_plane(1, 1)
-        quantise(0, 1, 2, woven[:, W : 2 * W, :], "early11")
-        woven02 = weave(plain[0], 2, 3, "woven02", "late11")
+        quantise(0, 1, woven_first[:, W : 2 * W, :], "early11")
+        woven_last = weave(0, 2, 3, "late11")
         woven1 = []
         for i in range(PIECES):
-            gather(plain[1][:, 1, i * W : (i + 1) * W], 1, 1, i, i + 1)
-            woven1.append(weave(plain[1], i, i + 1, f"woven1{i}"))
-        quantise(1, 0, 1, woven1[0])
-        quantise(1, 1, 2, woven1[1])
-        quantise(0, 2, 3, woven02, "woven10")
-        scaled00 = keep.tile([P, W], F32, name="scaled00")
+            gather(1, 1, i, i + 1)
+            woven1.append(weave(1, i, i + 1))
+        quantise(1, 0, woven1[0])
+        quantise(1, 1, woven1[1])
+        quantise(0, 2, woven_last, "woven10")
+        scaled_first = keep.tile([P, W], F32, name="scaled_first")
         for e in range(PIECE):
             one_pass(0, e, 1, 0)
             slots = slice(e * C, (e + 1) * C)
             nc.vector.scalar_tensor_tensor(
-                scaled00[:, slots], sums[0][e], bias[:, 0, e : e + 1], gates[0][:, slots], ADD, MULT
+                scaled_first[:, slots], sums[0][e], bias[:, 0, e : e + 1], gates[0][:, slots], ADD, MULT
             )
         multiply(1, 0)
-        quantise(1, 2, 3, woven1[2], "codes10")
+        quantise(1, 2, woven1[2], "codes10")
         scaled1 = keep.tile([P, S], F32, name="scaled1")
-        times_gate(scaled1[:, 0:W], add_bias(1, 0), 0)
-        scatter(0, 0, W, scaled00[:])
-        scatter(1, 0, SECOND, scaled1[:, 0:SECOND])
-        later0 = keep.tile([P, S - W], F32, name="later0")
-        later = [later0[:], scaled1[:, W:S]]
+        bias_and_gate(1, 0, scaled1[:, 0:W])
+        scatter(0, 0, W, scaled_first[:])
+        scatter(1, 0, SECOND_SCATTER, scaled1[:, 0:SECOND_SCATTER])
+        scaled_later = keep.tile([P, S - W], F32, name="scaled_later")
+        later = [scaled_later[:], scaled1[:, W:S]]
         for h in range(HALVES):
             for i in range(1, PIECES):
                 multiply(h, i)
-                times_gate(later[h][:, (i - 1) * W : i * W], add_bias(h, i), i)
+                bias_and_gate(h, i, later[h][:, (i - 1) * W : i * W])
         scatter(0, W, S, later[0])
-        finish(nc.gpsimd, nc.sync, 0, ((0, 640), (640, T)))
-        scatter(1, SECOND, S, scaled1[:, SECOND:S])
-        finish(nc.vector, nc.scalar, 1, ((0, 320), (320, 640), (640, 960), (960, T)))
+        add_residual_and_store(nc.gpsimd, nc.sync, 0, GPSIMD_SUMS)
+        scatter(1, SECOND_SCATTER, S, scaled1[:, SECOND_SCATTER:S])
+        add_residual_and_store(nc.vector, nc.scalar, 1, VECTOR_SUMS)

@@ -121,28 +121,35 @@ def tile_moe_res_lin_bias_kernel(tc, xT, xr, w_words, w_scales, b, gate, offs, o
             listed = pairs[a, u][:].indirect(offsets[:, i0 * W // 16 : i1 * W // 16])
             nc.vector.tensor_copy(gathered[a][:, u, i0 * W : i1 * W], listed)
 
+        def weave_into(woven, a, i0, i1):
+            nc.scalar.copy(woven, gathered[a][:, :, i0 * W : i1 * W].rearrange("p u s -> p s u"))
+            return woven
+
         def weave(a, i0, i1, behind=""):
             woven = keep.tile([P, (i1 - i0) * W, 2], U32, name=f"woven{a}{i0}", tag=behind, align_bytes=ALIGN)
-            nc.scalar.copy(woven[:], gathered[a][:, :, i0 * W : i1 * W].rearrange("p u s -> p s u"))
-            return woven[:]
+            return weave_into(woven[:], a, i0, i1)
 
         codes, scales = {}, {}
 
-        def quantise(a, i, woven, behind=""):
-            codes[a, i] = keep.tile([P, W], U32, name=f"codes{a}{i}", tag=behind, align_bytes=ALIGN)
-            scales[a, i] = keep.tile([P, W], U8, name=f"scales{a}{i}", align_bytes=ALIGN)
+        def quantise(parts, woven, behind=""):
+            a, i = parts[0]
+            code = keep.tile([P, len(parts) * W], U32, name=f"codes{a}{i}", tag=behind, align_bytes=ALIGN)
+            scale = keep.tile([P, len(parts) * W], U8, name=f"scales{a}{i}", align_bytes=ALIGN)
             nc.vector.quantize_mx(
-                out=codes[a, i][:].bitcast(FP8X4),
-                scales=scales[a, i][:],
+                out=code[:].bitcast(FP8X4),
+                scales=scale[:],
                 in_=woven.rearrange("p s u -> p (s u)").bitcast(BF16),
             )
+            for n, part in enumerate(parts):
+                codes[part] = code[:, n * W : (n + 1) * W]
+                scales[part] = scale[:, n * W : (n + 1) * W]
 
         sums = [[None] * E for h in range(HALVES)]
         for h in range(HALVES):
             for i in range(PIECES):
-                if (h, i) == (0, 0):
+                if i == 0:
                     for e in range(PIECE):
-                        sums[h][e] = psum.tile([P, C], F32, name=f"lone{e}")[:]
+                        sums[h][e] = psum.tile([P, C], F32, name=f"lone{h}_{e}")[:]
                 else:
                     bank = psum.tile([P, W], F32, name=f"bank{h}_{i}")
                     for j in range(PIECE):
@@ -188,19 +195,22 @@ def tile_moe_res_lin_bias_kernel(tc, xT, xr, w_words, w_scales, b, gate, offs, o
         round_plane(1, 0)
         woven_first = weave(0, 0, 2, "early10")
         gather(1, 0, 0, PIECES)
-        quantise(0, 0, woven_first[:, 0:W, :])
-        for e in range(PIECE):
-            one_pass(0, e, 0, 0)
+        quantise([(0, 0)], woven_first[:, 0:W, :])
+        for h in range(HALVES):
+            for e in range(PIECE):
+                one_pass(h, e, 0, 0)
         round_plane(1, 1)
-        quantise(0, 1, woven_first[:, W : 2 * W, :], "early11")
-        woven_last = weave(0, 2, 3, "late11")
-        woven1 = []
-        for i in range(PIECES):
-            gather(1, 1, i, i + 1)
-            woven1.append(weave(1, i, i + 1))
-        quantise(1, 0, woven1[0])
-        quantise(1, 1, woven1[1])
-        quantise(0, 2, woven_last, "woven10")
+        quantise([(0, 1)], woven_first[:, W : 2 * W, :], "early11")
+        woven_two = keep.tile([P, 2 * W, 2], U32, name="woven_two", tag="late11", align_bytes=ALIGN)
+        weave_into(woven_two[:, 0:W, :], 0, 2, 3)
+        gather(1, 1, 0, 1)
+        woven10 = weave(1, 0, 1)
+        gather(1, 1, 1, 2)
+        weave_into(woven_two[:, W : 2 * W, :], 1, 1, 2)
+        gather(1, 1, 2, 3)
+        woven12 = weave(1, 2, 3)
+        quantise([(1, 0)], woven10)
+        quantise([(0, 2), (1, 1)], woven_two[:])
         scaled_first = keep.tile([P, W], F32, name="scaled_first")
         for e in range(PIECE):
             one_pass(0, e, 1, 0)
@@ -208,8 +218,9 @@ def tile_moe_res_lin_bias_kernel(tc, xT, xr, w_words, w_scales, b, gate, offs, o
             nc.vector.scalar_tensor_tensor(
                 scaled_first[:, slots], sums[0][e], bias[:, 0, e : e + 1], gates[0][:, slots], ADD, MULT
             )
-        multiply(1, 0)
-        quantise(1, 2, woven1[2], "codes10")
+        for e in range(PIECE):
+            one_pass(1, e, 1, 0)
+        quantise([(1, 2)], woven12, "codes10")
         scaled1 = keep.tile([P, S], F32, name="scaled1")
         bias_and_gate(1, 0, scaled1[:, 0:W])
         scatter(0, 0, W, scaled_first[:])

@@ -28,8 +28,8 @@ IDENTITY = mybir.ActivationFunctionType.Identity
 
 ALIGN = 256
 BIAS_ROW = 8
-FIRST_LOAD = (T, 704, 640, 672)
-SCALAR_TOKENS = (512, 704, 640, 928)
+FIRST_LOAD = (T, 704, 704, 672)
+SCALAR_TOKENS = (512, 704, 704, 928)
 SECOND_SCATTER = 224
 GPSIMD_SUMS, VECTOR_SUMS = 2, 4
 
@@ -64,22 +64,23 @@ def tile_moe_res_lin_bias_kernel(tc, xT, xr, w_words, w_scales, b, gate, offs, o
             rows = xT[a * K_PASS : (a + 1) * K_PASS, :].rearrange("(p d) t -> p d t", d=4)
             return rows[:, 2 * u : 2 * u + 2, :]
 
-        for u in range(2):
-            cut, share = FIRST_LOAD[u], SCALAR_TOKENS[u]
-            run = plane_rows(0, u).rearrange("p e t -> p (e t)")
-            raw = keep.tile([P, 2 * T], F32, name=f"raw0{u}", align_bytes=ALIGN)
+        for n in range(3):
+            a, u = divmod(n, 2)
+            cut, share = FIRST_LOAD[n], SCALAR_TOKENS[n]
+            run = plane_rows(a, u).rearrange("p e t -> p (e t)")
+            raw = keep.tile([P, 2 * T], F32, name=f"raw{a}{u}", align_bytes=ALIGN)
             nc.sync.dma_start(raw[:, 0 : T + cut], run[:, 0 : T + cut])
-            if u == 0:
+            if n == 0:
                 nc.sync.dma_start(offsets[:], offs)
             else:
                 nc.sync.dma_start(raw[:, T + cut :], run[:, T + cut :])
             both = raw[:].rearrange("p (e t) -> p e t", e=2)
-            shares[0, u] = [
+            shares[a, u] = [
                 (round_on_scalar, 0, share, both[:, :, 0:share]),
                 (nc.vector.tensor_copy, share, T, both[:, :, share:T]),
             ]
 
-        for u in range(2):
+        for u in range(1, 2):
             cut, share = FIRST_LOAD[2 + u], SCALAR_TOKENS[2 + u]
             early = keep.tile([P, 2, cut], F32, name=f"early1{u}", align_bytes=ALIGN)
             nc.sync.dma_start(early[:], plane_rows(1, u)[:, :, 0:cut])
@@ -189,18 +190,21 @@ def tile_moe_res_lin_bias_kernel(tc, xT, xr, w_words, w_scales, b, gate, offs, o
                 engine.tensor_tensor(total[h][:, tokens], window[h][:, tokens], residual[:, h, tokens], ADD)
                 queue.dma_start(out[h * P : (h + 1) * P, tokens], total[h][:, tokens])
 
-        for u in range(2):
-            round_plane(0, u)
-            gather(0, u, 0, PIECES)
+        round_plane(0, 0)
+        gather(0, 0, 0, PIECES)
+        round_plane(0, 1)
+        gather(0, 1, 0, 1)
+        woven00 = weave(0, 0, 1)
+        gather(0, 1, 1, PIECES)
+        quantise([(0, 0)], woven00)
         round_plane(1, 0)
-        woven_first = weave(0, 0, 2, "early10")
+        woven01 = weave(0, 1, 2, "raw10")
         gather(1, 0, 0, PIECES)
-        quantise([(0, 0)], woven_first[:, 0:W, :])
         for h in range(HALVES):
             for e in range(PIECE):
                 one_pass(h, e, 0, 0)
         round_plane(1, 1)
-        quantise([(0, 1)], woven_first[:, W : 2 * W, :], "early11")
+        quantise([(0, 1)], woven01, "early11")
         woven_two = keep.tile([P, 2 * W, 2], U32, name="woven_two", tag="late11", align_bytes=ALIGN)
         weave_into(woven_two[:, 0:W, :], 0, 2, 3)
         gather(1, 1, 0, 1)

@@ -28,8 +28,9 @@ IDENTITY = mybir.ActivationFunctionType.Identity
 
 ALIGN = 256
 BIAS_ROW = 8
-FIRST_LOAD = (T, 704, 704, 672)
-SCALAR_TOKENS = (512, 704, 704, 928)
+FIRST_LOAD = (T, 704, 704, 832)
+SCALAR_TOKENS = (512, 864, 832, 1008)
+GPSIMD_TOKENS = (0, 256, 256, 352)
 SECOND_SCATTER = 224
 GPSIMD_SUMS, VECTOR_SUMS = 2, 4
 
@@ -58,6 +59,9 @@ def tile_moe_res_lin_bias_kernel(tc, xT, xr, w_words, w_scales, b, gate, offs, o
         def round_on_scalar(dst, src):
             nc.scalar.activation(dst, src, IDENTITY)
 
+        def round_on_gpsimd(dst, src):
+            nc.gpsimd.tensor_scalar(dst, src, 1.0, 0.0, MULT, ADD)
+
         shares = {}
 
         def plane_rows(a, u):
@@ -75,10 +79,10 @@ def tile_moe_res_lin_bias_kernel(tc, xT, xr, w_words, w_scales, b, gate, offs, o
             else:
                 nc.sync.dma_start(raw[:, T + cut :], run[:, T + cut :])
             both = raw[:].rearrange("p (e t) -> p e t", e=2)
-            shares[a, u] = [
-                (round_on_scalar, 0, share, both[:, :, 0:share]),
-                (nc.vector.tensor_copy, share, T, both[:, :, share:T]),
-            ]
+            head = GPSIMD_TOKENS[n]
+            ends = [(round_on_gpsimd, head), (round_on_scalar, min(cut, share)), (round_on_scalar, share), (nc.vector.tensor_copy, T)]
+            starts = [0] + [end for copy, end in ends[:-1]]
+            shares[a, u] = [(copy, t0, t1, both[:, :, t0:t1]) for t0, (copy, t1) in zip(starts, ends) if t1 > t0]
 
         for u in range(1, 2):
             cut, share = FIRST_LOAD[2 + u], SCALAR_TOKENS[2 + u]
@@ -86,7 +90,8 @@ def tile_moe_res_lin_bias_kernel(tc, xT, xr, w_words, w_scales, b, gate, offs, o
             nc.sync.dma_start(early[:], plane_rows(1, u)[:, :, 0:cut])
             late = keep.tile([P, 2, T - cut], F32, name=f"late1{u}", align_bytes=ALIGN)
             nc.sync.dma_start(late[:], plane_rows(1, u)[:, :, cut:T])
-            shares[1, u] = [(round_on_scalar, 0, cut, early[:])]
+            head = GPSIMD_TOKENS[2 + u]
+            shares[1, u] = [(round_on_gpsimd, 0, head, early[:, :, 0:head]), (round_on_scalar, head, cut, early[:, :, head:cut])]
             if share > cut:
                 shares[1, u].append((round_on_scalar, cut, share, late[:, :, 0 : share - cut]))
             shares[1, u].append((nc.vector.tensor_copy, share, T, late[:, :, share - cut :]))
@@ -193,18 +198,16 @@ def tile_moe_res_lin_bias_kernel(tc, xT, xr, w_words, w_scales, b, gate, offs, o
         round_plane(0, 0)
         gather(0, 0, 0, PIECES)
         round_plane(0, 1)
-        gather(0, 1, 0, 1)
-        woven00 = weave(0, 0, 1)
-        gather(0, 1, 1, PIECES)
-        quantise([(0, 0)], woven00)
+        gather(0, 1, 0, PIECES)
         round_plane(1, 0)
-        woven01 = weave(0, 1, 2, "raw10")
+        woven_first = weave(0, 0, 2, "raw10")
         gather(1, 0, 0, PIECES)
+        quantise([(0, 0)], woven_first[:, 0:W, :])
         for h in range(HALVES):
             for e in range(PIECE):
                 one_pass(h, e, 0, 0)
         round_plane(1, 1)
-        quantise([(0, 1)], woven01, "early11")
+        quantise([(0, 1)], woven_first[:, W : 2 * W, :], "early11")
         woven_two = keep.tile([P, 2 * W, 2], U32, name="woven_two", tag="late11", align_bytes=ALIGN)
         weave_into(woven_two[:, 0:W, :], 0, 2, 3)
         gather(1, 1, 0, 1)

@@ -28,9 +28,9 @@ IDENTITY = mybir.ActivationFunctionType.Identity
 
 ALIGN = 256
 BIAS_ROW = 8
-FIRST_LOAD = (T, 704, 704, 832)
-SCALAR_TOKENS = (512, 864, 832, 1008)
-GPSIMD_TOKENS = (0, 256, 256, 352)
+FIRST_LOAD = (T, 640, 640, 832)
+SCALAR_TOKENS = (448, 960, 848, 1008)
+GPSIMD_TOKENS = (0, 320, 288, 352)
 SECOND_SCATTER = 224
 GPSIMD_SUMS, VECTOR_SUMS = 2, 4
 

@@ -11,6 +11,7 @@ HALVES = N // P
 PIECE = 2
 PIECES = E // PIECE
 W = PIECE * C
+PLANES = [(a, u) for a in range(PASSES) for u in range(2)]
 
 FLOPS = 2 * S * K * N
 BYTES = 4 * K * T + 8 * N * T + E * K * N // 2 + E * K * N // 32 + 4 * N * E + 4 * S + 2 * P * S // 16
@@ -29,8 +30,8 @@ IDENTITY = mybir.ActivationFunctionType.Identity
 ALIGN = 256
 BIAS_ROW = 8
 FIRST_LOAD = (T, 640, 640, 832)
-SCALAR_TOKENS = (448, 960, 848, 1008)
-GPSIMD_TOKENS = (0, 320, 288, 352)
+SCALAR_TOKENS = (448, 960, 864, 1008)
+GPSIMD_TOKENS = (0, 352, 320, 384)
 SECOND_SCATTER = 224
 GPSIMD_SUMS, VECTOR_SUMS = 2, 4
 
@@ -68,8 +69,7 @@ def tile_moe_res_lin_bias_kernel(tc, xT, xr, w_words, w_scales, b, gate, offs, o
             rows = xT[a * K_PASS : (a + 1) * K_PASS, :].rearrange("(p d) t -> p d t", d=4)
             return rows[:, 2 * u : 2 * u + 2, :]
 
-        for n in range(3):
-            a, u = divmod(n, 2)
+        for n, (a, u) in enumerate(PLANES[:-1]):
             cut, share = FIRST_LOAD[n], SCALAR_TOKENS[n]
             run = plane_rows(a, u).rearrange("p e t -> p (e t)")
             raw = keep.tile([P, 2 * T], F32, name=f"raw{a}{u}", align_bytes=ALIGN)
@@ -79,22 +79,24 @@ def tile_moe_res_lin_bias_kernel(tc, xT, xr, w_words, w_scales, b, gate, offs, o
             else:
                 nc.sync.dma_start(raw[:, T + cut :], run[:, T + cut :])
             both = raw[:].rearrange("p (e t) -> p e t", e=2)
-            head = GPSIMD_TOKENS[n]
-            ends = [(round_on_gpsimd, head), (round_on_scalar, min(cut, share)), (round_on_scalar, share), (nc.vector.tensor_copy, T)]
-            starts = [0] + [end for copy, end in ends[:-1]]
-            shares[a, u] = [(copy, t0, t1, both[:, :, t0:t1]) for t0, (copy, t1) in zip(starts, ends) if t1 > t0]
+            marks = (0, GPSIMD_TOKENS[n], min(cut, share), share, T)
+            copies = (round_on_gpsimd, round_on_scalar, round_on_scalar, nc.vector.tensor_copy)
+            shares[a, u] = [
+                (copy, t0, t1, both[:, :, t0:t1]) for copy, t0, t1 in zip(copies, marks, marks[1:]) if t1 > t0
+            ]
 
-        for u in range(1, 2):
-            cut, share = FIRST_LOAD[2 + u], SCALAR_TOKENS[2 + u]
-            early = keep.tile([P, 2, cut], F32, name=f"early1{u}", align_bytes=ALIGN)
-            nc.sync.dma_start(early[:], plane_rows(1, u)[:, :, 0:cut])
-            late = keep.tile([P, 2, T - cut], F32, name=f"late1{u}", align_bytes=ALIGN)
-            nc.sync.dma_start(late[:], plane_rows(1, u)[:, :, cut:T])
-            head = GPSIMD_TOKENS[2 + u]
-            shares[1, u] = [(round_on_gpsimd, 0, head, early[:, :, 0:head]), (round_on_scalar, head, cut, early[:, :, head:cut])]
-            if share > cut:
-                shares[1, u].append((round_on_scalar, cut, share, late[:, :, 0 : share - cut]))
-            shares[1, u].append((nc.vector.tensor_copy, share, T, late[:, :, share - cut :]))
+        a, u = PLANES[-1]
+        cut, share, head = FIRST_LOAD[-1], SCALAR_TOKENS[-1], GPSIMD_TOKENS[-1]
+        early = keep.tile([P, 2, cut], F32, name="early", align_bytes=ALIGN)
+        nc.sync.dma_start(early[:], plane_rows(a, u)[:, :, 0:cut])
+        late = keep.tile([P, 2, T - cut], F32, name="late", align_bytes=ALIGN)
+        nc.sync.dma_start(late[:], plane_rows(a, u)[:, :, cut:T])
+        shares[a, u] = [
+            (round_on_gpsimd, 0, head, early[:, :, 0:head]),
+            (round_on_scalar, head, cut, early[:, :, head:cut]),
+            (round_on_scalar, cut, share, late[:, :, 0 : share - cut]),
+            (nc.vector.tensor_copy, share, T, late[:, :, share - cut :]),
+        ]
 
         code_rows = w_words.rearrange("e a p n -> p (e a) n")
 
@@ -195,10 +197,9 @@ def tile_moe_res_lin_bias_kernel(tc, xT, xr, w_words, w_scales, b, gate, offs, o
                 engine.tensor_tensor(total[h][:, tokens], window[h][:, tokens], residual[:, h, tokens], ADD)
                 queue.dma_start(out[h * P : (h + 1) * P, tokens], total[h][:, tokens])
 
-        round_plane(0, 0)
-        gather(0, 0, 0, PIECES)
-        round_plane(0, 1)
-        gather(0, 1, 0, PIECES)
+        for u in range(2):
+            round_plane(0, u)
+            gather(0, u, 0, PIECES)
         round_plane(1, 0)
         woven_first = weave(0, 0, 2, "raw10")
         gather(1, 0, 0, PIECES)
@@ -207,8 +208,8 @@ def tile_moe_res_lin_bias_kernel(tc, xT, xr, w_words, w_scales, b, gate, offs, o
             for e in range(PIECE):
                 one_pass(h, e, 0, 0)
         round_plane(1, 1)
-        quantise([(0, 1)], woven_first[:, W : 2 * W, :], "early11")
-        woven_two = keep.tile([P, 2 * W, 2], U32, name="woven_two", tag="late11", align_bytes=ALIGN)
+        quantise([(0, 1)], woven_first[:, W : 2 * W, :], "early")
+        woven_two = keep.tile([P, 2 * W, 2], U32, name="woven_two", tag="late", align_bytes=ALIGN)
         weave_into(woven_two[:, 0:W, :], 0, 2, 3)
         gather(1, 1, 0, 1)
         woven10 = weave(1, 0, 1)

@@ -7,11 +7,11 @@ S = E * C
 P = 128
 K_PASS = 512
 PASSES = K // K_PASS
+PACK = 4
 HALVES = N // P
 PIECE = 2
 PIECES = E // PIECE
 W = PIECE * C
-PLANES = [(a, u) for a in range(PASSES) for u in range(2)]
 
 FLOPS = 2 * S * K * N
 BYTES = 4 * K * T + 8 * N * T + E * K * N // 2 + E * K * N // 32 + 4 * N * E + 4 * S + 2 * P * S // 16
@@ -26,14 +26,13 @@ FP8X4 = mybir.dt.float8_e4m3fn_x4
 FP4X4 = mybir.dt.float4_e2m1fn_x4
 ADD, MULT = mybir.AluOpType.add, mybir.AluOpType.mult
 IDENTITY = mybir.ActivationFunctionType.Identity
+COPY = mybir.ActivationFunctionType.Copy
 
 ALIGN = 256
 BIAS_ROW = 8
-FIRST_LOAD = (T, 640, 640, 832)
-SCALAR_TOKENS = (448, 960, 864, 1008)
-GPSIMD_TOKENS = (0, 352, 320, 384)
-SECOND_SCATTER = 224
-GPSIMD_SUMS, VECTOR_SUMS = 2, 4
+SUMS = (2, 4)
+VECTOR_PLAIN = 64
+SCATTERS = (3, 3)
 
 
 def tile_moe_res_lin_bias_kernel(tc, xT, xr, w_words, w_scales, b, gate, offs, out):
@@ -45,58 +44,27 @@ def tile_moe_res_lin_bias_kernel(tc, xT, xr, w_words, w_scales, b, gate, offs, o
         offsets = keep.tile([P, S // 16], U16, name="offsets")
         w_code = keep.tile([P, E * PASSES, 2 * N], U8, name="w_code", align_bytes=ALIGN)
         w_scale = keep.tile([P, E * PASSES * N], U8, name="w_scale", align_bytes=ALIGN)
-        window = [keep.tile([P, T], F32, name=f"window{h}", align_bytes=ALIGN) for h in range(HALVES)]
+        spare = (0, HALVES * BIAS_ROW)
+        window = [keep.tile([P, T + spare[h]], F32, name=f"window{h}", align_bytes=ALIGN) for h in range(HALVES)]
         total = [keep.tile([P, T], F32, name=f"total{h}", align_bytes=ALIGN) for h in range(HALVES)]
         residual = keep.tile([P, HALVES, T], F32, name="residual", align_bytes=ALIGN)
-        bias = keep.tile([P, HALVES, BIAS_ROW], F32, name="bias")
+        bias = window[1][:, T:].rearrange("p (h e) -> p h e", h=HALVES)
         first_gates = keep.tile([P, W], F32, name="first_gates", align_bytes=ALIGN)
         later_gates = keep.tile([P, S - W], F32, name="later_gates", align_bytes=ALIGN)
         gates = [first_gates[:], later_gates[:, 0:W], later_gates[:, W : 2 * W]]
 
         nc.gpsimd.memset(w_scale[:].bitcast(I32), 0)
-        for h in range(HALVES):
-            nc.vector.memset(window[h][:], 0.0)
+        nc.vector.memset(window[0][:], 0.0)
+        nc.scalar.activation(window[1][:, 0:T], window[0][:], IDENTITY)
 
-        def round_on_scalar(dst, src):
-            nc.scalar.activation(dst, src, IDENTITY)
-
-        def round_on_gpsimd(dst, src):
-            nc.gpsimd.tensor_scalar(dst, src, 1.0, 0.0, MULT, ADD)
-
-        shares = {}
-
-        def plane_rows(a, u):
-            rows = xT[a * K_PASS : (a + 1) * K_PASS, :].rearrange("(p d) t -> p d t", d=4)
-            return rows[:, 2 * u : 2 * u + 2, :]
-
-        for n, (a, u) in enumerate(PLANES[:-1]):
-            cut, share = FIRST_LOAD[n], SCALAR_TOKENS[n]
-            run = plane_rows(a, u).rearrange("p e t -> p (e t)")
-            raw = keep.tile([P, 2 * T], F32, name=f"raw{a}{u}", align_bytes=ALIGN)
-            nc.sync.dma_start(raw[:, 0 : T + cut], run[:, 0 : T + cut])
-            if n == 0:
-                nc.sync.dma_start(offsets[:], offs)
-            else:
-                nc.sync.dma_start(raw[:, T + cut :], run[:, T + cut :])
-            both = raw[:].rearrange("p (e t) -> p e t", e=2)
-            marks = (0, GPSIMD_TOKENS[n], min(cut, share), share, T)
-            copies = (round_on_gpsimd, round_on_scalar, round_on_scalar, nc.vector.tensor_copy)
-            shares[a, u] = [
-                (copy, t0, t1, both[:, :, t0:t1]) for copy, t0, t1 in zip(copies, marks, marks[1:]) if t1 > t0
-            ]
-
-        a, u = PLANES[-1]
-        cut, share, head = FIRST_LOAD[-1], SCALAR_TOKENS[-1], GPSIMD_TOKENS[-1]
-        early = keep.tile([P, 2, cut], F32, name="early", align_bytes=ALIGN)
-        nc.sync.dma_start(early[:], plane_rows(a, u)[:, :, 0:cut])
-        late = keep.tile([P, 2, T - cut], F32, name="late", align_bytes=ALIGN)
-        nc.sync.dma_start(late[:], plane_rows(a, u)[:, :, cut:T])
-        shares[a, u] = [
-            (round_on_gpsimd, 0, head, early[:, :, 0:head]),
-            (round_on_scalar, head, cut, early[:, :, head:cut]),
-            (round_on_scalar, cut, share, late[:, :, 0 : share - cut]),
-            (nc.vector.tensor_copy, share, T, late[:, :, share - cut :]),
-        ]
+        rows = {}
+        for a in range(PASSES):
+            by_row = xT[a * K_PASS : (a + 1) * K_PASS, :].rearrange("(p d) t -> d p t", d=PACK)
+            for d in range(PACK):
+                rows[a, d] = keep.tile([P, T], F32, name=f"row{a}{d}", align_bytes=ALIGN)
+                nc.sync.dma_start(rows[a, d][:], by_row[d])
+                if (a, d) == (0, 0):
+                    nc.sync.dma_start(offsets[:], offs)
 
         code_rows = w_words.rearrange("e a p n -> p (e a) n")
 
@@ -115,42 +83,36 @@ def tile_moe_res_lin_bias_kernel(tc, xT, xr, w_words, w_scales, b, gate, offs, o
         nc.sync.dma_start(later_gates[:], gate[0:P, W:S])
         nc.sync.dma_start(residual[:], xr.rearrange("(h p) t -> p h t", p=P))
 
-        pairs = {}
+        def listed(tile, s0, s1):
+            return tile[:].indirect(offsets[:, s0 // 16 : s1 // 16])
 
-        def round_plane(a, u):
-            pairs[a, u] = keep.tile([P, T], U32, name=f"pairs{a}{u}", align_bytes=ALIGN)
-            for copy, t0, t1, src in shares[a, u]:
-                dst = pairs[a, u][:, t0:t1].bitcast(BF16).rearrange("p (t e) -> p t e", e=2)
-                copy(dst, src.rearrange("p e t -> p t e"))
+        first = [keep.tile([P, W, PACK], BF16, name=f"first{a}", align_bytes=ALIGN) for a in range(PASSES)]
+        plain = [keep.tile([P, PACK, S - W], BF16, name=f"plain{a}", align_bytes=ALIGN) for a in range(PASSES)]
 
-        gathered = [keep.tile([P, 2, S], U32, name=f"gathered{a}") for a in range(PASSES)]
+        def gather_first(a, d):
+            nc.vector.tensor_copy(first[a][:, :, d], listed(rows[a, d], 0, W))
 
-        def gather(a, u, i0, i1):
-            listed = pairs[a, u][:].indirect(offsets[:, i0 * W // 16 : i1 * W // 16])
-            nc.vector.tensor_copy(gathered[a][:, u, i0 * W : i1 * W], listed)
+        def gather_plain(a, d, s0, s1):
+            nc.scalar.activation(plain[a][:, d, s0 - W : s1 - W], listed(rows[a, d], s0, s1), COPY)
 
-        def weave_into(woven, a, i0, i1):
-            nc.scalar.copy(woven, gathered[a][:, :, i0 * W : i1 * W].rearrange("p u s -> p s u"))
-            return woven
-
-        def weave(a, i0, i1, behind=""):
-            woven = keep.tile([P, (i1 - i0) * W, 2], U32, name=f"woven{a}{i0}", tag=behind, align_bytes=ALIGN)
-            return weave_into(woven[:], a, i0, i1)
+        def gather_row(a, d):
+            gather_first(a, d)
+            cut = W + VECTOR_PLAIN
+            nc.vector.tensor_copy(plain[a][:, d, 0:VECTOR_PLAIN], listed(rows[a, d], W, cut))
+            gather_plain(a, d, cut, S)
 
         codes, scales = {}, {}
 
-        def quantise(parts, woven, behind=""):
-            a, i = parts[0]
-            code = keep.tile([P, len(parts) * W], U32, name=f"codes{a}{i}", tag=behind, align_bytes=ALIGN)
-            scale = keep.tile([P, len(parts) * W], U8, name=f"scales{a}{i}", align_bytes=ALIGN)
-            nc.vector.quantize_mx(
-                out=code[:].bitcast(FP8X4),
-                scales=scale[:],
-                in_=woven.rearrange("p s u -> p (s u)").bitcast(BF16),
-            )
-            for n, part in enumerate(parts):
-                codes[part] = code[:, n * W : (n + 1) * W]
-                scales[part] = scale[:, n * W : (n + 1) * W]
+        def quantise(a, i0, i1, woven, behind=""):
+            code = keep.tile([P, (i1 - i0) * W], U32, name=f"codes{a}{i0}", tag=behind, align_bytes=ALIGN)
+            scale = keep.tile([P, (i1 - i0) * W], U8, name=f"scales{a}{i0}", align_bytes=ALIGN)
+            nc.vector.quantize_mx(out=code[:].bitcast(FP8X4), scales=scale[:], in_=woven.rearrange("p s d -> p (s d)"))
+            for i in range(i0, i1):
+                codes[a, i] = code[:, (i - i0) * W : (i - i0 + 1) * W]
+                scales[a, i] = scale[:, (i - i0) * W : (i - i0 + 1) * W]
+
+        def unwoven(a, i0, i1):
+            return plain[a][:, :, (i0 - 1) * W : (i1 - 1) * W].rearrange("p d s -> p s d")
 
         sums = [[None] * E for h in range(HALVES)]
         for h in range(HALVES):
@@ -181,65 +143,60 @@ def tile_moe_res_lin_bias_kernel(tc, xT, xr, w_words, w_scales, b, gate, offs, o
                 for a in reversed(range(PASSES)):
                     one_pass(h, e, a, PASSES - 1)
 
-        def bias_and_gate(h, i, scaled):
+        scaled = [keep.tile([P, S], F32, name=f"scaled{h}", align_bytes=ALIGN) for h in range(HALVES)]
+
+        def bias_and_gate(h, i):
             biased = keep.tile([P, W], F32, name=f"biased{h}{i}", align_bytes=ALIGN)
             for j in range(PIECE):
                 e = i * PIECE + j
                 nc.scalar.activation(biased[:, j * C : (j + 1) * C], sums[h][e], IDENTITY, bias=bias[:, h, e : e + 1])
-            nc.gpsimd.tensor_tensor(scaled, biased[:], gates[i], MULT)
+            nc.gpsimd.tensor_tensor(scaled[h][:, i * W : (i + 1) * W], biased[:], gates[i], MULT)
 
-        def scatter(h, s0, s1, scaled):
-            nc.vector.tensor_copy(window[h][:].indirect(offsets[:, s0 // 16 : s1 // 16]), scaled)
+        def scatter(h, s0, s1):
+            if h == 0:
+                nc.vector.tensor_copy(listed(window[h], s0, s1), scaled[h][:, s0:s1])
+            else:
+                nc.scalar.activation(listed(window[h], s0, s1), scaled[h][:, s0:s1], COPY)
 
-        def add_residual_and_store(engine, queue, h, parts):
-            for t0 in range(0, T, T // parts):
-                tokens = slice(t0, t0 + T // parts)
-                engine.tensor_tensor(total[h][:, tokens], window[h][:, tokens], residual[:, h, tokens], ADD)
-                queue.dma_start(out[h * P : (h + 1) * P, tokens], total[h][:, tokens])
-
-        for u in range(2):
-            round_plane(0, u)
-            gather(0, u, 0, PIECES)
-        round_plane(1, 0)
-        woven_first = weave(0, 0, 2, "raw10")
-        gather(1, 0, 0, PIECES)
-        quantise([(0, 0)], woven_first[:, 0:W, :])
+        for d in range(PACK):
+            gather_row(0, d)
+        quantise(0, 0, 1, first[0][:])
+        woven0 = keep.tile([P, S - W, PACK], BF16, name="woven0", tag="first0", align_bytes=ALIGN)
+        nc.gpsimd.tensor_scalar(woven0[:], unwoven(0, 1, 3), 1.0, 0.0, MULT, ADD)
+        for d in range(PACK - 1):
+            gather_row(1, d)
+        quantise(0, 1, 3, woven0[:], "row11")
         for h in range(HALVES):
             for e in range(PIECE):
                 one_pass(h, e, 0, 0)
-        round_plane(1, 1)
-        quantise([(0, 1)], woven_first[:, W : 2 * W, :], "early")
-        woven_two = keep.tile([P, 2 * W, 2], U32, name="woven_two", tag="late", align_bytes=ALIGN)
-        weave_into(woven_two[:, 0:W, :], 0, 2, 3)
-        gather(1, 1, 0, 1)
-        woven10 = weave(1, 0, 1)
-        gather(1, 1, 1, 2)
-        weave_into(woven_two[:, W : 2 * W, :], 1, 1, 2)
-        gather(1, 1, 2, 3)
-        woven12 = weave(1, 2, 3)
-        quantise([(1, 0)], woven10)
-        quantise([(0, 2), (1, 1)], woven_two[:])
-        scaled_first = keep.tile([P, W], F32, name="scaled_first")
+        gather_first(1, PACK - 1)
+        gather_plain(1, PACK - 1, W, 2 * W)
+        gather_plain(1, PACK - 1, 2 * W, S)
+        woven11 = keep.tile([P, W, PACK], BF16, name="woven11", align_bytes=ALIGN)
+        nc.vector.tensor_copy(woven11[:], unwoven(1, 1, 2))
+        woven12 = keep.tile([P, W, PACK], BF16, name="woven12", align_bytes=ALIGN)
+        nc.scalar.copy(woven12[:], unwoven(1, 2, 3))
+        quantise(1, 0, 1, first[1][:])
+        quantise(1, 1, 2, woven11[:])
         for e in range(PIECE):
             one_pass(0, e, 1, 0)
             slots = slice(e * C, (e + 1) * C)
             nc.vector.scalar_tensor_tensor(
-                scaled_first[:, slots], sums[0][e], bias[:, 0, e : e + 1], gates[0][:, slots], ADD, MULT
+                scaled[0][:, slots], sums[0][e], bias[:, 0, e : e + 1], gates[0][:, slots], ADD, MULT
             )
         for e in range(PIECE):
             one_pass(1, e, 1, 0)
-        quantise([(1, 2)], woven12, "codes10")
-        scaled1 = keep.tile([P, S], F32, name="scaled1")
-        bias_and_gate(1, 0, scaled1[:, 0:W])
-        scatter(0, 0, W, scaled_first[:])
-        scatter(1, 0, SECOND_SCATTER, scaled1[:, 0:SECOND_SCATTER])
-        scaled_later = keep.tile([P, S - W], F32, name="scaled_later")
-        later = [scaled_later[:], scaled1[:, W:S]]
-        for h in range(HALVES):
-            for i in range(1, PIECES):
+        quantise(1, 2, 3, woven12[:])
+        bias_and_gate(1, 0)
+        for i in range(1, PIECES):
+            for h in range(HALVES):
                 multiply(h, i)
-                bias_and_gate(h, i, later[h][:, (i - 1) * W : i * W])
-        scatter(0, W, S, later[0])
-        add_residual_and_store(nc.gpsimd, nc.sync, 0, GPSIMD_SUMS)
-        scatter(1, SECOND_SCATTER, S, scaled1[:, SECOND_SCATTER:S])
-        add_residual_and_store(nc.vector, nc.scalar, 1, VECTOR_SUMS)
+                bias_and_gate(h, i)
+        for h in range(HALVES):
+            for s0 in range(0, S, S // SCATTERS[h]):
+                scatter(h, s0, s0 + S // SCATTERS[h])
+        for h in range(HALVES):
+            for t0 in range(0, T, T // SUMS[h]):
+                tokens = slice(t0, t0 + T // SUMS[h])
+                nc.vector.tensor_tensor(total[h][:, tokens], window[h][:, tokens], residual[:, h, tokens], ADD)
+                nc.sync.dma_start(out[h * P : (h + 1) * P, tokens], total[h][:, tokens])

@@ -30,9 +30,10 @@ COPY = mybir.ActivationFunctionType.Copy
 
 ALIGN = 256
 BIAS_ROW = 8
-SUMS = (2, 4)
+SPARE = HALVES * BIAS_ROW
+SUMS = (4, 4)
 VECTOR_PLAIN = 64
-SCATTERS = (3, 3)
+FIRST_ON_SCALAR = 192
 
 
 def tile_moe_res_lin_bias_kernel(tc, xT, xr, w_words, w_scales, b, gate, offs, out):
@@ -44,8 +45,7 @@ def tile_moe_res_lin_bias_kernel(tc, xT, xr, w_words, w_scales, b, gate, offs, o
         offsets = keep.tile([P, S // 16], U16, name="offsets")
         w_code = keep.tile([P, E * PASSES, 2 * N], U8, name="w_code", align_bytes=ALIGN)
         w_scale = keep.tile([P, E * PASSES * N], U8, name="w_scale", align_bytes=ALIGN)
-        spare = (0, HALVES * BIAS_ROW)
-        window = [keep.tile([P, T + spare[h]], F32, name=f"window{h}", align_bytes=ALIGN) for h in range(HALVES)]
+        window = [keep.tile([P, T + h * SPARE], F32, name=f"window{h}", align_bytes=ALIGN) for h in range(HALVES)]
         total = [keep.tile([P, T], F32, name=f"total{h}", align_bytes=ALIGN) for h in range(HALVES)]
         residual = keep.tile([P, HALVES, T], F32, name="residual", align_bytes=ALIGN)
         bias = window[1][:, T:].rearrange("p (h e) -> p h e", h=HALVES)
@@ -54,8 +54,8 @@ def tile_moe_res_lin_bias_kernel(tc, xT, xr, w_words, w_scales, b, gate, offs, o
         gates = [first_gates[:], later_gates[:, 0:W], later_gates[:, W : 2 * W]]
 
         nc.gpsimd.memset(w_scale[:].bitcast(I32), 0)
-        nc.vector.memset(window[0][:], 0.0)
-        nc.scalar.activation(window[1][:, 0:T], window[0][:], IDENTITY)
+        nc.vector.memset(window[0][:, 0:T], 0.0)
+        nc.scalar.activation(window[1][:, 0:T], window[0][:, 0:T], IDENTITY)
 
         rows = {}
         for a in range(PASSES):
@@ -72,15 +72,22 @@ def tile_moe_res_lin_bias_kernel(tc, xT, xr, w_words, w_scales, b, gate, offs, o
             groups = slice(i0 * PIECE * PASSES, i1 * PIECE * PASSES)
             nc.sync.dma_start(w_code[:, groups, :], code_rows[:, groups, :])
 
-        nc.sync.dma_start(bias[:, :, 0:E], b.rearrange("(h p) e -> p h e", p=P))
-        load_codes(0, 1)
         w_scale_words = w_scale[:].bitcast(I32).rearrange("p (g n) -> p g n", g=E * PASSES)
         scale_rows = w_scales.bitcast(I32).rearrange("e a (q r) n -> r q (e a) n", r=4)
-        for r in range(4):
-            nc.sync.dma_start(w_scale_words[r:P:32], scale_rows[r])
+
+        def load_scales(i0, i1):
+            groups = slice(i0 * PIECE * PASSES, i1 * PIECE * PASSES)
+            for r in range(4):
+                nc.sync.dma_start(w_scale_words[r:P:32, groups, :], scale_rows[r][:, groups, :])
+
+        load_codes(0, 1)
+        load_scales(0, 1)
+        nc.sync.dma_start(bias[:, :, 0:E], b.rearrange("(h p) e -> p h e", p=P))
         nc.sync.dma_start(first_gates[:], gate[0:P, 0:W])
-        load_codes(1, PIECES)
+        load_codes(1, 2)
+        load_scales(1, PIECES)
         nc.sync.dma_start(later_gates[:], gate[0:P, W:S])
+        load_codes(2, 3)
         nc.sync.dma_start(residual[:], xr.rearrange("(h p) t -> p h t", p=P))
 
         def listed(tile, s0, s1):
@@ -103,16 +110,16 @@ def tile_moe_res_lin_bias_kernel(tc, xT, xr, w_words, w_scales, b, gate, offs, o
 
         codes, scales = {}, {}
 
-        def quantise(a, i0, i1, woven, behind=""):
-            code = keep.tile([P, (i1 - i0) * W], U32, name=f"codes{a}{i0}", tag=behind, align_bytes=ALIGN)
-            scale = keep.tile([P, (i1 - i0) * W], U8, name=f"scales{a}{i0}", align_bytes=ALIGN)
+        def quantise(a, e0, e1, woven, behind=""):
+            code = keep.tile([P, (e1 - e0) * C], U32, name=f"codes{a}{e0}", tag=behind, align_bytes=ALIGN)
+            scale = keep.tile([P, (e1 - e0) * C], U8, name=f"scales{a}{e0}", align_bytes=ALIGN)
             nc.vector.quantize_mx(out=code[:].bitcast(FP8X4), scales=scale[:], in_=woven.rearrange("p s d -> p (s d)"))
-            for i in range(i0, i1):
-                codes[a, i] = code[:, (i - i0) * W : (i - i0 + 1) * W]
-                scales[a, i] = scale[:, (i - i0) * W : (i - i0 + 1) * W]
+            for e in range(e0, e1):
+                codes[a, e] = code[:, (e - e0) * C : (e - e0 + 1) * C]
+                scales[a, e] = scale[:, (e - e0) * C : (e - e0 + 1) * C]
 
-        def unwoven(a, i0, i1):
-            return plain[a][:, :, (i0 - 1) * W : (i1 - 1) * W].rearrange("p d s -> p s d")
+        def unwoven(a, e0, e1):
+            return plain[a][:, :, e0 * C - W : e1 * C - W].rearrange("p d s -> p s d")
 
         sums = [[None] * E for h in range(HALVES)]
         for h in range(HALVES):
@@ -126,22 +133,20 @@ def tile_moe_res_lin_bias_kernel(tc, xT, xr, w_words, w_scales, b, gate, offs, o
                         sums[h][i * PIECE + j] = bank[:, j * C : (j + 1) * C]
 
         def one_pass(h, e, a, opening_pass):
-            i, j = divmod(e, PIECE)
             group = e * PASSES + a
             nc.tensor.matmul_mx(
                 out=sums[h][e],
                 lhsT=w_code[:, group, 2 * P * h : 2 * P * (h + 1)].bitcast(FP4X4),
                 lhsT_scale=w_scale[:, group * N + h * P : group * N + (h + 1) * P],
-                rhs=codes[a, i][:, j * C : (j + 1) * C].bitcast(FP8X4),
-                rhs_scale=scales[a, i][:, j * C : (j + 1) * C],
+                rhs=codes[a, e].bitcast(FP8X4),
+                rhs_scale=scales[a, e],
                 start=(a == opening_pass),
                 stop=(a != opening_pass),
             )
 
-        def multiply(h, i):
-            for e in range(i * PIECE, (i + 1) * PIECE):
-                for a in reversed(range(PASSES)):
-                    one_pass(h, e, a, PASSES - 1)
+        def multiply(h, e):
+            for a in reversed(range(PASSES)):
+                one_pass(h, e, a, PASSES - 1)
 
         scaled = [keep.tile([P, S], F32, name=f"scaled{h}", align_bytes=ALIGN) for h in range(HALVES)]
 
@@ -152,6 +157,18 @@ def tile_moe_res_lin_bias_kernel(tc, xT, xr, w_words, w_scales, b, gate, offs, o
                 nc.scalar.activation(biased[:, j * C : (j + 1) * C], sums[h][e], IDENTITY, bias=bias[:, h, e : e + 1])
             nc.gpsimd.tensor_tensor(scaled[h][:, i * W : (i + 1) * W], biased[:], gates[i], MULT)
 
+        def empty_on_vector(h, i):
+            for j in range(PIECE):
+                e = i * PIECE + j
+                nc.vector.scalar_tensor_tensor(
+                    scaled[h][:, e * C : (e + 1) * C],
+                    sums[h][e],
+                    first_bias[h][:, e : e + 1],
+                    gates[i][:, j * C : (j + 1) * C],
+                    ADD,
+                    MULT,
+                )
+
         def scatter(h, s0, s1):
             if h == 0:
                 nc.vector.tensor_copy(listed(window[h], s0, s1), scaled[h][:, s0:s1])
@@ -160,41 +177,44 @@ def tile_moe_res_lin_bias_kernel(tc, xT, xr, w_words, w_scales, b, gate, offs, o
 
         for d in range(PACK):
             gather_row(0, d)
-        quantise(0, 0, 1, first[0][:])
+        quantise(0, 0, 2, first[0][:])
         woven0 = keep.tile([P, S - W, PACK], BF16, name="woven0", tag="first0", align_bytes=ALIGN)
-        nc.gpsimd.tensor_scalar(woven0[:], unwoven(0, 1, 3), 1.0, 0.0, MULT, ADD)
+        nc.gpsimd.tensor_scalar(woven0[:], unwoven(0, 2, 6), 1.0, 0.0, MULT, ADD)
         for d in range(PACK - 1):
             gather_row(1, d)
-        quantise(0, 1, 3, woven0[:], "row11")
-        for h in range(HALVES):
+        quantise(0, 2, 6, woven0[:], "row11")
+        first_bias = {}
+        for h in reversed(range(HALVES)):
+            first_bias[h] = keep.tile([P, PIECE], F32, name=f"first_bias{h}", align_bytes=ALIGN)
+            nc.gpsimd.tensor_copy(first_bias[h][:], bias[:, h, 0:PIECE])
             for e in range(PIECE):
                 one_pass(h, e, 0, 0)
         gather_first(1, PACK - 1)
-        gather_plain(1, PACK - 1, W, 2 * W)
+        nc.vector.tensor_copy(plain[1][:, PACK - 1, 0:VECTOR_PLAIN], listed(rows[1, PACK - 1], W, W + VECTOR_PLAIN))
+        gather_plain(1, PACK - 1, W + VECTOR_PLAIN, 2 * W)
         gather_plain(1, PACK - 1, 2 * W, S)
-        woven11 = keep.tile([P, W, PACK], BF16, name="woven11", align_bytes=ALIGN)
-        nc.vector.tensor_copy(woven11[:], unwoven(1, 1, 2))
+        quantise(1, 0, 2, first[1][:])
         woven12 = keep.tile([P, W, PACK], BF16, name="woven12", align_bytes=ALIGN)
-        nc.scalar.copy(woven12[:], unwoven(1, 2, 3))
-        quantise(1, 0, 1, first[1][:])
-        quantise(1, 1, 2, woven11[:])
-        for e in range(PIECE):
-            one_pass(0, e, 1, 0)
-            slots = slice(e * C, (e + 1) * C)
-            nc.vector.scalar_tensor_tensor(
-                scaled[0][:, slots], sums[0][e], bias[:, 0, e : e + 1], gates[0][:, slots], ADD, MULT
-            )
-        for e in range(PIECE):
-            one_pass(1, e, 1, 0)
-        quantise(1, 2, 3, woven12[:])
-        bias_and_gate(1, 0)
+        nc.vector.tensor_copy(woven12[:], unwoven(1, 2, 4))
+        woven14 = keep.tile([P, W, PACK], BF16, name="woven14", align_bytes=ALIGN)
+        nc.scalar.copy(woven14[:], unwoven(1, 4, 6))
+        for h in reversed(range(HALVES)):
+            for e in range(PIECE):
+                one_pass(h, e, 1, 0)
+            empty_on_vector(h, 0)
+        quantise(1, 2, 4, woven12[:], "first_bias1")
+        quantise(1, 4, 6, woven14[:], "first_bias0")
+        scatter(0, 0, W)
+        scatter(1, 0, FIRST_ON_SCALAR)
         for i in range(1, PIECES):
             for h in range(HALVES):
-                multiply(h, i)
+                for e in range(i * PIECE, (i + 1) * PIECE):
+                    multiply(h, e)
                 bias_and_gate(h, i)
-        for h in range(HALVES):
-            for s0 in range(0, S, S // SCATTERS[h]):
-                scatter(h, s0, s0 + S // SCATTERS[h])
+        for i in range(1, PIECES):
+            scatter(0, i * W, (i + 1) * W)
+        scatter(1, FIRST_ON_SCALAR, 2 * W)
+        scatter(1, 2 * W, S)
         for h in range(HALVES):
             for t0 in range(0, T, T // SUMS[h]):
                 tokens = slice(t0, t0 + T // SUMS[h])

@@ -31,8 +31,9 @@ COPY = mybir.ActivationFunctionType.Copy
 ALIGN = 256
 BIAS_ROW = 8
 SPARE = HALVES * BIAS_ROW
-SUMS = (4, 4)
+SUM_CUTS = (0, 384, 832, T)
 VECTOR_PLAIN = 64
+STEPPED = (3 * C, 2 * C)
 FIRST_ON_SCALAR = 192
 
 
@@ -80,32 +81,35 @@ def tile_moe_res_lin_bias_kernel(tc, xT, xr, w_words, w_scales, b, gate, offs, o
             for r in range(4):
                 nc.sync.dma_start(w_scale_words[r:P:32, groups, :], scale_rows[r][:, groups, :])
 
+        nc.sync.dma_start(bias[:, :, 0:E], b.rearrange("(h p) e -> p h e", p=P))
         load_codes(0, 1)
         load_scales(0, 1)
-        nc.sync.dma_start(bias[:, :, 0:E], b.rearrange("(h p) e -> p h e", p=P))
         nc.sync.dma_start(first_gates[:], gate[0:P, 0:W])
         load_codes(1, 2)
         load_scales(1, PIECES)
-        nc.sync.dma_start(later_gates[:], gate[0:P, W:S])
+        nc.sync.dma_start(later_gates[:, 0:W], gate[0:P, W : 2 * W])
         load_codes(2, 3)
-        nc.sync.dma_start(residual[:], xr.rearrange("(h p) t -> p h t", p=P))
+        nc.sync.dma_start(later_gates[:, W : 2 * W], gate[0:P, 2 * W : S])
+        for h in range(HALVES):
+            nc.sync.dma_start(residual[:, h, :], xr[h * P : (h + 1) * P, :])
 
         def listed(tile, s0, s1):
             return tile[:].indirect(offsets[:, s0 // 16 : s1 // 16])
 
-        first = [keep.tile([P, W, PACK], BF16, name=f"first{a}", align_bytes=ALIGN) for a in range(PASSES)]
-        plain = [keep.tile([P, PACK, S - W], BF16, name=f"plain{a}", align_bytes=ALIGN) for a in range(PASSES)]
+        first = [keep.tile([P, STEPPED[a], PACK], BF16, name=f"first{a}", align_bytes=ALIGN) for a in range(PASSES)]
+        plain = [keep.tile([P, PACK, S - STEPPED[a]], BF16, name=f"plain{a}", align_bytes=ALIGN) for a in range(PASSES)]
 
         def gather_first(a, d):
-            nc.vector.tensor_copy(first[a][:, :, d], listed(rows[a, d], 0, W))
+            nc.vector.tensor_copy(first[a][:, :, d], listed(rows[a, d], 0, STEPPED[a]))
 
         def gather_plain(a, d, s0, s1):
-            nc.scalar.activation(plain[a][:, d, s0 - W : s1 - W], listed(rows[a, d], s0, s1), COPY)
+            nc.scalar.activation(plain[a][:, d, s0 - STEPPED[a] : s1 - STEPPED[a]], listed(rows[a, d], s0, s1), COPY)
 
-        def gather_row(a, d):
+        def gather_row(a, d, extra):
             gather_first(a, d)
-            cut = W + VECTOR_PLAIN
-            nc.vector.tensor_copy(plain[a][:, d, 0:VECTOR_PLAIN], listed(rows[a, d], W, cut))
+            cut = STEPPED[a] + extra
+            if extra:
+                nc.vector.tensor_copy(plain[a][:, d, 0:extra], listed(rows[a, d], STEPPED[a], cut))
             gather_plain(a, d, cut, S)
 
         codes, scales = {}, {}
@@ -119,7 +123,7 @@ def tile_moe_res_lin_bias_kernel(tc, xT, xr, w_words, w_scales, b, gate, offs, o
                 scales[a, e] = scale[:, (e - e0) * C : (e - e0 + 1) * C]
 
         def unwoven(a, e0, e1):
-            return plain[a][:, :, e0 * C - W : e1 * C - W].rearrange("p d s -> p s d")
+            return plain[a][:, :, e0 * C - STEPPED[a] : e1 * C - STEPPED[a]].rearrange("p d s -> p s d")
 
         sums = [[None] * E for h in range(HALVES)]
         for h in range(HALVES):
@@ -176,19 +180,19 @@ def tile_moe_res_lin_bias_kernel(tc, xT, xr, w_words, w_scales, b, gate, offs, o
                 nc.scalar.activation(listed(window[h], s0, s1), scaled[h][:, s0:s1], COPY)
 
         for d in range(PACK):
-            gather_row(0, d)
-        quantise(0, 0, 2, first[0][:])
-        woven0 = keep.tile([P, S - W, PACK], BF16, name="woven0", tag="first0", align_bytes=ALIGN)
-        nc.gpsimd.tensor_scalar(woven0[:], unwoven(0, 2, 6), 1.0, 0.0, MULT, ADD)
+            gather_row(0, d, 0)
+        quantise(0, 0, 3, first[0][:])
+        woven0 = keep.tile([P, S - STEPPED[0], PACK], BF16, name="woven0", tag="first0", align_bytes=ALIGN)
+        nc.gpsimd.tensor_scalar(woven0[:], unwoven(0, 3, 6), 1.0, 0.0, MULT, ADD)
         for d in range(PACK - 1):
-            gather_row(1, d)
-        quantise(0, 2, 6, woven0[:], "row11")
+            gather_row(1, d, VECTOR_PLAIN)
+        quantise(0, 3, 6, woven0[:], "row11")
         first_bias = {}
         for h in reversed(range(HALVES)):
             first_bias[h] = keep.tile([P, PIECE], F32, name=f"first_bias{h}", align_bytes=ALIGN)
             nc.gpsimd.tensor_copy(first_bias[h][:], bias[:, h, 0:PIECE])
-            for e in range(PIECE):
-                one_pass(h, e, 0, 0)
+        for e in range(PIECE):
+            one_pass(1, e, 0, 0)
         gather_first(1, PACK - 1)
         nc.vector.tensor_copy(plain[1][:, PACK - 1, 0:VECTOR_PLAIN], listed(rows[1, PACK - 1], W, W + VECTOR_PLAIN))
         gather_plain(1, PACK - 1, W + VECTOR_PLAIN, 2 * W)
@@ -198,10 +202,12 @@ def tile_moe_res_lin_bias_kernel(tc, xT, xr, w_words, w_scales, b, gate, offs, o
         nc.vector.tensor_copy(woven12[:], unwoven(1, 2, 4))
         woven14 = keep.tile([P, W, PACK], BF16, name="woven14", align_bytes=ALIGN)
         nc.scalar.copy(woven14[:], unwoven(1, 4, 6))
-        for h in reversed(range(HALVES)):
-            for e in range(PIECE):
-                one_pass(h, e, 1, 0)
-            empty_on_vector(h, 0)
+        for e in range(PIECE):
+            one_pass(1, e, 1, 0)
+        empty_on_vector(1, 0)
+        for e in range(PIECE):
+            multiply(0, e)
+        empty_on_vector(0, 0)
         quantise(1, 2, 4, woven12[:], "first_bias1")
         quantise(1, 4, 6, woven14[:], "first_bias0")
         scatter(0, 0, W)
@@ -216,7 +222,7 @@ def tile_moe_res_lin_bias_kernel(tc, xT, xr, w_words, w_scales, b, gate, offs, o
         scatter(1, FIRST_ON_SCALAR, 2 * W)
         scatter(1, 2 * W, S)
         for h in range(HALVES):
-            for t0 in range(0, T, T // SUMS[h]):
-                tokens = slice(t0, t0 + T // SUMS[h])
+            for t0, t1 in zip(SUM_CUTS, SUM_CUTS[1:]):
+                tokens = slice(t0, t1)
                 nc.vector.tensor_tensor(total[h][:, tokens], window[h][:, tokens], residual[:, h, tokens], ADD)
                 nc.sync.dma_start(out[h * P : (h + 1) * P, tokens], total[h][:, tokens])

@@ -182,11 +182,11 @@ def tile_moe_res_lin_bias_kernel(tc, xT, xr, w_words, w_scales, b, gate, offs, o
         for d in range(PACK):
             gather_row(0, d, 0)
         quantise(0, 0, 3, first[0][:])
-        woven0 = keep.tile([P, S - STEPPED[0], PACK], BF16, name="woven0", tag="first0", align_bytes=ALIGN)
-        nc.gpsimd.tensor_scalar(woven0[:], unwoven(0, 3, 6), 1.0, 0.0, MULT, ADD)
+        woven0 = keep.tile([P, S - STEPPED[0], PACK], BF16, name="woven0", align_bytes=ALIGN)
+        nc.vector.tensor_copy(woven0[:], unwoven(0, 3, 6))
         for d in range(PACK - 1):
-            gather_row(1, d, VECTOR_PLAIN)
-        quantise(0, 3, 6, woven0[:], "row11")
+            gather_row(1, d, 0)
+        quantise(0, 3, 6, woven0[:])
         first_bias = {}
         for h in reversed(range(HALVES)):
             first_bias[h] = keep.tile([P, PIECE], F32, name=f"first_bias{h}", align_bytes=ALIGN)

@@ -30,11 +30,11 @@ COPY = mybir.ActivationFunctionType.Copy
 
 ALIGN = 256
 BIAS_ROW = 8
-SPARE = HALVES * BIAS_ROW
-SUM_CUTS = (0, 384, 832, T)
+STEPPED_EXPERTS = (3, PIECE)
 VECTOR_PLAIN = 64
-STEPPED = (3 * C, 2 * C)
+RUN = 4
 FIRST_ON_SCALAR = 192
+SUM_CUTS = (0, 384, 832, T)
 
 
 def tile_moe_res_lin_bias_kernel(tc, xT, xr, w_words, w_scales, b, gate, offs, out):
@@ -46,7 +46,8 @@ def tile_moe_res_lin_bias_kernel(tc, xT, xr, w_words, w_scales, b, gate, offs, o
         offsets = keep.tile([P, S // 16], U16, name="offsets")
         w_code = keep.tile([P, E * PASSES, 2 * N], U8, name="w_code", align_bytes=ALIGN)
         w_scale = keep.tile([P, E * PASSES * N], U8, name="w_scale", align_bytes=ALIGN)
-        window = [keep.tile([P, T + h * SPARE], F32, name=f"window{h}", align_bytes=ALIGN) for h in range(HALVES)]
+        spare = (0, HALVES * BIAS_ROW)
+        window = [keep.tile([P, T + spare[h]], F32, name=f"window{h}", align_bytes=ALIGN) for h in range(HALVES)]
         total = [keep.tile([P, T], F32, name=f"total{h}", align_bytes=ALIGN) for h in range(HALVES)]
         residual = keep.tile([P, HALVES, T], F32, name="residual", align_bytes=ALIGN)
         bias = window[1][:, T:].rearrange("p (h e) -> p h e", h=HALVES)
@@ -68,49 +69,52 @@ def tile_moe_res_lin_bias_kernel(tc, xT, xr, w_words, w_scales, b, gate, offs, o
                     nc.sync.dma_start(offsets[:], offs)
 
         code_rows = w_words.rearrange("e a p n -> p (e a) n")
-
-        def load_codes(i0, i1):
-            groups = slice(i0 * PIECE * PASSES, i1 * PIECE * PASSES)
-            nc.sync.dma_start(w_code[:, groups, :], code_rows[:, groups, :])
-
         w_scale_words = w_scale[:].bitcast(I32).rearrange("p (g n) -> p g n", g=E * PASSES)
         scale_rows = w_scales.bitcast(I32).rearrange("e a (q r) n -> r q (e a) n", r=4)
 
-        def load_scales(i0, i1):
-            groups = slice(i0 * PIECE * PASSES, i1 * PIECE * PASSES)
+        def load_codes(e0, e1):
+            groups = slice(e0 * PASSES, e1 * PASSES)
+            nc.sync.dma_start(w_code[:, groups, :], code_rows[:, groups, :])
+
+        def load_scales(e0, e1):
+            groups = slice(e0 * PASSES, e1 * PASSES)
             for r in range(4):
                 nc.sync.dma_start(w_scale_words[r:P:32, groups, :], scale_rows[r][:, groups, :])
 
+        def load_gates(i):
+            nc.sync.dma_start(gates[i], gate[0:P, i * W : (i + 1) * W])
+
         nc.sync.dma_start(bias[:, :, 0:E], b.rearrange("(h p) e -> p h e", p=P))
-        load_codes(0, 1)
-        load_scales(0, 1)
-        nc.sync.dma_start(first_gates[:], gate[0:P, 0:W])
-        load_codes(1, 2)
-        load_scales(1, PIECES)
-        nc.sync.dma_start(later_gates[:, 0:W], gate[0:P, W : 2 * W])
-        load_codes(2, 3)
-        nc.sync.dma_start(later_gates[:, W : 2 * W], gate[0:P, 2 * W : S])
+        load_codes(0, PIECE)
+        load_scales(0, PIECE)
+        load_gates(0)
+        load_codes(PIECE, 2 * PIECE)
+        load_scales(PIECE, E)
+        load_gates(1)
+        load_codes(2 * PIECE, E)
+        load_gates(2)
         for h in range(HALVES):
             nc.sync.dma_start(residual[:, h, :], xr[h * P : (h + 1) * P, :])
 
         def listed(tile, s0, s1):
             return tile[:].indirect(offsets[:, s0 // 16 : s1 // 16])
 
-        first = [keep.tile([P, STEPPED[a], PACK], BF16, name=f"first{a}", align_bytes=ALIGN) for a in range(PASSES)]
-        plain = [keep.tile([P, PACK, S - STEPPED[a]], BF16, name=f"plain{a}", align_bytes=ALIGN) for a in range(PASSES)]
+        stepped = [experts * C for experts in STEPPED_EXPERTS]
+        direct = [keep.tile([P, stepped[a], PACK], BF16, name=f"direct{a}", align_bytes=ALIGN) for a in range(PASSES)]
+        plain = [keep.tile([P, PACK, S - stepped[a]], BF16, name=f"plain{a}", align_bytes=ALIGN) for a in range(PASSES)]
 
-        def gather_first(a, d):
-            nc.vector.tensor_copy(first[a][:, :, d], listed(rows[a, d], 0, STEPPED[a]))
+        def gather_direct(a, d):
+            nc.vector.tensor_copy(direct[a][:, :, d], listed(rows[a, d], 0, stepped[a]))
+
+        def plain_run(a, d, s0, s1):
+            return plain[a][:, d, s0 - stepped[a] : s1 - stepped[a]]
 
         def gather_plain(a, d, s0, s1):
-            nc.scalar.activation(plain[a][:, d, s0 - STEPPED[a] : s1 - STEPPED[a]], listed(rows[a, d], s0, s1), COPY)
+            nc.scalar.activation(plain_run(a, d, s0, s1), listed(rows[a, d], s0, s1), COPY)
 
-        def gather_row(a, d, extra):
-            gather_first(a, d)
-            cut = STEPPED[a] + extra
-            if extra:
-                nc.vector.tensor_copy(plain[a][:, d, 0:extra], listed(rows[a, d], STEPPED[a], cut))
-            gather_plain(a, d, cut, S)
+        def weave(copy, woven, a, e0, e1):
+            runs = plain[a][:, :, e0 * C - stepped[a] : e1 * C - stepped[a]]
+            copy(woven.rearrange("p (c i) d -> p c d i", i=RUN), runs.rearrange("p d (c i) -> p c d i", i=RUN))
 
         codes, scales = {}, {}
 
@@ -121,9 +125,6 @@ def tile_moe_res_lin_bias_kernel(tc, xT, xr, w_words, w_scales, b, gate, offs, o
             for e in range(e0, e1):
                 codes[a, e] = code[:, (e - e0) * C : (e - e0 + 1) * C]
                 scales[a, e] = scale[:, (e - e0) * C : (e - e0 + 1) * C]
-
-        def unwoven(a, e0, e1):
-            return plain[a][:, :, e0 * C - STEPPED[a] : e1 * C - STEPPED[a]].rearrange("p d s -> p s d")
 
         sums = [[None] * E for h in range(HALVES)]
         for h in range(HALVES):
@@ -161,66 +162,67 @@ def tile_moe_res_lin_bias_kernel(tc, xT, xr, w_words, w_scales, b, gate, offs, o
                 nc.scalar.activation(biased[:, j * C : (j + 1) * C], sums[h][e], IDENTITY, bias=bias[:, h, e : e + 1])
             nc.gpsimd.tensor_tensor(scaled[h][:, i * W : (i + 1) * W], biased[:], gates[i], MULT)
 
-        def empty_on_vector(h, i):
-            for j in range(PIECE):
-                e = i * PIECE + j
+        first_bias = {}
+
+        def empty_first_piece(h):
+            for e in range(PIECE):
+                slots = slice(e * C, (e + 1) * C)
                 nc.vector.scalar_tensor_tensor(
-                    scaled[h][:, e * C : (e + 1) * C],
-                    sums[h][e],
-                    first_bias[h][:, e : e + 1],
-                    gates[i][:, j * C : (j + 1) * C],
-                    ADD,
-                    MULT,
+                    scaled[h][:, slots], sums[h][e], first_bias[h][:, e : e + 1], gates[0][:, slots], ADD, MULT
                 )
 
-        def scatter(h, s0, s1):
-            if h == 0:
-                nc.vector.tensor_copy(listed(window[h], s0, s1), scaled[h][:, s0:s1])
-            else:
-                nc.scalar.activation(listed(window[h], s0, s1), scaled[h][:, s0:s1], COPY)
+        def scatter_on_vector(s0, s1):
+            nc.vector.tensor_copy(listed(window[0], s0, s1), scaled[0][:, s0:s1])
+
+        def scatter_on_scalar(s0, s1):
+            nc.scalar.activation(listed(window[1], s0, s1), scaled[1][:, s0:s1], COPY)
 
         for d in range(PACK):
-            gather_row(0, d, 0)
-        quantise(0, 0, 3, first[0][:])
-        woven0 = keep.tile([P, S - STEPPED[0], PACK], BF16, name="woven0", align_bytes=ALIGN)
-        nc.vector.tensor_copy(woven0[:], unwoven(0, 3, 6))
-        for d in range(PACK - 1):
-            gather_row(1, d, 0)
-        quantise(0, 3, 6, woven0[:])
-        first_bias = {}
+            gather_direct(0, d)
+            gather_plain(0, d, stepped[0], S)
+        first_plain = STEPPED_EXPERTS[0]
+        woven0 = keep.tile([P, S - stepped[0], PACK], BF16, name="woven0", align_bytes=ALIGN)
+        cut = (E - 1 - first_plain) * C
+        weave(nc.vector.tensor_copy, woven0[:, 0:cut, :], 0, first_plain, E - 1)
+        weave(nc.scalar.copy, woven0[:, cut:, :], 0, E - 1, E)
+        quantise(0, 0, first_plain, direct[0][:], "row03")
+        last = PACK - 1
+        for d in range(last):
+            gather_direct(1, d)
+            gather_plain(1, d, W, S)
+        quantise(0, first_plain, E, woven0[:])
         for h in reversed(range(HALVES)):
             first_bias[h] = keep.tile([P, PIECE], F32, name=f"first_bias{h}", align_bytes=ALIGN)
             nc.gpsimd.tensor_copy(first_bias[h][:], bias[:, h, 0:PIECE])
         for e in range(PIECE):
             one_pass(1, e, 0, 0)
-        gather_first(1, PACK - 1)
-        nc.vector.tensor_copy(plain[1][:, PACK - 1, 0:VECTOR_PLAIN], listed(rows[1, PACK - 1], W, W + VECTOR_PLAIN))
-        gather_plain(1, PACK - 1, W + VECTOR_PLAIN, 2 * W)
-        gather_plain(1, PACK - 1, 2 * W, S)
-        quantise(1, 0, 2, first[1][:])
-        woven12 = keep.tile([P, W, PACK], BF16, name="woven12", align_bytes=ALIGN)
-        nc.vector.tensor_copy(woven12[:], unwoven(1, 2, 4))
-        woven14 = keep.tile([P, W, PACK], BF16, name="woven14", align_bytes=ALIGN)
-        nc.scalar.copy(woven14[:], unwoven(1, 4, 6))
+        gather_direct(1, last)
+        nc.vector.tensor_copy(plain_run(1, last, W, W + VECTOR_PLAIN), listed(rows[1, last], W, W + VECTOR_PLAIN))
+        gather_plain(1, last, W + VECTOR_PLAIN, 2 * W)
+        gather_plain(1, last, 2 * W, S)
+        quantise(1, 0, PIECE, direct[1][:])
+        woven1 = [keep.tile([P, W, PACK], BF16, name=f"woven1{i}", align_bytes=ALIGN) for i in range(1, PIECES)]
+        weave(nc.vector.tensor_copy, woven1[0][:], 1, PIECE, 2 * PIECE)
+        weave(nc.scalar.copy, woven1[1][:], 1, 2 * PIECE, E)
         for e in range(PIECE):
             one_pass(1, e, 1, 0)
-        empty_on_vector(1, 0)
+        empty_first_piece(1)
         for e in range(PIECE):
             multiply(0, e)
-        empty_on_vector(0, 0)
-        quantise(1, 2, 4, woven12[:], "first_bias1")
-        quantise(1, 4, 6, woven14[:], "first_bias0")
-        scatter(0, 0, W)
-        scatter(1, 0, FIRST_ON_SCALAR)
+        empty_first_piece(0)
+        quantise(1, PIECE, 2 * PIECE, woven1[0][:], "first_bias1")
+        quantise(1, 2 * PIECE, E, woven1[1][:], "first_bias0")
+        scatter_on_vector(0, W)
+        scatter_on_scalar(0, FIRST_ON_SCALAR)
         for i in range(1, PIECES):
             for h in range(HALVES):
                 for e in range(i * PIECE, (i + 1) * PIECE):
                     multiply(h, e)
                 bias_and_gate(h, i)
         for i in range(1, PIECES):
-            scatter(0, i * W, (i + 1) * W)
-        scatter(1, FIRST_ON_SCALAR, 2 * W)
-        scatter(1, 2 * W, S)
+            scatter_on_vector(i * W, (i + 1) * W)
+        scatter_on_scalar(FIRST_ON_SCALAR, 2 * W)
+        scatter_on_scalar(2 * W, S)
         for h in range(HALVES):
             for t0, t1 in zip(SUM_CUTS, SUM_CUTS[1:]):
                 tokens = slice(t0, t1)

@@ -34,6 +34,7 @@ STEPPED_EXPERTS = (3, PIECE)
 VECTOR_PLAIN = 64
 RUN = 4
 FIRST_ON_SCALAR = 192
+FREE = ((0, 2), (0, 3), (1, 5))
 SUM_CUTS = (0, 384, 832, T)
 
 
@@ -155,12 +156,17 @@ def tile_moe_res_lin_bias_kernel(tc, xT, xr, w_words, w_scales, b, gate, offs, o
 
         scaled = [keep.tile([P, S], F32, name=f"scaled{h}", align_bytes=ALIGN) for h in range(HALVES)]
 
-        def bias_and_gate(h, i):
-            biased = keep.tile([P, W], F32, name=f"biased{h}{i}", align_bytes=ALIGN)
-            for j in range(PIECE):
-                e = i * PIECE + j
-                nc.scalar.activation(biased[:, j * C : (j + 1) * C], sums[h][e], IDENTITY, bias=bias[:, h, e : e + 1])
-            nc.gpsimd.tensor_tensor(scaled[h][:, i * W : (i + 1) * W], biased[:], gates[i], MULT)
+        free_bias = keep.tile([P, HALVES, BIAS_ROW], F32, name="free_bias")
+        biased = [keep.tile([P, S - W], F32, name=f"biased{h}", align_bytes=ALIGN) for h in range(HALVES)]
+
+        def add_bias(h, e):
+            slots = slice(e * C - W, (e + 1) * C - W)
+            source = free_bias if (h, e) in FREE else bias
+            nc.scalar.activation(biased[h][:, slots], sums[h][e], IDENTITY, bias=source[:, h, e : e + 1])
+
+        def apply_gates(h, e0, e1):
+            slots = slice(e0 * C - W, e1 * C - W)
+            nc.gpsimd.tensor_tensor(scaled[h][:, e0 * C : e1 * C], biased[h][:, slots], later_gates[:, slots], MULT)
 
         first_bias = {}
 
@@ -194,6 +200,7 @@ def tile_moe_res_lin_bias_kernel(tc, xT, xr, w_words, w_scales, b, gate, offs, o
         for h in reversed(range(HALVES)):
             first_bias[h] = keep.tile([P, PIECE], F32, name=f"first_bias{h}", align_bytes=ALIGN)
             nc.gpsimd.tensor_copy(first_bias[h][:], bias[:, h, 0:PIECE])
+        nc.gpsimd.tensor_copy(free_bias[:, :, 0:E], bias[:, :, 0:E])
         for e in range(PIECE):
             one_pass(1, e, 0, 0)
         gather_direct(1, last)
@@ -218,11 +225,15 @@ def tile_moe_res_lin_bias_kernel(tc, xT, xr, w_words, w_scales, b, gate, offs, o
             for h in range(HALVES):
                 for e in range(i * PIECE, (i + 1) * PIECE):
                     multiply(h, e)
-                bias_and_gate(h, i)
-        for i in range(1, PIECES):
-            scatter_on_vector(i * W, (i + 1) * W)
-        scatter_on_scalar(FIRST_ON_SCALAR, 2 * W)
-        scatter_on_scalar(2 * W, S)
+                for e in range(i * PIECE, (i + 1) * PIECE):
+                    add_bias(h, e)
+        apply_gates(0, PIECE, 2 * PIECE)
+        apply_gates(1, PIECE, E // 2)
+        apply_gates(1, E // 2, E)
+        scatter_on_vector(W, 2 * W)
+        nc.vector.tensor_tensor(listed(window[0], 2 * W, S), biased[0][:, W : 2 * W], gates[2], MULT)
+        scatter_on_scalar(FIRST_ON_SCALAR, S // 2)
+        scatter_on_scalar(S // 2, S)
         for h in range(HALVES):
             for t0, t1 in zip(SUM_CUTS, SUM_CUTS[1:]):
                 tokens = slice(t0, t1)

@@ -34,7 +34,7 @@ STEPPED_EXPERTS = (3, PIECE)
 VECTOR_PLAIN = 64
 RUN = 4
 FIRST_ON_SCALAR = 192
-FREE = ((0, 2), (0, 3), (1, 5))
+BESIDE_A_SCATTER = ((0, PIECE), (0, PIECE + 1), (1, E - 1))
 SUM_CUTS = (0, 384, 832, T)
 
 
@@ -133,6 +133,8 @@ def tile_moe_res_lin_bias_kernel(tc, xT, xr, w_words, w_scales, b, gate, offs, o
                 if i == 0:
                     for e in range(PIECE):
                         sums[h][e] = psum.tile([P, C], F32, name=f"lone{h}_{e}")[:]
+                elif (h, i) == (0, 1):
+                    sums[h][PIECE] = psum.tile([P, C], F32, name="bank0_1")[:]
                 else:
                     bank = psum.tile([P, W], F32, name=f"bank{h}_{i}")
                     for j in range(PIECE):
@@ -155,13 +157,12 @@ def tile_moe_res_lin_bias_kernel(tc, xT, xr, w_words, w_scales, b, gate, offs, o
                 one_pass(h, e, a, PASSES - 1)
 
         scaled = [keep.tile([P, S], F32, name=f"scaled{h}", align_bytes=ALIGN) for h in range(HALVES)]
-
         free_bias = keep.tile([P, HALVES, BIAS_ROW], F32, name="free_bias")
         biased = [keep.tile([P, S - W], F32, name=f"biased{h}", align_bytes=ALIGN) for h in range(HALVES)]
 
         def add_bias(h, e):
             slots = slice(e * C - W, (e + 1) * C - W)
-            source = free_bias if (h, e) in FREE else bias
+            source = free_bias if (h, e) in BESIDE_A_SCATTER else bias
             nc.scalar.activation(biased[h][:, slots], sums[h][e], IDENTITY, bias=source[:, h, e : e + 1])
 
         def apply_gates(h, e0, e1):
@@ -170,12 +171,10 @@ def tile_moe_res_lin_bias_kernel(tc, xT, xr, w_words, w_scales, b, gate, offs, o
 
         first_bias = {}
 
-        def empty_first_piece(h):
-            for e in range(PIECE):
-                slots = slice(e * C, (e + 1) * C)
-                nc.vector.scalar_tensor_tensor(
-                    scaled[h][:, slots], sums[h][e], first_bias[h][:, e : e + 1], gates[0][:, slots], ADD, MULT
-                )
+        def empty_on_vector(h, e):
+            slots = slice(e * C, (e + 1) * C)
+            source = first_bias[h][:] if e == 0 else free_bias[:, h, e : e + 1]
+            nc.vector.scalar_tensor_tensor(scaled[h][:, slots], sums[h][e], source, gates[0][:, slots], ADD, MULT)
 
         def scatter_on_vector(s0, s1):
             nc.vector.tensor_copy(listed(window[0], s0, s1), scaled[0][:, s0:s1])
@@ -198,8 +197,8 @@ def tile_moe_res_lin_bias_kernel(tc, xT, xr, w_words, w_scales, b, gate, offs, o
             gather_plain(1, d, W, S)
         quantise(0, first_plain, E, woven0[:])
         for h in reversed(range(HALVES)):
-            first_bias[h] = keep.tile([P, PIECE], F32, name=f"first_bias{h}", align_bytes=ALIGN)
-            nc.gpsimd.tensor_copy(first_bias[h][:], bias[:, h, 0:PIECE])
+            first_bias[h] = keep.tile([P, 1], F32, name=f"first_bias{h}", align_bytes=ALIGN)
+            nc.gpsimd.tensor_copy(first_bias[h][:], bias[:, h, 0:1])
         nc.gpsimd.tensor_copy(free_bias[:, :, 0:E], bias[:, :, 0:E])
         for e in range(PIECE):
             one_pass(1, e, 0, 0)
@@ -213,12 +212,14 @@ def tile_moe_res_lin_bias_kernel(tc, xT, xr, w_words, w_scales, b, gate, offs, o
         weave(nc.scalar.copy, woven1[1][:], 1, 2 * PIECE, E)
         for e in range(PIECE):
             one_pass(1, e, 1, 0)
-        empty_first_piece(1)
+        for e in range(PIECE):
+            empty_on_vector(1, e)
+        quantise(1, PIECE, 2 * PIECE, woven1[0][:], "first_bias1")
         for e in range(PIECE):
             multiply(0, e)
-        empty_first_piece(0)
-        quantise(1, PIECE, 2 * PIECE, woven1[0][:], "first_bias1")
+            empty_on_vector(0, e)
         quantise(1, 2 * PIECE, E, woven1[1][:], "first_bias0")
+        sums[0][PIECE + 1] = psum.tile([P, C], F32, name="again1_0", tag="lone1_0")[:]
         scatter_on_vector(0, W)
         scatter_on_scalar(0, FIRST_ON_SCALAR)
         for i in range(1, PIECES):

@@ -35,7 +35,7 @@ VECTOR_PLAIN = 64
 RUN = 4
 FIRST_ON_SCALAR = 192
 BESIDE_A_SCATTER = ((0, PIECE), (0, PIECE + 1), (1, E - 1))
-SUM_CUTS = (0, 384, 832, T)
+SUM_CUTS = (0, 256, 768, T)
 
 
 def tile_moe_res_lin_bias_kernel(tc, xT, xr, w_words, w_scales, b, gate, offs, out):

@@ -31,8 +31,6 @@ COPY = mybir.ActivationFunctionType.Copy
 ALIGN = 256
 BIAS_ROW = 8
 STEPPED_EXPERTS = (3, PIECE)
-VECTOR_PLAIN = 64
-RUN = 4
 FIRST_ON_SCALAR = 192
 BESIDE_A_SCATTER = ((0, PIECE), (0, PIECE + 1), (1, E - 1))
 SUM_CUTS = (0, 256, 768, T)
@@ -102,20 +100,20 @@ def tile_moe_res_lin_bias_kernel(tc, xT, xr, w_words, w_scales, b, gate, offs, o
 
         stepped = [experts * C for experts in STEPPED_EXPERTS]
         direct = [keep.tile([P, stepped[a], PACK], BF16, name=f"direct{a}", align_bytes=ALIGN) for a in range(PASSES)]
-        plain = [keep.tile([P, PACK, S - stepped[a]], BF16, name=f"plain{a}", align_bytes=ALIGN) for a in range(PASSES)]
+        pairs = [keep.tile([P, 2, S - stepped[a], 2], BF16, name=f"pairs{a}", align_bytes=ALIGN) for a in range(PASSES)]
 
         def gather_direct(a, d):
             nc.vector.tensor_copy(direct[a][:, :, d], listed(rows[a, d], 0, stepped[a]))
 
         def plain_run(a, d, s0, s1):
-            return plain[a][:, d, s0 - stepped[a] : s1 - stepped[a]]
+            return pairs[a][:, d // 2, s0 - stepped[a] : s1 - stepped[a], d % 2]
 
         def gather_plain(a, d, s0, s1):
             nc.scalar.activation(plain_run(a, d, s0, s1), listed(rows[a, d], s0, s1), COPY)
 
-        def weave(copy, woven, a, e0, e1):
-            runs = plain[a][:, :, e0 * C - stepped[a] : e1 * C - stepped[a]]
-            copy(woven.rearrange("p (c i) d -> p c d i", i=RUN), runs.rearrange("p d (c i) -> p c d i", i=RUN))
+        def weave(copy, word, woven, a, e0, e1):
+            runs = pairs[a][:].bitcast(word)[:, :, e0 * C - stepped[a] : e1 * C - stepped[a], 0]
+            copy(woven.bitcast(word), runs.rearrange("p u s -> p s u"))
 
         codes, scales = {}, {}
 
@@ -188,8 +186,8 @@ def tile_moe_res_lin_bias_kernel(tc, xT, xr, w_words, w_scales, b, gate, offs, o
         first_plain = STEPPED_EXPERTS[0]
         woven0 = keep.tile([P, S - stepped[0], PACK], BF16, name="woven0", align_bytes=ALIGN)
         cut = (E - 1 - first_plain) * C
-        weave(nc.vector.tensor_copy, woven0[:, 0:cut, :], 0, first_plain, E - 1)
-        weave(nc.scalar.copy, woven0[:, cut:, :], 0, E - 1, E)
+        weave(nc.vector.tensor_copy, I32, woven0[:, 0:cut, :], 0, first_plain, E - 1)
+        weave(nc.scalar.copy, U32, woven0[:, cut:, :], 0, E - 1, E)
         quantise(0, 0, first_plain, direct[0][:], "row03")
         last = PACK - 1
         for d in range(last):
@@ -203,13 +201,12 @@ def tile_moe_res_lin_bias_kernel(tc, xT, xr, w_words, w_scales, b, gate, offs, o
         for e in range(PIECE):
             one_pass(1, e, 0, 0)
         gather_direct(1, last)
-        nc.vector.tensor_copy(plain_run(1, last, W, W + VECTOR_PLAIN), listed(rows[1, last], W, W + VECTOR_PLAIN))
-        gather_plain(1, last, W + VECTOR_PLAIN, 2 * W)
+        gather_plain(1, last, W, 2 * W)
         gather_plain(1, last, 2 * W, S)
         quantise(1, 0, PIECE, direct[1][:])
         woven1 = [keep.tile([P, W, PACK], BF16, name=f"woven1{i}", align_bytes=ALIGN) for i in range(1, PIECES)]
-        weave(nc.vector.tensor_copy, woven1[0][:], 1, PIECE, 2 * PIECE)
-        weave(nc.scalar.copy, woven1[1][:], 1, 2 * PIECE, E)
+        weave(nc.vector.tensor_copy, I32, woven1[0][:], 1, PIECE, 2 * PIECE)
+        weave(nc.scalar.copy, U32, woven1[1][:], 1, 2 * PIECE, E)
         for e in range(PIECE):
             one_pass(1, e, 1, 0)
         for e in range(PIECE):

from contextlib import ExitStack

import concourse.mybir as mybir

K, T, E, C, N = 1024, 1280, 6, 128, 256
S = E * C
P = 128
K_PASS = 512
PASSES = K // K_PASS
PACK = 4
HALVES = N // P
PIECE = 2
PIECES = E // PIECE
W = PIECE * C

FLOPS = 2 * S * K * N
BYTES = 4 * K * T + 8 * N * T + E * K * N // 2 + E * K * N // 32 + 4 * N * E + 4 * S + 2 * P * S // 16

F32 = mybir.dt.float32
BF16 = mybir.dt.bfloat16
I32 = mybir.dt.int32
U32 = mybir.dt.uint32
U16 = mybir.dt.uint16
U8 = mybir.dt.uint8
FP8X4 = mybir.dt.float8_e4m3fn_x4
FP4X4 = mybir.dt.float4_e2m1fn_x4
ADD, MULT = mybir.AluOpType.add, mybir.AluOpType.mult
IDENTITY = mybir.ActivationFunctionType.Identity
COPY = mybir.ActivationFunctionType.Copy

ALIGN = 256
BIAS_ROW = 8
STEPPED_EXPERTS = (3, PIECE)
FIRST_ON_SCALAR = 192
BESIDE_A_SCATTER = ((0, PIECE), (0, PIECE + 1), (1, E - 1))
SUM_CUTS = (0, 256, 768, T)


def tile_moe_res_lin_bias_kernel(tc, xT, xr, w_words, w_scales, b, gate, offs, out):
    nc = tc.nc
    with ExitStack() as ctx:
        keep = ctx.enter_context(tc.tile_pool(name="keep", bufs=1))
        psum = ctx.enter_context(tc.psum_pool(name="psum", bufs=1))

        offsets = keep.tile([P, S // 16], U16, name="offsets")
        w_code = keep.tile([P, E * PASSES, 2 * N], U8, name="w_code", align_bytes=ALIGN)
        w_scale = keep.tile([P, E * PASSES * N], U8, name="w_scale", align_bytes=ALIGN)
        spare = (0, HALVES * BIAS_ROW)
        window = [keep.tile([P, T + spare[h]], F32, name=f"window{h}", align_bytes=ALIGN) for h in range(HALVES)]
        total = [keep.tile([P, T], F32, name=f"total{h}", align_bytes=ALIGN) for h in range(HALVES)]
        residual = keep.tile([P, HALVES, T], F32, name="residual", align_bytes=ALIGN)
        bias = window[1][:, T:].rearrange("p (h e) -> p h e", h=HALVES)
        first_gates = keep.tile([P, W], F32, name="first_gates", align_bytes=ALIGN)
        later_gates = keep.tile([P, S - W], F32, name="later_gates", align_bytes=ALIGN)
        gates = [first_gates[:], later_gates[:, 0:W], later_gates[:, W : 2 * W]]

        nc.gpsimd.memset(w_scale[:].bitcast(I32), 0)
        nc.vector.memset(window[0][:, 0:T], 0.0)
        nc.scalar.activation(window[1][:, 0:T], window[0][:, 0:T], IDENTITY)

        rows = {}
        for a in range(PASSES):
            by_row = xT[a * K_PASS : (a + 1) * K_PASS, :].rearrange("(p d) t -> d p t", d=PACK)
            for d in range(PACK):
                rows[a, d] = keep.tile([P, T], F32, name=f"row{a}{d}", align_bytes=ALIGN)
                nc.sync.dma_start(rows[a, d][:], by_row[d])
                if (a, d) == (0, 0):
                    nc.sync.dma_start(offsets[:], offs)

        code_rows = w_words.rearrange("e a p n -> p (e a) n")
        w_scale_words = w_scale[:].bitcast(I32).rearrange("p (g n) -> p g n", g=E * PASSES)
        scale_rows = w_scales.bitcast(I32).rearrange("e a (q r) n -> r q (e a) n", r=4)

        def load_codes(e0, e1):
            groups = slice(e0 * PASSES, e1 * PASSES)
            nc.sync.dma_start(w_code[:, groups, :], code_rows[:, groups, :])

        def load_scales(e0, e1):
            groups = slice(e0 * PASSES, e1 * PASSES)
            for r in range(4):
                nc.sync.dma_start(w_scale_words[r:P:32, groups, :], scale_rows[r][:, groups, :])

        def load_gates(i):
            nc.sync.dma_start(gates[i], gate[0:P, i * W : (i + 1) * W])

        nc.sync.dma_start(bias[:, :, 0:E], b.rearrange("(h p) e -> p h e", p=P))
        load_codes(0, PIECE)
        load_scales(0, PIECE)
        load_gates(0)
        load_codes(PIECE, 2 * PIECE)
        load_scales(PIECE, E)
        load_gates(1)
        load_codes(2 * PIECE, E)
        load_gates(2)
        for h in range(HALVES):
            nc.sync.dma_start(residual[:, h, :], xr[h * P : (h + 1) * P, :])

        def listed(tile, s0, s1):
            return tile[:].indirect(offsets[:, s0 // 16 : s1 // 16])

        stepped = [experts * C for experts in STEPPED_EXPERTS]
        direct = [keep.tile([P, stepped[a], PACK], BF16, name=f"direct{a}", align_bytes=ALIGN) for a in range(PASSES)]
        pairs = [keep.tile([P, 2, S - stepped[a], 2], BF16, name=f"pairs{a}", align_bytes=ALIGN) for a in range(PASSES)]

        def gather_direct(a, d):
            nc.vector.tensor_copy(direct[a][:, :, d], listed(rows[a, d], 0, stepped[a]))

        def plain_run(a, d, s0, s1):
            return pairs[a][:, d // 2, s0 - stepped[a] : s1 - stepped[a], d % 2]

        def gather_plain(a, d, s0, s1):
            nc.scalar.activation(plain_run(a, d, s0, s1), listed(rows[a, d], s0, s1), COPY)

        def weave(copy, word, woven, a, e0, e1):
            runs = pairs[a][:].bitcast(word)[:, :, e0 * C - stepped[a] : e1 * C - stepped[a], 0]
            copy(woven.bitcast(word), runs.rearrange("p u s -> p s u"))

        codes, scales = {}, {}

        def quantise(a, e0, e1, woven, behind=""):
            code = keep.tile([P, (e1 - e0) * C], U32, name=f"codes{a}{e0}", tag=behind, align_bytes=ALIGN)
            scale = keep.tile([P, (e1 - e0) * C], U8, name=f"scales{a}{e0}", align_bytes=ALIGN)
            nc.vector.quantize_mx(out=code[:].bitcast(FP8X4), scales=scale[:], in_=woven.rearrange("p s d -> p (s d)"))
            for e in range(e0, e1):
                codes[a, e] = code[:, (e - e0) * C : (e - e0 + 1) * C]
                scales[a, e] = scale[:, (e - e0) * C : (e - e0 + 1) * C]

        sums = [[None] * E for h in range(HALVES)]
        for h in range(HALVES):
            for i in range(PIECES):
                if i == 0:
                    for e in range(PIECE):
                        sums[h][e] = psum.tile([P, C], F32, name=f"lone{h}_{e}")[:]
                elif (h, i) == (0, 1):
                    sums[h][PIECE] = psum.tile([P, C], F32, name="bank0_1")[:]
                else:
                    bank = psum.tile([P, W], F32, name=f"bank{h}_{i}")
                    for j in range(PIECE):
                        sums[h][i * PIECE + j] = bank[:, j * C : (j + 1) * C]

        def one_pass(h, e, a, opening_pass):
            group = e * PASSES + a
            nc.tensor.matmul_mx(
                out=sums[h][e],
                lhsT=w_code[:, group, 2 * P * h : 2 * P * (h + 1)].bitcast(FP4X4),
                lhsT_scale=w_scale[:, group * N + h * P : group * N + (h + 1) * P],
                rhs=codes[a, e].bitcast(FP8X4),
                rhs_scale=scales[a, e],
                start=(a == opening_pass),
                stop=(a != opening_pass),
            )

        def multiply(h, e):
            for a in reversed(range(PASSES)):
                one_pass(h, e, a, PASSES - 1)

        scaled = [keep.tile([P, S], F32, name=f"scaled{h}", align_bytes=ALIGN) for h in range(HALVES)]
        free_bias = keep.tile([P, HALVES, BIAS_ROW], F32, name="free_bias")
        biased = [keep.tile([P, S - W], F32, name=f"biased{h}", align_bytes=ALIGN) for h in range(HALVES)]

        def add_bias(h, e):
            slots = slice(e * C - W, (e + 1) * C - W)
            source = free_bias if (h, e) in BESIDE_A_SCATTER else bias
            nc.scalar.activation(biased[h][:, slots], sums[h][e], IDENTITY, bias=source[:, h, e : e + 1])

        def apply_gates(h, e0, e1):
            slots = slice(e0 * C - W, e1 * C - W)
            nc.gpsimd.tensor_tensor(scaled[h][:, e0 * C : e1 * C], biased[h][:, slots], later_gates[:, slots], MULT)

        first_bias = {}

        def empty_on_vector(h, e):
            slots = slice(e * C, (e + 1) * C)
            source = first_bias[h][:] if e == 0 else free_bias[:, h, e : e + 1]
            nc.vector.scalar_tensor_tensor(scaled[h][:, slots], sums[h][e], source, gates[0][:, slots], ADD, MULT)

        def scatter_on_vector(s0, s1):
            nc.vector.tensor_copy(listed(window[0], s0, s1), scaled[0][:, s0:s1])

        def scatter_on_scalar(s0, s1):
            nc.scalar.activation(listed(window[1], s0, s1), scaled[1][:, s0:s1], COPY)

        for d in range(PACK):
            gather_direct(0, d)
            gather_plain(0, d, stepped[0], S)
        first_plain = STEPPED_EXPERTS[0]
        woven0 = keep.tile([P, S - stepped[0], PACK], BF16, name="woven0", align_bytes=ALIGN)
        cut = (E - 1 - first_plain) * C
        weave(nc.vector.tensor_copy, I32, woven0[:, 0:cut, :], 0, first_plain, E - 1)
        weave(nc.scalar.copy, U32, woven0[:, cut:, :], 0, E - 1, E)
        quantise(0, 0, first_plain, direct[0][:], "row03")
        last = PACK - 1
        for d in range(last):
            gather_direct(1, d)
            gather_plain(1, d, W, S)
        quantise(0, first_plain, E, woven0[:])
        for h in reversed(range(HALVES)):
            first_bias[h] = keep.tile([P, 1], F32, name=f"first_bias{h}", align_bytes=ALIGN)
            nc.gpsimd.tensor_copy(first_bias[h][:], bias[:, h, 0:1])
        nc.gpsimd.tensor_copy(free_bias[:, :, 0:E], bias[:, :, 0:E])
        for e in range(PIECE):
            one_pass(1, e, 0, 0)
        gather_direct(1, last)
        gather_plain(1, last, W, 2 * W)
        gather_plain(1, last, 2 * W, S)
        quantise(1, 0, PIECE, direct[1][:])
        woven1 = [keep.tile([P, W, PACK], BF16, name=f"woven1{i}", align_bytes=ALIGN) for i in range(1, PIECES)]
        weave(nc.vector.tensor_copy, I32, woven1[0][:], 1, PIECE, 2 * PIECE)
        weave(nc.scalar.copy, U32, woven1[1][:], 1, 2 * PIECE, E)
        for e in range(PIECE):
            one_pass(1, e, 1, 0)
        for e in range(PIECE):
            empty_on_vector(1, e)
        quantise(1, PIECE, 2 * PIECE, woven1[0][:], "first_bias1")
        for e in range(PIECE):
            multiply(0, e)
            empty_on_vector(0, e)
        quantise(1, 2 * PIECE, E, woven1[1][:], "first_bias0")
        sums[0][PIECE + 1] = psum.tile([P, C], F32, name="again1_0", tag="lone1_0")[:]
        scatter_on_vector(0, W)
        scatter_on_scalar(0, FIRST_ON_SCALAR)
        for i in range(1, PIECES):
            for h in range(HALVES):
                for e in range(i * PIECE, (i + 1) * PIECE):
                    multiply(h, e)
                for e in range(i * PIECE, (i + 1) * PIECE):
                    add_bias(h, e)
        apply_gates(0, PIECE, 2 * PIECE)
        apply_gates(1, PIECE, E // 2)
        apply_gates(1, E // 2, E)
        scatter_on_vector(W, 2 * W)
        nc.vector.tensor_tensor(listed(window[0], 2 * W, S), biased[0][:, W : 2 * W], gates[2], MULT)
        scatter_on_scalar(FIRST_ON_SCALAR, S // 2)
        scatter_on_scalar(S // 2, S)
        for h in range(HALVES):
            for t0, t1 in zip(SUM_CUTS, SUM_CUTS[1:]):
                tokens = slice(t0, t1)
                nc.vector.tensor_tensor(total[h][:, tokens], window[h][:, tokens], residual[:, h, tokens], ADD)
                nc.sync.dma_start(out[h * P : (h + 1) * P, tokens], total[h][:, tokens])
